import numpy as np
import ml_dtypes


def mxq(x, axis, fmt="e4m3"):
    dtype, down = {"e4m3": (ml_dtypes.float8_e4m3fn, 7), "e5m2": (ml_dtypes.float8_e5m2, 14)}[fmt]
    v = np.moveaxis(np.asarray(x, np.float32).astype(ml_dtypes.bfloat16).astype(np.float64), axis, -1)
    blocks = v.reshape(v.shape[:-1] + (-1, 32))
    amax = np.abs(blocks).max(-1, keepdims=True)
    byte = np.maximum(np.where(amax > 0, np.frexp(amax)[1] - 1 + 127, 0) - down, 1)
    scale = np.exp2(byte - 127.0)
    codes = (blocks / scale).astype(np.float32).astype(dtype).astype(np.float64)
    return np.moveaxis((codes * scale).reshape(v.shape), -1, axis)


WIDE = False


def mx_kscale(k):
    if not WIDE:
        return np.ones(k)
    levels = np.array([10, -10, 5, -5, 0])
    if k % 512:
        return np.exp2(np.random.permutation(np.resize(levels, k // 32))).repeat(32)
    a = np.empty((k // 512, 16))
    for p in range(k // 512):
        a[p, :8] = np.random.permutation(np.resize(levels, 8))
        for g in range(8):
            far = levels[np.abs(levels - a[p, g]) >= 10]
            a[p, g + 8] = far[np.random.randint(len(far))]
    return np.exp2(a.ravel()).repeat(32)


def f64(x):
    return np.asarray(x).astype(np.float64)


def striped(idx):
    return np.tile(idx.reshape(-1, 16).T, (8, 1)).astype(np.uint16)


def unstriped(offs):
    return offs[:16].T.reshape(-1).astype(np.int64)


E2M1 = np.array([0.0, 0.5, 1.0, 1.5, 2.0, 3.0, 4.0, 6.0, -0.0, -0.5, -1.0, -1.5, -2.0, -3.0, -4.0, -6.0])


def pack_weight(w, fmt):
    k, n = w.shape
    w = f64(np.asarray(w, np.float32).astype(ml_dtypes.bfloat16)).reshape(k // 32, 32, n)
    amax = np.abs(w).max(1)
    if fmt == "e4m3":
        byte = np.frexp(amax)[1] - 1 + 127 - 7
    else:
        mant, ex = np.frexp(amax / 6.0)
        byte = np.where(mant > 0.5, ex, ex - 1) + 127
    byte = np.clip(np.where(amax > 0, byte, 1), 1, 254)
    scaled = (w * np.exp2(127.0 - byte)[:, None, :]).reshape(k, n).astype(np.float32)
    by_word = np.ascontiguousarray(scaled.reshape(k // 512, 128, 4, n).transpose(0, 1, 3, 2))
    if fmt == "e4m3":
        words = by_word.astype(ml_dtypes.float8_e4m3fn).view(np.uint8)
    else:
        c = by_word.astype(ml_dtypes.float4_e2m1fn).view(np.uint8) & 0xF
        words = (c[..., 0::2] | (c[..., 1::2] << 4)).reshape(k // 512, 128, 2 * n)
    return np.ascontiguousarray(words), np.ascontiguousarray(byte.astype(np.uint8).reshape(k // 512, 16, n))


def unpack_weight(words, scales, fmt):
    g, _, n = scales.shape
    words = np.ascontiguousarray(words).reshape(g, 128, n, -1)
    if fmt == "e4m3":
        vals = words.view(ml_dtypes.float8_e4m3fn).astype(np.float64)
    else:
        nib = np.empty((g, 128, n, 4), np.uint8)
        nib[..., 0::2] = words & 0xF
        nib[..., 1::2] = words >> 4
        vals = E2M1[nib]
    vals = vals * np.repeat(np.exp2(scales.astype(np.float64) - 127.0), 8, axis=1)[..., None]
    return vals.transpose(0, 1, 3, 2).reshape(g * 512, n)


def gelu(v):
    return 0.5 * v * (1.0 + np.tanh(np.sqrt(2.0 / np.pi) * (v + 0.044715 * v**3)))


def striped8(idx):
    return np.concatenate([v.reshape(-1, 16).T for v in idx]).astype(np.uint16)


def unstriped8(offs):
    return np.stack([offs[16 * g:16 * g + 16].T.reshape(-1) for g in range(8)]).astype(np.int64)


def runs(v, idx8):
    k = np.arange(v.shape[0])
    return v[k[:, None], idx8[k % 512 // 64]]


def put_heads(h, wgs, idx8, t2):
    r = np.arange(h.shape[0])
    page = np.zeros((h.shape[0], t2))
    page[r[:, None], idx8[r % 512 // 64]] = wgs[r // 4 % 128] * h
    return page


def often(T, S):
    return np.random.permutation(T)[(T * np.random.uniform(0, 1, S) ** 4).astype(np.int64)]


K, T, S, T2, H, N = 1024, 2048, 1024, 2048, 512, 512


def setup_inputs():
    n = np.random.standard_normal
    s = mx_kscale(K)[:, None]
    u = mx_kscale(H)[:, None]
    tab_words, tab_scales = pack_weight(n((K, T)) * s, "e4m3")
    w4_words, w4_scales = pack_weight(n((K, H)) * u.T / s / np.sqrt(K), "e2m1")
    wa = (n((K, H)) / s / np.sqrt(K)).astype(np.float32)
    wb = (n((H, N)) / u / np.sqrt(H)).astype(np.float32)
    w8_words, w8_scales = pack_weight(n((H, N)) / u / np.sqrt(H), "e4m3")
    wgo = np.repeat(np.random.uniform(0.5, 2.0, (8, S)), 16, axis=0).astype(np.float32)
    offs = striped8(np.stack([often(T, S) for _ in range(8)]))
    offs2 = striped8(np.stack([np.random.permutation(T2)[:S] for _ in range(8)]))
    return {"tab_words": tab_words, "tab_scales": tab_scales,
            "w4_words": w4_words, "w4_scales": w4_scales, "wa": wa, "wb": wb,
            "w8_words": w8_words, "w8_scales": w8_scales, "wgo": wgo,
            "offs": offs, "offs2": offs2}


def reference(tab_words, tab_scales, w4_words, w4_scales, wa, wb, w8_words, w8_scales, wgo, offs, offs2):
    v = runs(unpack_weight(tab_words, tab_scales, "e4m3"), unstriped8(offs))
    w4 = unpack_weight(w4_words, w4_scales, "e2m1")
    w8 = unpack_weight(w8_words, w8_scales, "e4m3")
    x = w4.T @ v
    av = mxq(f64(wa), 0, "e4m3").T @ v
    h = mxq(x * av, 0, "e4m3")
    b = mxq(f64(wb), 0, "e4m3").T @ h
    d = w8.T @ h
    y = b / (1.0 + np.square(d))
    return put_heads(y, f64(wgo), unstriped8(offs2), T2)

@@ -1,0 +1,257 @@
+from contextlib import ExitStack
+
+import concourse.mybir as mybir
+from concourse.masks import make_identity
+
+K, T, S, T2, H, N = 1024, 2048, 1024, 2048, 512, 512
+FLOPS = 2 * (2 * K * H * S + 2 * H * N * S)
+
+F32 = mybir.dt.float32
+BF16 = mybir.dt.bfloat16
+I32 = mybir.dt.int32
+U32 = mybir.dt.uint32
+U16 = mybir.dt.uint16
+U8 = mybir.dt.uint8
+FP8X4 = mybir.dt.float8_e4m3fn_x4
+FP4X4 = mybir.dt.float4_e2m1fn_x4
+ACT = mybir.ActivationFunctionType
+MULT = mybir.AluOpType.mult
+
+P = 128
+PACK = 4
+PASSES = K // (P * PACK)
+CH = 128
+CHUNKS = S // CH
+GROUPS = 8
+GP = P // GROUPS
+GATHER_CUTS = (0, 2, 4, 8)
+SCATTER_CUTS = (0, 1, 2, 3, 5, 8)
+
+
+def tile_list_allele_mixture_scores_kernel(
+    tc, tab_words, tab_scales, w4_words, w4_scales, wa, wb, w8_words, w8_scales, wgo, offs, offs2, out
+):
+    nc = tc.nc
+    with ExitStack() as ctx:
+        keep = ctx.enter_context(tc.tile_pool(name="keep", bufs=1))
+        ring = ctx.enter_context(tc.tile_pool(name="ring", bufs=2))
+        psum2 = ctx.enter_context(tc.psum_pool(name="psum2", bufs=2))
+        psum1 = ctx.enter_context(tc.psum_pool(name="psum1", bufs=1))
+
+        def held(name, shape, dtype):
+            return keep.tile(shape, dtype, name=name, align_bytes=64)
+
+        picks = keep.tile([P, S // 16], U16, name="picks")
+        bins = keep.tile([P, S // 16], U16, name="bins")
+        tab_s = held("tab_s", [P, T], U8)
+        wb_raw = held("wb_raw", [P, PACK, N], F32)
+        tab_w = [held(f"tab_w{a}", [P, T], U32) for a in range(PASSES)]
+        wa_raw = [held(f"wa_raw{a}", [P, PACK, H], F32) for a in range(PASSES)]
+        w4_raw = held("w4_raw", [P, PASSES * 2 * H], U8)
+        w4_s_raw = held("w4_s_raw", [P, PASSES * H], U8)
+        wgo_rows = held("wgo_rows", [P, S], F32)
+        picked_s = held("picked_s", [P, S], U8)
+        v_s = held("v_s", [P, PASSES * S], U8)
+        v_w0 = held("v_w0", [P, S], U32)
+        v_w1 = held("v_w1", [P, S], U32)
+        v_w = [v_w0, v_w1]
+        ident = held("ident", [P, P], F32)
+        pages = [held(f"page{i}", [P, T2], F32) for i in range(PACK)]
+        one = held("one", [P, 1], F32)
+        warm = held("warm", [P, 1], F32)
+
+        nc.gpsimd.memset(tab_s[:].bitcast(I32), 0)
+        nc.vector.memset(w4_s_raw[:].bitcast(I32), 0)
+        nc.vector.memset(wgo_rows[:], 0.0)
+        nc.vector.memset(one[:], 1.0)
+        nc.vector.memset(v_s[:].bitcast(I32), 0)
+        nc.vector.memset(pages[0][:], 0.0)
+        nc.scalar.activation(warm[:], one[:], ACT.Abs_reciprocal_sqrt)
+        make_identity(nc, ident[:])
+        nc.gpsimd.dma_start(wgo_rows[0:GROUPS, :], wgo[0:P:GP, :])
+
+        def load_rows(tile, rows):
+            nc.sync.dma_start(tile[:], rows.rearrange("(p j) c -> p j c", j=PACK))
+
+        def load_words(tile, words):
+            nc.sync.dma_start(tile[:].bitcast(I32), words.rearrange("p t i -> p (t i)").bitcast(I32))
+
+        nc.sync.dma_start(picks[:], offs)
+        nc.sync.dma_start(
+            w4_raw[:].bitcast(I32).rearrange("p (a c) -> p a c", a=PASSES),
+            w4_words.bitcast(I32).rearrange("a p c -> p a c"),
+        )
+        for a in range(PASSES):
+            nc.sync.dma_start(tab_s[a:P:8, :].bitcast(I32), tab_scales[a].bitcast(I32))
+        load_words(tab_w[0], tab_words[0])
+        for d in range(4):
+            nc.sync.dma_start(
+                w4_s_raw[32 * d : 32 * d + 4, :].bitcast(I32).rearrange("r (a c) -> r a c", a=PASSES),
+                w4_scales[:, 4 * d : 4 * d + 4, :].bitcast(I32).rearrange("a r c -> r a c"),
+            )
+        load_rows(wa_raw[0], wa[0:512, :])
+        load_words(tab_w[1], tab_words[1])
+        load_rows(wa_raw[1], wa[512:1024, :])
+        nc.sync.dma_start(bins[:], offs2)
+        load_rows(wb_raw, wb)
+
+        nc.vector.tensor_copy(picked_s[:], tab_s[:].indirect(picks[:]))
+        for a, queue in enumerate((nc.scalar, nc.gpsimd)):
+            for d in range(4):
+                queue.dma_start(
+                    v_s[32 * d : 32 * d + 4, a * S : (a + 1) * S].bitcast(I32), picked_s[32 * d + a : 32 * d + 32 : 8, :].bitcast(I32)
+                )
+
+        winv = held("winv", [P, CHUNKS, GROUPS], F32)
+        for half in range(2):
+            bank = psum2.tile([P, PACK, CH], F32, name="b_bank")
+            for c in range(PACK):
+                cc = PACK * half + c
+                nc.tensor.transpose(bank[:, c, :], wgo_rows[:, cc * CH : (cc + 1) * CH], ident[:])
+            nc.vector.reciprocal(winv[:, PACK * half : PACK * (half + 1), :], bank[:, :, 0:GROUPS])
+
+        def regroup(name, raw, t0, t1, copy):
+            grouped = held(name, [P, t1 - t0, P, PACK], BF16)
+            copy(grouped[:].rearrange("p t m j -> p m j t"), raw[:].rearrange("p j (m t) -> p m j t", t=PACK)[:, :, :, t0:t1])
+            return grouped
+
+        def quantise(name, grouped):
+            slices = grouped.shape[1]
+            codes = held(name + "_w", [P, slices * P], U32)
+            scales = held(name + "_s", [P, slices * P], U8)
+            nc.vector.quantize_mx(codes[:].bitcast(FP8X4), scales[:], grouped[:].rearrange("p t m j -> p (t m j)"))
+            return [(codes[:, t * P : (t + 1) * P].bitcast(FP8X4), scales[:, t * P : (t + 1) * P]) for t in range(slices)]
+
+        nc.vector.tensor_copy(v_w0[:], tab_w[0][:].indirect(picks[:]))
+        w4_w = held("w4_w", [P, PASSES * 2 * H], U8)
+        w4_s = held("w4_s", [P, PASSES * H], U8)
+        nc.vector.tensor_copy(
+            w4_w[:].bitcast(U16).rearrange("p (a t m) -> p a t m", a=PASSES, t=PACK),
+            w4_raw[:].bitcast(U16).rearrange("p (a m t) -> p a t m", a=PASSES, t=PACK),
+        )
+        nc.vector.tensor_copy(
+            w4_s[:].rearrange("p (a t m) -> p a t m", a=PASSES, t=PACK),
+            w4_s_raw[:].rearrange("p (a m t) -> p a t m", a=PASSES, t=PACK),
+        )
+        w8_w, w8_s = w4_raw, w4_s_raw
+        load_words(w8_w, w8_words[0])
+        for d in range(4):
+            nc.gpsimd.dma_start(w8_s[32 * d : 32 * d + 4, 0:N].bitcast(I32), w8_scales[0, 4 * d : 4 * d + 4, :].bitcast(I32))
+        for page in pages[1:]:
+            nc.gpsimd.memset(page[:], 0.0)
+        wa_q = [quantise("wa_q0", regroup("wa_g0", wa_raw[0], 0, PACK, nc.scalar.copy))]
+
+        def gather_words(c0, c1):
+            nc.vector.tensor_copy(v_w1[:, c0 * CH : c1 * CH], tab_w[1][:].indirect(picks[:, c0 * CH // 16 : c1 * CH // 16]))
+
+        h_w = held("h_w", [P, S], U32)
+        h_s = held("h_s", [P, S], U8)
+
+        def product(c, name, weights):
+            bank = psum2.tile([P, PACK, CH], F32, name=name)
+            for a in range(PASSES):
+                for t in range(PACK):
+                    codes, scales = weights[a][t]
+                    nc.tensor.matmul_mx(
+                        bank[:, t, :], lhsT=codes, lhsT_scale=scales,
+                        rhs=v_w[a][:, c * CH : (c + 1) * CH].bitcast(FP8X4), rhs_scale=v_s[:, a * S + c * CH : a * S + (c + 1) * CH],
+                        start=(a == 0 and t == 0), stop=(a == PASSES - 1 and t == PACK - 1),
+                    )
+            return bank
+
+        w4_q = [
+            [(w4_w[:, 2 * col : 2 * (col + P)].bitcast(FP4X4), w4_s[:, col : col + P]) for col in range(a * H, (a + 1) * H, P)]
+            for a in range(PASSES)
+        ]
+
+        def project(c):
+            x_bank = product(c, "x_bank", w4_q)
+            x_sb = ring.tile([P, CH, PACK], F32, name="x_sb")
+            nc.scalar.copy(x_sb[:], x_bank[:].rearrange("p t n -> p n t"))
+            return x_sb
+
+        def first_stage(c, x_sb=None):
+            if x_sb is None:
+                x_sb = project(c)
+            av_bank = product(c, "av_bank", wa_q)
+            h_bf = ring.tile([P, CH, PACK], BF16, name="h_bf", align_bytes=64)
+            nc.vector.tensor_tensor(h_bf[:], av_bank[:].rearrange("p t n -> p n t"), x_sb[:], MULT)
+            nc.vector.quantize_mx(
+                h_w[:, c * CH : (c + 1) * CH].bitcast(FP8X4), h_s[:, c * CH : (c + 1) * CH], h_bf[:].rearrange("p n t -> p (n t)")
+            )
+
+        b_sb = held("b_sb", [P, PACK * S], F32)
+        damp = held("damp", [P, PACK * S], F32)
+
+        def piece_view(tile, c):
+            k = max(k for k in range(len(SCATTER_CUTS) - 1) if SCATTER_CUTS[k] <= c)
+            c0, c1 = SCATTER_CUTS[k], SCATTER_CUTS[k + 1]
+            block = tile[:, PACK * c0 * CH : PACK * c1 * CH].rearrange("p (i j) -> p i j", i=PACK)
+            return block[:, :, (c - c0) * CH : (c - c0 + 1) * CH]
+
+        def damping(c):
+            hw = h_w[:, c * CH : (c + 1) * CH].bitcast(FP8X4)
+            hs = h_s[:, c * CH : (c + 1) * CH]
+            d_bank = psum1.tile([P, N], F32, name="d_bank")
+            nc.tensor.matmul_mx(d_bank[:], lhsT=hw, lhsT_scale=hs, rhs=w8_w[:].bitcast(FP8X4), rhs_scale=w8_s[:, 0:N], start=True, stop=True)
+            sq = ring.tile([P, PACK, P], F32, name="sq")
+            nc.scalar.activation(sq[:], d_bank[:].rearrange("p (m i) -> p i m", i=PACK), ACT.Square)
+            root = ring.tile([P, PACK, P], F32, name="root")
+            for g in range(GROUPS):
+                nc.scalar.activation(
+                    root[:, :, g * GP : (g + 1) * GP], sq[:, :, g * GP : (g + 1) * GP], ACT.Abs_reciprocal_sqrt,
+                    bias=winv[:, c, g : g + 1], scale=winv[:, c, g : g + 1],
+                )
+            return root
+
+        def second_stage(c, wb_q, root=None):
+            if root is None:
+                root = damping(c)
+            hw = h_w[:, c * CH : (c + 1) * CH].bitcast(FP8X4)
+            hs = h_s[:, c * CH : (c + 1) * CH]
+            b_bank = psum2.tile([P, PACK, CH], F32, name="b_bank")
+            for i in range(PACK):
+                nc.tensor.matmul_mx(
+                    b_bank[:, i, :], lhsT=wb_q[i][0], lhsT_scale=wb_q[i][1],
+                    rhs=hw, rhs_scale=hs, start=True, stop=True,
+                )
+            nc.scalar.copy(piece_view(b_sb, c), b_bank[:])
+            r_bank = psum1.tile([P, PACK, CH], F32, name="r_bank")
+            for i in range(PACK):
+                nc.tensor.transpose(r_bank[:, i, :], root[:, i, :], ident[:])
+            nc.scalar.activation(piece_view(damp, c), r_bank[:], ACT.Square)
+
+        def scatter(k):
+            c0, c1 = SCATTER_CUTS[k], SCATTER_CUTS[k + 1]
+            width = (c1 - c0) * CH
+            for i in range(PACK):
+                cols = slice(PACK * c0 * CH + i * width, PACK * c0 * CH + (i + 1) * width)
+                nc.vector.tensor_tensor(
+                    pages[i][:].indirect(bins[:, c0 * CH // 16 : c1 * CH // 16]), b_sb[:, cols], damp[:, cols], MULT
+                )
+                if c1 == CHUNKS:
+                    nc.sync.dma_start(out.rearrange("(p i) t -> p i t", i=PACK)[:, i, :], pages[i][:])
+
+        for k in range(len(GATHER_CUTS) - 1):
+            gather_words(GATHER_CUTS[k], GATHER_CUTS[k + 1])
+        x_first = [project(0), project(1)]
+        low = regroup("wa_g1a", wa_raw[1], 0, 2, nc.scalar.copy)
+        high = regroup("wa_g1b", wa_raw[1], 2, PACK, nc.vector.tensor_copy)
+        high = quantise("wa_q1b", high)
+        wa_q.append(quantise("wa_q1a", low) + high)
+        first_stage(0, x_first[0])
+        first_stage(1, x_first[1])
+        wb_q = quantise("wb_qa", regroup("wb_ga", wb_raw, 0, 2, nc.scalar.copy))
+        first_stage(2)
+        root_first = damping(0)
+        wb_q = wb_q + quantise("wb_qb", regroup("wb_gb", wb_raw, 2, PACK, nc.scalar.copy))
+        first_stage(3)
+        second_stage(0, wb_q, root_first)
+        order = ["s1", 4, "s2", 1, "sc", 0, "s1", 5, "s2", 2, "s1", 6, "sc", 1, "s1", 7, "s2", 3, "sc", 2, "s2", 4, "sc", 3, "s2", 5, "s2", 6, "s2", 7, "sc", 4]
+        for what, c in zip(order[0::2], order[1::2]):
+            if what == "s1":
+                first_stage(c)
+            elif what == "s2":
+                second_stage(c, wb_q)
+            else:
+                scatter(c)

@@ -26,6 +26,11 @@ GROUPS = 8
 GP = P // GROUPS
 GATHER_CUTS = (0, 2, 4, 8)
 SCATTER_CUTS = (0, 1, 2, 3, 5, 8)
+QUANTISE_CUTS = (0, 1, 2, 4, 6, 8)
+
+
+def cut_of(cuts, c):
+    return max(lo for lo in cuts if lo <= c), min(hi for hi in cuts if hi > c)
 
 
 def tile_list_allele_mixture_scores_kernel(
@@ -38,37 +43,36 @@ def tile_list_allele_mixture_scores_kernel(
         psum2 = ctx.enter_context(tc.psum_pool(name="psum2", bufs=2))
         psum1 = ctx.enter_context(tc.psum_pool(name="psum1", bufs=1))
 
-        def held(name, shape, dtype):
-            return keep.tile(shape, dtype, name=name, align_bytes=64)
+        def held(name, shape, dtype, after=None):
+            return keep.tile(shape, dtype, name=name, tag=after or name, align_bytes=64)
 
         picks = keep.tile([P, S // 16], U16, name="picks")
         bins = keep.tile([P, S // 16], U16, name="bins")
         tab_s = held("tab_s", [P, T], U8)
-        wb_raw = held("wb_raw", [P, PACK, N], F32)
-        tab_w = [held(f"tab_w{a}", [P, T], U32) for a in range(PASSES)]
-        wa_raw = [held(f"wa_raw{a}", [P, PACK, H], F32) for a in range(PASSES)]
+        tab_w0 = held("tab_w0", [P, T], U32)
         w4_raw = held("w4_raw", [P, PASSES * 2 * H], U8)
         w4_s_raw = held("w4_s_raw", [P, PASSES * H], U8)
         wgo_rows = held("wgo_rows", [P, S], F32)
         picked_s = held("picked_s", [P, S], U8)
-        v_s = held("v_s", [P, PASSES * S], U8)
+        v_s = [held(f"v_s{a}", [P, S], U8) for a in range(PASSES)]
         v_w0 = held("v_w0", [P, S], U32)
         v_w1 = held("v_w1", [P, S], U32)
         v_w = [v_w0, v_w1]
         ident = held("ident", [P, P], F32)
-        pages = [held(f"page{i}", [P, T2], F32) for i in range(PACK)]
-        one = held("one", [P, 1], F32)
-        warm = held("warm", [P, 1], F32)
+        wa_raw0 = held("wa_raw0", [P, PACK, H], F32)
+        pages = [held("page0", [P, T2], F32)]
 
         nc.gpsimd.memset(tab_s[:].bitcast(I32), 0)
         nc.vector.memset(w4_s_raw[:].bitcast(I32), 0)
-        nc.vector.memset(wgo_rows[:], 0.0)
-        nc.vector.memset(one[:], 1.0)
-        nc.vector.memset(v_s[:].bitcast(I32), 0)
-        nc.vector.memset(pages[0][:], 0.0)
-        nc.scalar.activation(warm[:], one[:], ACT.Abs_reciprocal_sqrt)
+        nc.vector.memset(wgo_rows[:].bitcast(I32), 0)
+        nc.vector.memset(v_s[1][:].bitcast(I32), 0)
+        nc.vector.memset(pages[0][:].bitcast(I32), 0)
         make_identity(nc, ident[:])
-        nc.gpsimd.dma_start(wgo_rows[0:GROUPS, :], wgo[0:P:GP, :])
+
+        def new_page(after):
+            page = held(f"page{len(pages)}", [P, T2], F32, after)
+            nc.vector.memset(page[:].bitcast(I32), 0)
+            pages.append(page)
 
         def load_rows(tile, rows):
             nc.sync.dma_start(tile[:], rows.rearrange("(p j) c -> p j c", j=PACK))
@@ -77,38 +81,41 @@ def tile_list_allele_mixture_scores_kernel(
             nc.sync.dma_start(tile[:].bitcast(I32), words.rearrange("p t i -> p (t i)").bitcast(I32))
 
         nc.sync.dma_start(picks[:], offs)
+        nc.sync.dma_start(bins[:], offs2)
         nc.sync.dma_start(
             w4_raw[:].bitcast(I32).rearrange("p (a c) -> p a c", a=PASSES),
             w4_words.bitcast(I32).rearrange("a p c -> p a c"),
         )
-        for a in range(PASSES):
-            nc.sync.dma_start(tab_s[a:P:8, :].bitcast(I32), tab_scales[a].bitcast(I32))
-        load_words(tab_w[0], tab_words[0])
+        load_words(tab_w0, tab_words[0])
+        load_rows(wa_raw0, wa[0:512, :])
+        for e in range(2):
+            nc.scalar.dma_start(tab_s[e:P:GP, :].bitcast(I32), tab_scales[0, e:16:2, :].bitcast(I32))
+        nc.scalar.dma_start(tab_s[2:P:8, :].bitcast(I32), tab_scales[1].bitcast(I32))
         for d in range(4):
-            nc.sync.dma_start(
+            nc.scalar.dma_start(
                 w4_s_raw[32 * d : 32 * d + 4, :].bitcast(I32).rearrange("r (a c) -> r a c", a=PASSES),
                 w4_scales[:, 4 * d : 4 * d + 4, :].bitcast(I32).rearrange("a r c -> r a c"),
             )
-        load_rows(wa_raw[0], wa[0:512, :])
-        load_words(tab_w[1], tab_words[1])
-        load_rows(wa_raw[1], wa[512:1024, :])
-        nc.sync.dma_start(bins[:], offs2)
-        load_rows(wb_raw, wb)
+        nc.scalar.dma_start(wgo_rows[0:GROUPS, :], wgo[0:P:GP, :])
 
         nc.vector.tensor_copy(picked_s[:], tab_s[:].indirect(picks[:]))
-        for a, queue in enumerate((nc.scalar, nc.gpsimd)):
-            for d in range(4):
-                queue.dma_start(
-                    v_s[32 * d : 32 * d + 4, a * S : (a + 1) * S].bitcast(I32), picked_s[32 * d + a : 32 * d + 32 : 8, :].bitcast(I32)
-                )
+        tab_w1 = held("tab_w1", [P, T], U32, "tab_s")
+        load_words(tab_w1, tab_words[1])
+        nc.vector.tensor_copy(v_s[0][:].bitcast(I32), picked_s[:].bitcast(I32))
+        for d in range(4):
+            nc.scalar.dma_start(v_s[1][32 * d : 32 * d + 4, :].bitcast(I32), picked_s[32 * d + 2 : 32 * d + 32 : 8, :].bitcast(I32))
+        for e in range(2):
+            nc.scalar.dma_start(v_s[0][2 + e : P : 32, :].bitcast(I32), picked_s[GP + e : P : 32, :].bitcast(I32))
 
         winv = held("winv", [P, CHUNKS, GROUPS], F32)
+        wroot = held("wroot", [P, CHUNKS, GROUPS], F32)
         for half in range(2):
             bank = psum2.tile([P, PACK, CH], F32, name="b_bank")
             for c in range(PACK):
                 cc = PACK * half + c
                 nc.tensor.transpose(bank[:, c, :], wgo_rows[:, cc * CH : (cc + 1) * CH], ident[:])
-            nc.vector.reciprocal(winv[:, PACK * half : PACK * (half + 1), :], bank[:, :, 0:GROUPS])
+            nc.scalar.activation(wroot[:, PACK * half : PACK * (half + 1), :], bank[:, :, 0:GROUPS], ACT.Abs_reciprocal_sqrt)
+        nc.scalar.activation(winv[:], wroot[:], ACT.Square)
 
         def regroup(name, raw, t0, t1, copy):
             grouped = held(name, [P, t1 - t0, P, PACK], BF16)
@@ -122,7 +129,9 @@ def tile_list_allele_mixture_scores_kernel(
             nc.vector.quantize_mx(codes[:].bitcast(FP8X4), scales[:], grouped[:].rearrange("p t m j -> p (t m j)"))
             return [(codes[:, t * P : (t + 1) * P].bitcast(FP8X4), scales[:, t * P : (t + 1) * P]) for t in range(slices)]
 
-        nc.vector.tensor_copy(v_w0[:], tab_w[0][:].indirect(picks[:]))
+        nc.vector.tensor_copy(v_w0[:], tab_w0[:].indirect(picks[:]))
+        wa_raw1 = held("wa_raw1", [P, PACK, H], F32, "tab_w0")
+        load_rows(wa_raw1, wa[512:1024, :])
         w4_w = held("w4_w", [P, PASSES * 2 * H], U8)
         w4_s = held("w4_s", [P, PASSES * H], U8)
         nc.vector.tensor_copy(
@@ -133,19 +142,22 @@ def tile_list_allele_mixture_scores_kernel(
             w4_s[:].rearrange("p (a t m) -> p a t m", a=PASSES, t=PACK),
             w4_s_raw[:].rearrange("p (a m t) -> p a t m", a=PASSES, t=PACK),
         )
-        w8_w, w8_s = w4_raw, w4_s_raw
-        load_words(w8_w, w8_words[0])
+        w8_s = w4_s_raw
         for d in range(4):
-            nc.gpsimd.dma_start(w8_s[32 * d : 32 * d + 4, 0:N].bitcast(I32), w8_scales[0, 4 * d : 4 * d + 4, :].bitcast(I32))
-        for page in pages[1:]:
-            nc.gpsimd.memset(page[:], 0.0)
-        wa_q = [quantise("wa_q0", regroup("wa_g0", wa_raw[0], 0, PACK, nc.scalar.copy))]
+            nc.sync.dma_start(w8_s[32 * d : 32 * d + 4, 0:N].bitcast(I32), w8_scales[0, 4 * d : 4 * d + 4, :].bitcast(I32))
+        wa_g0 = regroup("wa_g0", wa_raw0, 0, PACK, nc.scalar.copy)
+        wb_raw = held("wb_raw", [P, PACK, N], F32, "wa_raw0")
+        load_rows(wb_raw, wb)
+        wa_q = [quantise("wa_q0", wa_g0)]
+        w8_w = held("w8_w", [P, N], U32, "wa_g0")
+        load_words(w8_w, w8_words[0])
 
         def gather_words(c0, c1):
-            nc.vector.tensor_copy(v_w1[:, c0 * CH : c1 * CH], tab_w[1][:].indirect(picks[:, c0 * CH // 16 : c1 * CH // 16]))
+            nc.vector.tensor_copy(v_w1[:, c0 * CH : c1 * CH], tab_w1[:].indirect(picks[:, c0 * CH // 16 : c1 * CH // 16]))
 
         h_w = held("h_w", [P, S], U32)
         h_s = held("h_s", [P, S], U8)
+        h_bf = held("h_bf", [P, S * PACK], BF16)
 
         def product(c, name, weights):
             bank = psum2.tile([P, PACK, CH], F32, name=name)
@@ -154,7 +166,7 @@ def tile_list_allele_mixture_scores_kernel(
                     codes, scales = weights[a][t]
                     nc.tensor.matmul_mx(
                         bank[:, t, :], lhsT=codes, lhsT_scale=scales,
-                        rhs=v_w[a][:, c * CH : (c + 1) * CH].bitcast(FP8X4), rhs_scale=v_s[:, a * S + c * CH : a * S + (c + 1) * CH],
+                        rhs=v_w[a][:, c * CH : (c + 1) * CH].bitcast(FP8X4), rhs_scale=v_s[a][:, c * CH : (c + 1) * CH],
                         start=(a == 0 and t == 0), stop=(a == PASSES - 1 and t == PACK - 1),
                     )
             return bank
@@ -174,18 +186,18 @@ def tile_list_allele_mixture_scores_kernel(
             if x_sb is None:
                 x_sb = project(c)
             av_bank = product(c, "av_bank", wa_q)
-            h_bf = ring.tile([P, CH, PACK], BF16, name="h_bf", align_bytes=64)
-            nc.vector.tensor_tensor(h_bf[:], av_bank[:].rearrange("p t n -> p n t"), x_sb[:], MULT)
-            nc.vector.quantize_mx(
-                h_w[:, c * CH : (c + 1) * CH].bitcast(FP8X4), h_s[:, c * CH : (c + 1) * CH], h_bf[:].rearrange("p n t -> p (n t)")
-            )
+            c0, c1 = cut_of(QUANTISE_CUTS, c)
+            nc.vector.tensor_tensor(h_bf[:, c * CH * PACK : (c + 1) * CH * PACK].rearrange("p (n t) -> p n t", t=PACK), av_bank[:].rearrange("p t n -> p n t"), x_sb[:], MULT)
+            if c + 1 == c1:
+                nc.vector.quantize_mx(
+                    h_w[:, c0 * CH : c1 * CH].bitcast(FP8X4), h_s[:, c0 * CH : c1 * CH], h_bf[:, c0 * CH * PACK : c1 * CH * PACK]
+                )
 
         b_sb = held("b_sb", [P, PACK * S], F32)
         damp = held("damp", [P, PACK * S], F32)
 
         def piece_view(tile, c):
-            k = max(k for k in range(len(SCATTER_CUTS) - 1) if SCATTER_CUTS[k] <= c)
-            c0, c1 = SCATTER_CUTS[k], SCATTER_CUTS[k + 1]
+            c0, c1 = cut_of(SCATTER_CUTS, c)
             block = tile[:, PACK * c0 * CH : PACK * c1 * CH].rearrange("p (i j) -> p i j", i=PACK)
             return block[:, :, (c - c0) * CH : (c - c0 + 1) * CH]
 
@@ -235,14 +247,16 @@ def tile_list_allele_mixture_scores_kernel(
         for k in range(len(GATHER_CUTS) - 1):
             gather_words(GATHER_CUTS[k], GATHER_CUTS[k + 1])
         x_first = [project(0), project(1)]
-        low = regroup("wa_g1a", wa_raw[1], 0, 2, nc.scalar.copy)
-        high = regroup("wa_g1b", wa_raw[1], 2, PACK, nc.vector.tensor_copy)
-        high = quantise("wa_q1b", high)
-        wa_q.append(quantise("wa_q1a", low) + high)
+        low = regroup("wa_g1a", wa_raw1, 0, 2, nc.scalar.copy)
+        high = regroup("wa_g1b", wa_raw1, 2, PACK, nc.scalar.copy)
+        new_page("tab_s")
+        wa_q.append(quantise("wa_q1a", low) + quantise("wa_q1b", high))
+        new_page("tab_w0")
         first_stage(0, x_first[0])
         first_stage(1, x_first[1])
         wb_q = quantise("wb_qa", regroup("wb_ga", wb_raw, 0, 2, nc.scalar.copy))
         first_stage(2)
+        new_page("wb_ga")
         root_first = damping(0)
         wb_q = wb_q + quantise("wb_qb", regroup("wb_gb", wb_raw, 2, PACK, nc.scalar.copy))
         first_stage(3)

@@ -24,9 +24,9 @@ CH = 128
 CHUNKS = S // CH
 GROUPS = 8
 GP = P // GROUPS
-GATHER_CUTS = (0, 2, 4, 8)
-SCATTER_CUTS = (0, 1, 2, 3, 5, 8)
 QUANTISE_CUTS = (0, 1, 2, 4, 6, 8)
+LAST_PIECE = (1, 2, 3, 4)
+AHEAD = 4
 
 
 def cut_of(cuts, c):
@@ -39,6 +39,7 @@ def tile_list_allele_mixture_scores_kernel(
     nc = tc.nc
     with ExitStack() as ctx:
         keep = ctx.enter_context(tc.tile_pool(name="keep", bufs=1))
+        laid = ctx.enter_context(tc.tile_pool(name="laid", bufs=1))
         ring = ctx.enter_context(tc.tile_pool(name="ring", bufs=2))
         psum2 = ctx.enter_context(tc.psum_pool(name="psum2", bufs=2))
         psum1 = ctx.enter_context(tc.psum_pool(name="psum1", bufs=1))
@@ -46,79 +47,70 @@ def tile_list_allele_mixture_scores_kernel(
         def held(name, shape, dtype, after=None):
             return keep.tile(shape, dtype, name=name, tag=after or name, align_bytes=64)
 
+        def placed(name, shape, dtype, offset):
+            return laid.tile(shape, dtype, name=name, align_bytes=64, offset=offset)
+
         picks = keep.tile([P, S // 16], U16, name="picks")
         bins = keep.tile([P, S // 16], U16, name="bins")
         tab_s = held("tab_s", [P, T], U8)
-        tab_w0 = held("tab_w0", [P, T], U32)
-        w4_raw = held("w4_raw", [P, PASSES * 2 * H], U8)
+        tab_w0 = placed("tab_w0", [P, T], U32, 4 * T)
+        w4_raw = placed("w4_raw", [P, PASSES * 2 * H], U8, 12 * T)
         w4_s_raw = held("w4_s_raw", [P, PASSES * H], U8)
-        wgo_rows = held("wgo_rows", [P, S], F32)
+        wgo_rows = held("wgo_rows", [P, CH], F32)
         picked_s = held("picked_s", [P, S], U8)
-        v_s = [held(f"v_s{a}", [P, S], U8) for a in range(PASSES)]
+        v_s = held("v_s", [P, PASSES * S], U8)
         v_w0 = held("v_w0", [P, S], U32)
-        v_w1 = held("v_w1", [P, S], U32)
-        v_w = [v_w0, v_w1]
         ident = held("ident", [P, P], F32)
         wa_raw0 = held("wa_raw0", [P, PACK, H], F32)
-        pages = [held("page0", [P, T2], F32)]
+        pages = [held(f"page{i}", [P, T2], F32) for i in range(2)]
 
+        nc.gpsimd.memset(w4_s_raw[:].bitcast(I32), 0)
         nc.gpsimd.memset(tab_s[:].bitcast(I32), 0)
-        nc.vector.memset(w4_s_raw[:].bitcast(I32), 0)
-        nc.vector.memset(wgo_rows[:].bitcast(I32), 0)
-        nc.vector.memset(v_s[1][:].bitcast(I32), 0)
-        nc.vector.memset(pages[0][:].bitcast(I32), 0)
+        nc.gpsimd.memset(wgo_rows[:], 0.0)
         make_identity(nc, ident[:])
+        for lo, hi in ((0, T2 // 2 + 1), (T2 // 2 + 1, T2 // 2 + 2), (T2 // 2 + 2, T2)):
+            nc.vector.memset(pages[0][:, lo:hi].bitcast(I32), 0)
+        nc.vector.memset(v_s[:].bitcast(I32), 0)
+        nc.vector.memset(pages[1][:].bitcast(I32), 0)
 
         def new_page(after):
-            page = held(f"page{len(pages)}", [P, T2], F32, after)
-            nc.vector.memset(page[:].bitcast(I32), 0)
-            pages.append(page)
+            pages.append(held(f"page{len(pages)}", [P, T2], F32, after))
+            nc.vector.memset(pages[-1][:].bitcast(I32), 0)
 
         def load_rows(tile, rows):
             nc.sync.dma_start(tile[:], rows.rearrange("(p j) c -> p j c", j=PACK))
 
         def load_words(tile, words):
-            nc.sync.dma_start(tile[:].bitcast(I32), words.rearrange("p t i -> p (t i)").bitcast(I32))
+            nc.sync.dma_start(tile.bitcast(I32), words.rearrange("p t i -> p (t i)").bitcast(I32))
 
+        def load_w4_scales(d):
+            nc.sync.dma_start(
+                w4_s_raw[32 * d : 32 * d + 4, :].bitcast(I32).rearrange("r (a c) -> r a c", a=PASSES),
+                w4_scales[:, 4 * d : 4 * d + 4, :].bitcast(I32).rearrange("a r c -> r a c"),
+            )
+
+        nc.sync.dma_start(tab_s[0:P:4, :].bitcast(I32), tab_scales.bitcast(I32).rearrange("a q t -> q a t"))
+        nc.sync.dma_start(wgo_rows[0 : GROUPS * CHUNKS, :], wgo[0:P:GP, :])
         nc.sync.dma_start(picks[:], offs)
         nc.sync.dma_start(bins[:], offs2)
+        load_words(tab_w0[:], tab_words[0])
+        for d in range(4):
+            load_w4_scales(d)
         nc.sync.dma_start(
             w4_raw[:].bitcast(I32).rearrange("p (a c) -> p a c", a=PASSES),
             w4_words.bitcast(I32).rearrange("a p c -> p a c"),
         )
-        load_words(tab_w0, tab_words[0])
+        tab_w1 = held("tab_w1", [P, T], U32)
+        load_words(tab_w1[:], tab_words[1])
         load_rows(wa_raw0, wa[0:512, :])
-        for e in range(2):
-            nc.scalar.dma_start(tab_s[e:P:GP, :].bitcast(I32), tab_scales[0, e:16:2, :].bitcast(I32))
-        nc.scalar.dma_start(tab_s[2:P:8, :].bitcast(I32), tab_scales[1].bitcast(I32))
-        for d in range(4):
-            nc.scalar.dma_start(
-                w4_s_raw[32 * d : 32 * d + 4, :].bitcast(I32).rearrange("r (a c) -> r a c", a=PASSES),
-                w4_scales[:, 4 * d : 4 * d + 4, :].bitcast(I32).rearrange("a r c -> r a c"),
-            )
-        nc.scalar.dma_start(wgo_rows[0:GROUPS, :], wgo[0:P:GP, :])
 
         nc.vector.tensor_copy(picked_s[:], tab_s[:].indirect(picks[:]))
-        tab_w1 = held("tab_w1", [P, T], U32, "tab_s")
-        load_words(tab_w1, tab_words[1])
-        nc.vector.tensor_copy(v_s[0][:].bitcast(I32), picked_s[:].bitcast(I32))
         for d in range(4):
-            nc.scalar.dma_start(v_s[1][32 * d : 32 * d + 4, :].bitcast(I32), picked_s[32 * d + 2 : 32 * d + 32 : 8, :].bitcast(I32))
-        for e in range(2):
-            nc.scalar.dma_start(v_s[0][2 + e : P : 32, :].bitcast(I32), picked_s[GP + e : P : 32, :].bitcast(I32))
+            nc.sync.dma_start(v_s[32 * d : 32 * d + 4, :].bitcast(I32), picked_s[32 * d : 32 * d + 32 : 4, :].bitcast(I32))
 
-        winv = held("winv", [P, CHUNKS, GROUPS], F32)
-        wroot = held("wroot", [P, CHUNKS, GROUPS], F32)
-        for half in range(2):
-            bank = psum2.tile([P, PACK, CH], F32, name="b_bank")
-            for c in range(PACK):
-                cc = PACK * half + c
-                nc.tensor.transpose(bank[:, c, :], wgo_rows[:, cc * CH : (cc + 1) * CH], ident[:])
-            nc.scalar.activation(wroot[:, PACK * half : PACK * (half + 1), :], bank[:, :, 0:GROUPS], ACT.Abs_reciprocal_sqrt)
-        nc.scalar.activation(winv[:], wroot[:], ACT.Square)
-
-        def regroup(name, raw, t0, t1, copy):
-            grouped = held(name, [P, t1 - t0, P, PACK], BF16)
+        def regroup(name, raw, t0, t1, copy, after=None, offset=None):
+            shape = [P, t1 - t0, P, PACK]
+            grouped = held(name, shape, BF16, after) if offset is None else placed(name, shape, BF16, offset)
             copy(grouped[:].rearrange("p t m j -> p m j t"), raw[:].rearrange("p j (m t) -> p m j t", t=PACK)[:, :, :, t0:t1])
             return grouped
 
@@ -129,77 +121,89 @@ def tile_list_allele_mixture_scores_kernel(
             nc.vector.quantize_mx(codes[:].bitcast(FP8X4), scales[:], grouped[:].rearrange("p t m j -> p (t m j)"))
             return [(codes[:, t * P : (t + 1) * P].bitcast(FP8X4), scales[:, t * P : (t + 1) * P]) for t in range(slices)]
 
+        winv = held("winv", [P, GROUPS * CHUNKS], F32)
+        wroot = held("wroot", [P, GROUPS * CHUNKS], F32)
+        w_bank = psum1.tile([P, PACK, CH], F32, name="r_bank")
+        nc.tensor.transpose(w_bank[:, 0, :], wgo_rows[:], ident[:])
+        nc.scalar.activation(wroot[:], w_bank[:, 0, 0 : GROUPS * CHUNKS], ACT.Abs_reciprocal_sqrt)
+        nc.scalar.activation(winv[:], wroot[:], ACT.Square)
+
         nc.vector.tensor_copy(v_w0[:], tab_w0[:].indirect(picks[:]))
-        wa_raw1 = held("wa_raw1", [P, PACK, H], F32, "tab_w0")
+        wa_raw1 = placed("wa_raw1", [P, PACK, H], F32, 7 * T)
         load_rows(wa_raw1, wa[512:1024, :])
-        w4_w = held("w4_w", [P, PASSES * 2 * H], U8)
-        w4_s = held("w4_s", [P, PASSES * H], U8)
-        nc.vector.tensor_copy(
-            w4_w[:].bitcast(U16).rearrange("p (a t m) -> p a t m", a=PASSES, t=PACK),
-            w4_raw[:].bitcast(U16).rearrange("p (a m t) -> p a t m", a=PASSES, t=PACK),
-        )
+        wb_raw = placed("wb_raw", [P, PACK, N], F32, T)
+        load_rows(wb_raw, wb)
+        w4_w = placed("w4_w", [P, PASSES * 2 * H], U8, 5 * T)
+        w4_s = placed("w4_s", [P, PASSES * H], U8, 6 * T)
         nc.vector.tensor_copy(
             w4_s[:].rearrange("p (a t m) -> p a t m", a=PASSES, t=PACK),
             w4_s_raw[:].rearrange("p (a m t) -> p a t m", a=PASSES, t=PACK),
         )
+        nc.vector.tensor_copy(
+            w4_w[:].bitcast(U16).rearrange("p (a t m) -> p a t m", a=PASSES, t=PACK),
+            w4_raw[:].bitcast(U16).rearrange("p (a m t) -> p a t m", a=PASSES, t=PACK),
+        )
         w8_s = w4_s_raw
         for d in range(4):
             nc.sync.dma_start(w8_s[32 * d : 32 * d + 4, 0:N].bitcast(I32), w8_scales[0, 4 * d : 4 * d + 4, :].bitcast(I32))
-        wa_g0 = regroup("wa_g0", wa_raw0, 0, PACK, nc.scalar.copy)
-        wb_raw = held("wb_raw", [P, PACK, N], F32, "wa_raw0")
-        load_rows(wb_raw, wb)
-        wa_q = [quantise("wa_q0", wa_g0)]
-        w8_w = held("w8_w", [P, N], U32, "wa_g0")
-        load_words(w8_w, w8_words[0])
+        w8_w = placed("w8_w", [P, N], U32, 11 * T + T // 2)
+        load_words(w8_w[:], w8_words[0])
 
-        def gather_words(c0, c1):
-            nc.vector.tensor_copy(v_w1[:, c0 * CH : c1 * CH], tab_w1[:].indirect(picks[:, c0 * CH // 16 : c1 * CH // 16]))
+        v_w1 = {}
+
+        def gather_words(c0, c1, after=None, offset=None):
+            shape = [P, (c1 - c0) * CH]
+            piece = held(f"v_w1_{c0}", shape, U32, after) if offset is None else placed(f"v_w1_{c0}", shape, U32, offset)
+            nc.vector.tensor_copy(piece[:], tab_w1[:].indirect(picks[:, c0 * CH // 16 : c1 * CH // 16]))
+            for c in range(c0, c1):
+                v_w1[c] = piece[:, (c - c0) * CH : (c - c0 + 1) * CH]
 
         h_w = held("h_w", [P, S], U32)
         h_s = held("h_s", [P, S], U8)
         h_bf = held("h_bf", [P, S * PACK], BF16)
 
-        def product(c, name, weights):
-            bank = psum2.tile([P, PACK, CH], F32, name=name)
-            for a in range(PASSES):
-                for t in range(PACK):
-                    codes, scales = weights[a][t]
-                    nc.tensor.matmul_mx(
-                        bank[:, t, :], lhsT=codes, lhsT_scale=scales,
-                        rhs=v_w[a][:, c * CH : (c + 1) * CH].bitcast(FP8X4), rhs_scale=v_s[a][:, c * CH : (c + 1) * CH],
-                        start=(a == 0 and t == 0), stop=(a == PASSES - 1 and t == PACK - 1),
-                    )
-            return bank
+        def add_pass(bank, c, a, weights):
+            words = v_w0[:, c * CH : (c + 1) * CH] if a == 0 else v_w1[c]
+            for t in range(PACK):
+                codes, scales = weights[a][t]
+                nc.tensor.matmul_mx(
+                    bank[:, t, :], lhsT=codes, lhsT_scale=scales,
+                    rhs=words.bitcast(FP8X4), rhs_scale=v_s[:, a * S + c * CH : a * S + (c + 1) * CH],
+                    start=(a == 0 and t == 0), stop=(a == PASSES - 1 and t == PACK - 1),
+                )
 
         w4_q = [
             [(w4_w[:, 2 * col : 2 * (col + P)].bitcast(FP4X4), w4_s[:, col : col + P]) for col in range(a * H, (a + 1) * H, P)]
             for a in range(PASSES)
         ]
 
-        def project(c):
-            x_bank = product(c, "x_bank", w4_q)
-            x_sb = ring.tile([P, CH, PACK], F32, name="x_sb")
-            nc.scalar.copy(x_sb[:], x_bank[:].rearrange("p t n -> p n t"))
-            return x_sb
+        x_sb = {}
 
-        def first_stage(c, x_sb=None):
-            if x_sb is None:
-                x_sb = project(c)
-            av_bank = product(c, "av_bank", wa_q)
+        def project(c):
+            x_bank = psum2.tile([P, PACK, CH], F32, name="x_bank")
+            for a in range(PASSES):
+                add_pass(x_bank, c, a, w4_q)
+            shape = [P, CH, PACK]
+            x_sb[c] = placed(f"x{c}", shape, F32, (7 + c - 1) * T) if 1 <= c < 5 else held(f"x{c}", shape, F32)
+            nc.scalar.copy(x_sb[c][:], x_bank[:].rearrange("p t n -> p n t"))
+
+        def open_product(c):
+            av_bank = psum2.tile([P, PACK, CH], F32, name="av_bank")
+            add_pass(av_bank, c, 0, wa_q)
+            return av_bank
+
+        def first_stage(c, av_bank=None):
+            av_bank = av_bank or open_product(c)
+            add_pass(av_bank, c, 1, wa_q)
             c0, c1 = cut_of(QUANTISE_CUTS, c)
-            nc.vector.tensor_tensor(h_bf[:, c * CH * PACK : (c + 1) * CH * PACK].rearrange("p (n t) -> p n t", t=PACK), av_bank[:].rearrange("p t n -> p n t"), x_sb[:], MULT)
+            nc.vector.tensor_tensor(h_bf[:, c * CH * PACK : (c + 1) * CH * PACK].rearrange("p (n t) -> p n t", t=PACK), av_bank[:].rearrange("p t n -> p n t"), x_sb[c][:], MULT)
             if c + 1 == c1:
                 nc.vector.quantize_mx(
                     h_w[:, c0 * CH : c1 * CH].bitcast(FP8X4), h_s[:, c0 * CH : c1 * CH], h_bf[:, c0 * CH * PACK : c1 * CH * PACK]
                 )
 
-        b_sb = held("b_sb", [P, PACK * S], F32)
-        damp = held("damp", [P, PACK * S], F32)
-
-        def piece_view(tile, c):
-            c0, c1 = cut_of(SCATTER_CUTS, c)
-            block = tile[:, PACK * c0 * CH : PACK * c1 * CH].rearrange("p (i j) -> p i j", i=PACK)
-            return block[:, :, (c - c0) * CH : (c - c0 + 1) * CH]
+        b_sb = held("b_sb", [P, PACK, S], F32)
+        damp = held("damp", [P, PACK, S], F32)
 
         def damping(c):
             hw = h_w[:, c * CH : (c + 1) * CH].bitcast(FP8X4)
@@ -210,9 +214,10 @@ def tile_list_allele_mixture_scores_kernel(
             nc.scalar.activation(sq[:], d_bank[:].rearrange("p (m i) -> p i m", i=PACK), ACT.Square)
             root = ring.tile([P, PACK, P], F32, name="root")
             for g in range(GROUPS):
+                factor = winv[:, g * CHUNKS + c : g * CHUNKS + c + 1]
                 nc.scalar.activation(
                     root[:, :, g * GP : (g + 1) * GP], sq[:, :, g * GP : (g + 1) * GP], ACT.Abs_reciprocal_sqrt,
-                    bias=winv[:, c, g : g + 1], scale=winv[:, c, g : g + 1],
+                    bias=factor, scale=factor,
                 )
             return root
 
@@ -227,45 +232,58 @@ def tile_list_allele_mixture_scores_kernel(
                     b_bank[:, i, :], lhsT=wb_q[i][0], lhsT_scale=wb_q[i][1],
                     rhs=hw, rhs_scale=hs, start=True, stop=True,
                 )
-            nc.scalar.copy(piece_view(b_sb, c), b_bank[:])
+            nc.scalar.copy(b_sb[:, :, c * CH : (c + 1) * CH], b_bank[:])
             r_bank = psum1.tile([P, PACK, CH], F32, name="r_bank")
             for i in range(PACK):
                 nc.tensor.transpose(r_bank[:, i, :], root[:, i, :], ident[:])
-            nc.scalar.activation(piece_view(damp, c), r_bank[:], ACT.Square)
+            nc.scalar.activation(damp[:, :, c * CH : (c + 1) * CH], r_bank[:], ACT.Square)
 
-        def scatter(k):
-            c0, c1 = SCATTER_CUTS[k], SCATTER_CUTS[k + 1]
-            width = (c1 - c0) * CH
+        def scatter(c):
             for i in range(PACK):
-                cols = slice(PACK * c0 * CH + i * width, PACK * c0 * CH + (i + 1) * width)
+                last_from = CHUNKS - LAST_PIECE[i]
+                if last_from <= c < CHUNKS - 1:
+                    continue
+                c0 = min(c, last_from)
                 nc.vector.tensor_tensor(
-                    pages[i][:].indirect(bins[:, c0 * CH // 16 : c1 * CH // 16]), b_sb[:, cols], damp[:, cols], MULT
+                    pages[i][:].indirect(bins[:, c0 * CH // 16 : (c + 1) * CH // 16]),
+                    b_sb[:, i, c0 * CH : (c + 1) * CH], damp[:, i, c0 * CH : (c + 1) * CH], MULT,
                 )
-                if c1 == CHUNKS:
+                if c == CHUNKS - 1:
                     nc.sync.dma_start(out.rearrange("(p i) t -> p i t", i=PACK)[:, i, :], pages[i][:])
 
-        for k in range(len(GATHER_CUTS) - 1):
-            gather_words(GATHER_CUTS[k], GATHER_CUTS[k + 1])
-        x_first = [project(0), project(1)]
-        low = regroup("wa_g1a", wa_raw1, 0, 2, nc.scalar.copy)
-        high = regroup("wa_g1b", wa_raw1, 2, PACK, nc.scalar.copy)
-        new_page("tab_s")
-        wa_q.append(quantise("wa_q1a", low) + quantise("wa_q1b", high))
-        new_page("tab_w0")
-        first_stage(0, x_first[0])
-        first_stage(1, x_first[1])
-        wb_q = quantise("wb_qa", regroup("wb_ga", wb_raw, 0, 2, nc.scalar.copy))
+        def prepare_wa(a, raw, after=None, offset=None):
+            low = regroup(f"wa_g{a}a", raw, 0, 2, nc.vector.tensor_copy)
+            high = regroup(f"wa_g{a}b", raw, 2, PACK, nc.scalar.copy, after, offset)
+            return quantise(f"wa_q{a}a", low) + quantise(f"wa_q{a}b", high)
+
+        gather_words(0, 2)
+        gather_words(2, CHUNKS, offset=12 * T + T // 2)
+        wa_q = [prepare_wa(0, wa_raw0, "wgo_rows")]
+        project(0)
+        opened = [open_product(0)]
+        wa_q.append(prepare_wa(1, wa_raw1, offset=18 * T))
+        first_stage(0, opened[0])
+        pages.append(placed("page2", [P, T2], F32, 14 * T + T // 2))
+        nc.vector.memset(pages[2][:].bitcast(I32), 0)
+        project(1)
+        opened.append(open_product(1))
+        project(2)
+        project(3)
+        first_stage(1, opened[1])
+        wb_q = quantise("wb_qa", regroup("wb_ga", wb_raw, 0, 2, nc.vector.tensor_copy, "wa_g1a"))
+        project(4)
         first_stage(2)
-        new_page("wb_ga")
         root_first = damping(0)
-        wb_q = wb_q + quantise("wb_qb", regroup("wb_gb", wb_raw, 2, PACK, nc.scalar.copy))
+        wb_q = wb_q + quantise("wb_qb", regroup("wb_gb", wb_raw, 2, PACK, nc.scalar.copy, offset=18 * T + T // 2))
+        project(5)
         first_stage(3)
         second_stage(0, wb_q, root_first)
-        order = ["s1", 4, "s2", 1, "sc", 0, "s1", 5, "s2", 2, "s1", 6, "sc", 1, "s1", 7, "s2", 3, "sc", 2, "s2", 4, "sc", 3, "s2", 5, "s2", 6, "s2", 7, "sc", 4]
-        for what, c in zip(order[0::2], order[1::2]):
-            if what == "s1":
-                first_stage(c)
-            elif what == "s2":
-                second_stage(c, wb_q)
-            else:
-                scatter(c)
+        new_page("x0")
+        for c in range(CHUNKS):
+            if c + AHEAD + 2 < CHUNKS:
+                project(c + AHEAD + 2)
+            if c + AHEAD < CHUNKS:
+                first_stage(c + AHEAD)
+            if c + 1 < CHUNKS:
+                second_stage(c + 1, wb_q)
+            scatter(c)

@@ -24,13 +24,10 @@ CH = 128
 CHUNKS = S // CH
 GROUPS = 8
 GP = P // GROUPS
+OPENED = 4
+GATHER_CUTS = (0, 2, 4, 8)
 QUANTISE_CUTS = (0, 1, 2, 4, 6, 8)
-LAST_PIECE = (1, 2, 3, 4)
-AHEAD = 4
-
-
-def cut_of(cuts, c):
-    return max(lo for lo in cuts if lo <= c), min(hi for hi in cuts if hi > c)
+SCATTER_CUTS = ((0, 1, 2, 4, 6, 8), (0, 1, 2, 4, 6, 8), (0, 1, 2, 4, 5, 8), (0, 1, 2, 4, 5, 8))
 
 
 def tile_list_allele_mixture_scores_kernel(
@@ -41,100 +38,108 @@ def tile_list_allele_mixture_scores_kernel(
         keep = ctx.enter_context(tc.tile_pool(name="keep", bufs=1))
         laid = ctx.enter_context(tc.tile_pool(name="laid", bufs=1))
         ring = ctx.enter_context(tc.tile_pool(name="ring", bufs=2))
-        psum2 = ctx.enter_context(tc.psum_pool(name="psum2", bufs=2))
-        psum1 = ctx.enter_context(tc.psum_pool(name="psum1", bufs=1))
+        psum = ctx.enter_context(tc.psum_pool(name="psum", bufs=1))
 
-        def held(name, shape, dtype, after=None):
-            return keep.tile(shape, dtype, name=name, tag=after or name, align_bytes=64)
+        def held(name, shape, dtype):
+            return keep.tile(shape, dtype, name=name, align_bytes=64)
 
         def placed(name, shape, dtype, offset):
             return laid.tile(shape, dtype, name=name, align_bytes=64, offset=offset)
 
+        def new_bank(name, bank):
+            return psum.tile([P, PACK, CH], F32, name=name, tag=f"bank{bank}")
+
+        at_wa_g0 = 0
+        at_wa_g1 = at_wa_g0 + 2 * PACK * H
+        at_x = at_wa_g1 + 2 * PACK * H
+        at_wroot = at_wa_g1 - 2 * GROUPS * CHUNKS
+
         picks = keep.tile([P, S // 16], U16, name="picks")
         bins = keep.tile([P, S // 16], U16, name="bins")
         tab_s = held("tab_s", [P, T], U8)
-        tab_w0 = placed("tab_w0", [P, T], U32, 4 * T)
-        w4_raw = placed("w4_raw", [P, PASSES * 2 * H], U8, 12 * T)
-        w4_s_raw = held("w4_s_raw", [P, PASSES * H], U8)
         wgo_rows = held("wgo_rows", [P, CH], F32)
-        picked_s = held("picked_s", [P, S], U8)
-        v_s = held("v_s", [P, PASSES * S], U8)
-        v_w0 = held("v_w0", [P, S], U32)
+        w4_s_raw = held("w4_s_raw", [P, PASSES * H], U8)
         ident = held("ident", [P, P], F32)
-        wa_raw0 = held("wa_raw0", [P, PACK, H], F32)
-        pages = [held(f"page{i}", [P, T2], F32) for i in range(2)]
+        pages = [held(f"page{i}", [P, T2], F32) for i in range(PACK - 1)]
 
-        nc.gpsimd.memset(w4_s_raw[:].bitcast(I32), 0)
         nc.gpsimd.memset(tab_s[:].bitcast(I32), 0)
         nc.gpsimd.memset(wgo_rows[:], 0.0)
+        nc.gpsimd.memset(w4_s_raw[:].bitcast(I32), 0)
         make_identity(nc, ident[:])
         for lo, hi in ((0, T2 // 2 + 1), (T2 // 2 + 1, T2 // 2 + 2), (T2 // 2 + 2, T2)):
             nc.vector.memset(pages[0][:, lo:hi].bitcast(I32), 0)
+        v_s = held("v_s", [P, PASSES * S], U8)
         nc.vector.memset(v_s[:].bitcast(I32), 0)
-        nc.vector.memset(pages[1][:].bitcast(I32), 0)
-
-        def new_page(after):
-            pages.append(held(f"page{len(pages)}", [P, T2], F32, after))
-            nc.vector.memset(pages[-1][:].bitcast(I32), 0)
+        for page in pages[1:]:
+            nc.vector.memset(page[:].bitcast(I32), 0)
 
         def load_rows(tile, rows):
             nc.sync.dma_start(tile[:], rows.rearrange("(p j) c -> p j c", j=PACK))
 
         def load_words(tile, words):
-            nc.sync.dma_start(tile.bitcast(I32), words.rearrange("p t i -> p (t i)").bitcast(I32))
+            nc.sync.dma_start(tile[:].bitcast(I32), words.rearrange("p t i -> p (t i)").bitcast(I32))
 
-        def load_w4_scales(d):
-            nc.sync.dma_start(
+        nc.sync.dma_start(picks[:], offs)
+        nc.sync.dma_start(bins[:], offs2)
+        wa_raw0 = held("wa_raw0", [P, PACK, H], F32)
+        load_rows(wa_raw0, wa[0:512, :])
+        tab_w0 = held("tab_w0", [P, T], U32)
+        load_words(tab_w0, tab_words[0])
+        nc.scalar.dma_start(tab_s[0:P:4, :].bitcast(I32), tab_scales.bitcast(I32).rearrange("a q t -> q a t"))
+        nc.scalar.dma_start(wgo_rows[0 : GROUPS * CHUNKS, :], wgo[0:P:GP, :])
+        for d in range(4):
+            nc.scalar.dma_start(
                 w4_s_raw[32 * d : 32 * d + 4, :].bitcast(I32).rearrange("r (a c) -> r a c", a=PASSES),
                 w4_scales[:, 4 * d : 4 * d + 4, :].bitcast(I32).rearrange("a r c -> r a c"),
             )
 
-        nc.sync.dma_start(tab_s[0:P:4, :].bitcast(I32), tab_scales.bitcast(I32).rearrange("a q t -> q a t"))
-        nc.sync.dma_start(wgo_rows[0 : GROUPS * CHUNKS, :], wgo[0:P:GP, :])
-        nc.sync.dma_start(picks[:], offs)
-        nc.sync.dma_start(bins[:], offs2)
-        load_words(tab_w0[:], tab_words[0])
-        for d in range(4):
-            load_w4_scales(d)
+        winv = held("winv", [P, GROUPS * CHUNKS], F32)
+        w_bank = new_bank("w_bank", 7)
+        nc.tensor.transpose(w_bank[:, 0, :], wgo_rows[:], ident[:])
+        wroot = placed("wroot", [P, GROUPS * CHUNKS], F32, at_wroot)
+        nc.scalar.activation(wroot[:], w_bank[:, 0, 0 : GROUPS * CHUNKS], ACT.Abs_reciprocal_sqrt)
+        nc.scalar.activation(winv[:], wroot[:], ACT.Square)
+
+        wa_raw1 = held("wa_raw1", [P, PACK, H], F32)
+        load_rows(wa_raw1, wa[512:1024, :])
+        w4_raw = held("w4_raw", [P, PASSES * 2 * H], U8)
         nc.sync.dma_start(
             w4_raw[:].bitcast(I32).rearrange("p (a c) -> p a c", a=PASSES),
             w4_words.bitcast(I32).rearrange("a p c -> p a c"),
         )
-        tab_w1 = held("tab_w1", [P, T], U32)
-        load_words(tab_w1[:], tab_words[1])
-        load_rows(wa_raw0, wa[0:512, :])
 
+        picked_s = held("picked_s", [P, S], U8)
         nc.vector.tensor_copy(picked_s[:], tab_s[:].indirect(picks[:]))
         for d in range(4):
             nc.sync.dma_start(v_s[32 * d : 32 * d + 4, :].bitcast(I32), picked_s[32 * d : 32 * d + 32 : 4, :].bitcast(I32))
+        tab_w1 = held("tab_w1", [P, T], U32)
+        load_words(tab_w1, tab_words[1])
+        wb_raw = held("wb_raw", [P, PACK, N], F32)
+        load_rows(wb_raw, wb)
+        w8_w = held("w8_w", [P, N], U32)
+        load_words(w8_w, w8_words[0])
 
-        def regroup(name, raw, t0, t1, copy, after=None, offset=None):
-            shape = [P, t1 - t0, P, PACK]
-            grouped = held(name, shape, BF16, after) if offset is None else placed(name, shape, BF16, offset)
-            copy(grouped[:].rearrange("p t m j -> p m j t"), raw[:].rearrange("p j (m t) -> p m j t", t=PACK)[:, :, :, t0:t1])
-            return grouped
+
+        def regroup(copy, grouped, raw):
+            copy(grouped.rearrange("p t m j -> p m j t"), raw[:].rearrange("p j (m t) -> p m j t", t=PACK))
+
+        wa_g0 = placed("wa_g0", [P, PACK, P, PACK], BF16, at_wa_g0)
+        regroup(nc.scalar.copy, wa_g0[:], wa_raw0)
+
+        v_w0 = held("v_w0", [P, S], U32)
+        nc.vector.tensor_copy(v_w0[:], tab_w0[:].indirect(picks[:]))
 
         def quantise(name, grouped):
-            slices = grouped.shape[1]
-            codes = held(name + "_w", [P, slices * P], U32)
-            scales = held(name + "_s", [P, slices * P], U8)
+            codes = held(name + "_w", [P, PACK * P], U32)
+            scales = held(name + "_s", [P, PACK * P], U8)
             nc.vector.quantize_mx(codes[:].bitcast(FP8X4), scales[:], grouped[:].rearrange("p t m j -> p (t m j)"))
-            return [(codes[:, t * P : (t + 1) * P].bitcast(FP8X4), scales[:, t * P : (t + 1) * P]) for t in range(slices)]
+            return [(codes[:, t * P : (t + 1) * P].bitcast(FP8X4), scales[:, t * P : (t + 1) * P]) for t in range(PACK)]
 
-        winv = held("winv", [P, GROUPS * CHUNKS], F32)
-        wroot = held("wroot", [P, GROUPS * CHUNKS], F32)
-        w_bank = psum1.tile([P, PACK, CH], F32, name="r_bank")
-        nc.tensor.transpose(w_bank[:, 0, :], wgo_rows[:], ident[:])
-        nc.scalar.activation(wroot[:], w_bank[:, 0, 0 : GROUPS * CHUNKS], ACT.Abs_reciprocal_sqrt)
-        nc.scalar.activation(winv[:], wroot[:], ACT.Square)
+        wa_g1 = placed("wa_g1", [P, PACK, P, PACK], BF16, at_wa_g1)
+        regroup(nc.scalar.copy, wa_g1[:], wa_raw1)
 
-        nc.vector.tensor_copy(v_w0[:], tab_w0[:].indirect(picks[:]))
-        wa_raw1 = placed("wa_raw1", [P, PACK, H], F32, 7 * T)
-        load_rows(wa_raw1, wa[512:1024, :])
-        wb_raw = placed("wb_raw", [P, PACK, N], F32, T)
-        load_rows(wb_raw, wb)
-        w4_w = placed("w4_w", [P, PASSES * 2 * H], U8, 5 * T)
-        w4_s = placed("w4_s", [P, PASSES * H], U8, 6 * T)
+        w4_w = held("w4_w", [P, PASSES * 2 * H], U8)
+        w4_s = held("w4_s", [P, PASSES * H], U8)
         nc.vector.tensor_copy(
             w4_s[:].rearrange("p (a t m) -> p a t m", a=PASSES, t=PACK),
             w4_s_raw[:].rearrange("p (a m t) -> p a t m", a=PASSES, t=PACK),
@@ -143,24 +148,23 @@ def tile_list_allele_mixture_scores_kernel(
             w4_w[:].bitcast(U16).rearrange("p (a t m) -> p a t m", a=PASSES, t=PACK),
             w4_raw[:].bitcast(U16).rearrange("p (a m t) -> p a t m", a=PASSES, t=PACK),
         )
+        w4_q = [
+            [(w4_w[:, 2 * col : 2 * (col + P)].bitcast(FP4X4), w4_s[:, col : col + P]) for col in range(a * H, (a + 1) * H, P)]
+            for a in range(PASSES)
+        ]
+        wa_q = [quantise("wa_q0", wa_g0), quantise("wa_q1", wa_g1)]
         w8_s = w4_s_raw
         for d in range(4):
             nc.sync.dma_start(w8_s[32 * d : 32 * d + 4, 0:N].bitcast(I32), w8_scales[0, 4 * d : 4 * d + 4, :].bitcast(I32))
-        w8_w = placed("w8_w", [P, N], U32, 11 * T + T // 2)
-        load_words(w8_w[:], w8_words[0])
 
         v_w1 = {}
 
-        def gather_words(c0, c1, after=None, offset=None):
-            shape = [P, (c1 - c0) * CH]
-            piece = held(f"v_w1_{c0}", shape, U32, after) if offset is None else placed(f"v_w1_{c0}", shape, U32, offset)
-            nc.vector.tensor_copy(piece[:], tab_w1[:].indirect(picks[:, c0 * CH // 16 : c1 * CH // 16]))
+        def gather_words(piece):
+            c0, c1 = GATHER_CUTS[piece : piece + 2]
+            picked = placed(f"v_w1_{c0}", [P, (c1 - c0) * CH], U32, at_wa_g1 + 4 * c0 * CH)
+            nc.vector.tensor_copy(picked[:], tab_w1[:].indirect(picks[:, c0 * CH // 16 : c1 * CH // 16]))
             for c in range(c0, c1):
-                v_w1[c] = piece[:, (c - c0) * CH : (c - c0 + 1) * CH]
-
-        h_w = held("h_w", [P, S], U32)
-        h_s = held("h_s", [P, S], U8)
-        h_bf = held("h_bf", [P, S * PACK], BF16)
+                v_w1[c] = picked[:, (c - c0) * CH : (c - c0 + 1) * CH]
 
         def add_pass(bank, c, a, weights):
             words = v_w0[:, c * CH : (c + 1) * CH] if a == 0 else v_w1[c]
@@ -172,46 +176,52 @@ def tile_list_allele_mixture_scores_kernel(
                     start=(a == 0 and t == 0), stop=(a == PASSES - 1 and t == PACK - 1),
                 )
 
-        w4_q = [
-            [(w4_w[:, 2 * col : 2 * (col + P)].bitcast(FP4X4), w4_s[:, col : col + P]) for col in range(a * H, (a + 1) * H, P)]
-            for a in range(PASSES)
-        ]
+        h_w = held("h_w", [P, S], U32)
+        h_s = held("h_s", [P, S], U8)
+        h_bf = held("h_bf", [P, S * PACK], BF16)
+        banks = {}
 
         x_sb = {}
 
+        def open_sum(name, c, weights):
+            banks[name, c] = new_bank(f"{name}{c}", OPENED + c % OPENED if name == "av_bank" else c if c < OPENED else c % 2)
+            add_pass(banks[name, c], c, 0, weights)
+
         def project(c):
-            x_bank = psum2.tile([P, PACK, CH], F32, name="x_bank")
-            for a in range(PASSES):
-                add_pass(x_bank, c, a, w4_q)
-            shape = [P, CH, PACK]
-            x_sb[c] = placed(f"x{c}", shape, F32, (7 + c - 1) * T) if 1 <= c < 5 else held(f"x{c}", shape, F32)
-            nc.scalar.copy(x_sb[c][:], x_bank[:].rearrange("p t n -> p n t"))
+            if ("x_bank", c) not in banks:
+                open_sum("x_bank", c, w4_q)
+            add_pass(banks["x_bank", c], c, 1, w4_q)
+            x_sb[c] = placed(f"x{c}", [P, CH, PACK], F32, at_x + 4 * CH * PACK * c)
+            nc.scalar.copy(x_sb[c][:], banks["x_bank", c][:].rearrange("p t n -> p n t"))
 
-        def open_product(c):
-            av_bank = psum2.tile([P, PACK, CH], F32, name="av_bank")
-            add_pass(av_bank, c, 0, wa_q)
-            return av_bank
-
-        def first_stage(c, av_bank=None):
-            av_bank = av_bank or open_product(c)
+        def first_stage(c):
+            if ("av_bank", c) not in banks:
+                open_sum("av_bank", c, wa_q)
+            av_bank = banks["av_bank", c]
             add_pass(av_bank, c, 1, wa_q)
-            c0, c1 = cut_of(QUANTISE_CUTS, c)
-            nc.vector.tensor_tensor(h_bf[:, c * CH * PACK : (c + 1) * CH * PACK].rearrange("p (n t) -> p n t", t=PACK), av_bank[:].rearrange("p t n -> p n t"), x_sb[c][:], MULT)
-            if c + 1 == c1:
-                nc.vector.quantize_mx(
-                    h_w[:, c0 * CH : c1 * CH].bitcast(FP8X4), h_s[:, c0 * CH : c1 * CH], h_bf[:, c0 * CH * PACK : c1 * CH * PACK]
-                )
+            nc.vector.tensor_tensor(
+                h_bf[:, c * CH * PACK : (c + 1) * CH * PACK].rearrange("p (n t) -> p n t", t=PACK),
+                av_bank[:].rearrange("p t n -> p n t"), x_sb[c][:], MULT,
+            )
+
+        def quantise_h(piece):
+            c0, c1 = QUANTISE_CUTS[piece : piece + 2]
+            nc.vector.quantize_mx(
+                h_w[:, c0 * CH : c1 * CH].bitcast(FP8X4), h_s[:, c0 * CH : c1 * CH], h_bf[:, c0 * CH * PACK : c1 * CH * PACK]
+            )
 
         b_sb = held("b_sb", [P, PACK, S], F32)
         damp = held("damp", [P, PACK, S], F32)
 
+        roots = {}
+
         def damping(c):
             hw = h_w[:, c * CH : (c + 1) * CH].bitcast(FP8X4)
             hs = h_s[:, c * CH : (c + 1) * CH]
-            d_bank = psum1.tile([P, N], F32, name="d_bank")
-            nc.tensor.matmul_mx(d_bank[:], lhsT=hw, lhsT_scale=hs, rhs=w8_w[:].bitcast(FP8X4), rhs_scale=w8_s[:, 0:N], start=True, stop=True)
+            d_bank = new_bank(f"d_bank{c}", (2, 0)[c % 2])[:].rearrange("p i m -> p (i m)")
+            nc.tensor.matmul_mx(d_bank, lhsT=hw, lhsT_scale=hs, rhs=w8_w[:].bitcast(FP8X4), rhs_scale=w8_s[:, 0:N], start=True, stop=True)
             sq = ring.tile([P, PACK, P], F32, name="sq")
-            nc.scalar.activation(sq[:], d_bank[:].rearrange("p (m i) -> p i m", i=PACK), ACT.Square)
+            nc.scalar.activation(sq[:], d_bank.rearrange("p (m i) -> p i m", i=PACK), ACT.Square)
             root = ring.tile([P, PACK, P], F32, name="root")
             for g in range(GROUPS):
                 factor = winv[:, g * CHUNKS + c : g * CHUNKS + c + 1]
@@ -219,71 +229,68 @@ def tile_list_allele_mixture_scores_kernel(
                     root[:, :, g * GP : (g + 1) * GP], sq[:, :, g * GP : (g + 1) * GP], ACT.Abs_reciprocal_sqrt,
                     bias=factor, scale=factor,
                 )
-            return root
+            roots[c] = root
 
-        def second_stage(c, wb_q, root=None):
-            if root is None:
-                root = damping(c)
+        def second_stage(c):
+            if c not in roots:
+                damping(c)
+            root = roots[c]
             hw = h_w[:, c * CH : (c + 1) * CH].bitcast(FP8X4)
             hs = h_s[:, c * CH : (c + 1) * CH]
-            b_bank = psum2.tile([P, PACK, CH], F32, name="b_bank")
+            b_bank = new_bank(f"b_bank{c}", 4 + c % 2)
             for i in range(PACK):
                 nc.tensor.matmul_mx(
                     b_bank[:, i, :], lhsT=wb_q[i][0], lhsT_scale=wb_q[i][1],
                     rhs=hw, rhs_scale=hs, start=True, stop=True,
                 )
             nc.scalar.copy(b_sb[:, :, c * CH : (c + 1) * CH], b_bank[:])
-            r_bank = psum1.tile([P, PACK, CH], F32, name="r_bank")
+            r_bank = new_bank(f"r_bank{c}", (3, 1)[c % 2])
             for i in range(PACK):
                 nc.tensor.transpose(r_bank[:, i, :], root[:, i, :], ident[:])
             nc.scalar.activation(damp[:, :, c * CH : (c + 1) * CH], r_bank[:], ACT.Square)
 
         def scatter(c):
             for i in range(PACK):
-                last_from = CHUNKS - LAST_PIECE[i]
-                if last_from <= c < CHUNKS - 1:
-                    continue
-                c0 = min(c, last_from)
-                nc.vector.tensor_tensor(
-                    pages[i][:].indirect(bins[:, c0 * CH // 16 : (c + 1) * CH // 16]),
-                    b_sb[:, i, c0 * CH : (c + 1) * CH], damp[:, i, c0 * CH : (c + 1) * CH], MULT,
-                )
-                if c == CHUNKS - 1:
-                    nc.sync.dma_start(out.rearrange("(p i) t -> p i t", i=PACK)[:, i, :], pages[i][:])
+                if c + 1 in SCATTER_CUTS[i]:
+                    c0 = max(cut for cut in SCATTER_CUTS[i] if cut <= c)
+                    nc.vector.tensor_tensor(
+                        pages[i][:].indirect(bins[:, c0 * CH // 16 : (c + 1) * CH // 16]),
+                        b_sb[:, i, c0 * CH : (c + 1) * CH], damp[:, i, c0 * CH : (c + 1) * CH], MULT,
+                    )
+                    if c == CHUNKS - 1:
+                        nc.sync.dma_start(out.rearrange("(p i) t -> p i t", i=PACK)[:, i, :], pages[i][:])
 
-        def prepare_wa(a, raw, after=None, offset=None):
-            low = regroup(f"wa_g{a}a", raw, 0, 2, nc.vector.tensor_copy)
-            high = regroup(f"wa_g{a}b", raw, 2, PACK, nc.scalar.copy, after, offset)
-            return quantise(f"wa_q{a}a", low) + quantise(f"wa_q{a}b", high)
-
-        gather_words(0, 2)
-        gather_words(2, CHUNKS, offset=12 * T + T // 2)
-        wa_q = [prepare_wa(0, wa_raw0, "wgo_rows")]
-        project(0)
-        opened = [open_product(0)]
-        wa_q.append(prepare_wa(1, wa_raw1, offset=18 * T))
-        first_stage(0, opened[0])
-        pages.append(placed("page2", [P, T2], F32, 14 * T + T // 2))
-        nc.vector.memset(pages[2][:].bitcast(I32), 0)
-        project(1)
-        opened.append(open_product(1))
-        project(2)
-        project(3)
-        first_stage(1, opened[1])
-        wb_q = quantise("wb_qa", regroup("wb_ga", wb_raw, 0, 2, nc.vector.tensor_copy, "wa_g1a"))
+        for c in range(OPENED):
+            open_sum("av_bank", c, wa_q)
+            open_sum("x_bank", c, w4_q)
+        gather_words(0)
+        gather_words(1)
+        gather_words(2)
+        for c in range(OPENED):
+            project(c)
+            first_stage(c)
+            if c in (1, 2):
+                quantise_h(c - 1)
+        pages.append(placed("page3", [P, T2], F32, at_x))
+        nc.vector.memset(pages[3][:].bitcast(I32), 0)
+        quantise_h(2)
+        wb_g = held("wb_g", [P, PACK, P, PACK], BF16)
+        regroup(nc.scalar.copy, wb_g[:], wb_raw)
         project(4)
-        first_stage(2)
-        root_first = damping(0)
-        wb_q = wb_q + quantise("wb_qb", regroup("wb_gb", wb_raw, 2, PACK, nc.scalar.copy, offset=18 * T + T // 2))
+        first_stage(4)
         project(5)
-        first_stage(3)
-        second_stage(0, wb_q, root_first)
-        new_page("x0")
-        for c in range(CHUNKS):
-            if c + AHEAD + 2 < CHUNKS:
-                project(c + AHEAD + 2)
-            if c + AHEAD < CHUNKS:
-                first_stage(c + AHEAD)
+        first_stage(5)
+        damping(0)
+        wb_q = quantise("wb_q", wb_g)
+        quantise_h(3)
+        for c in range(6, CHUNKS):
+            project(c)
+            first_stage(c)
+        second_stage(0)
+        second_stage(1)
+        scatter(0)
+        quantise_h(4)
+        for c in range(1, CHUNKS):
             if c + 1 < CHUNKS:
-                second_stage(c + 1, wb_q)
+                second_stage(c + 1)
             scatter(c)

@@ -27,7 +27,8 @@ GP = P // GROUPS
 OPENED = 4
 GATHER_CUTS = (0, 2, 4, 8)
 QUANTISE_CUTS = (0, 1, 2, 4, 6, 8)
-SCATTER_CUTS = ((0, 1, 2, 4, 6, 8), (0, 1, 2, 4, 6, 8), (0, 1, 2, 4, 5, 8), (0, 1, 2, 4, 5, 8))
+PAGES = PACK - 1
+SCATTER_CUTS = ((0, 1, 2, 4, 6, 8), (0, 1, 2, 4, 6, 8), (0, 1, 2, 4, 8))
 
 
 def tile_list_allele_mixture_scores_kernel(
@@ -60,7 +61,7 @@ def tile_list_allele_mixture_scores_kernel(
         wgo_rows = held("wgo_rows", [P, CH], F32)
         w4_s_raw = held("w4_s_raw", [P, PASSES * H], U8)
         ident = held("ident", [P, P], F32)
-        pages = [held(f"page{i}", [P, T2], F32) for i in range(PACK - 1)]
+        pages = [held(f"page{i}", [P, T2], F32) for i in range(PAGES - 1)]
 
         nc.gpsimd.memset(tab_s[:].bitcast(I32), 0)
         nc.gpsimd.memset(wgo_rows[:], 0.0)
@@ -120,24 +121,32 @@ def tile_list_allele_mixture_scores_kernel(
         load_words(w8_w, w8_words[0])
 
 
-        def regroup(copy, grouped, raw):
-            copy(grouped.rearrange("p t m j -> p m j t"), raw[:].rearrange("p j (m t) -> p m j t", t=PACK))
+        def regroup(copy, grouped, raw, t0=0, t1=PACK):
+            copy(grouped.rearrange("p t m j -> p m j t"), raw[:].rearrange("p j (m t) -> p m j t", t=PACK)[:, :, :, t0:t1])
 
         wa_g0 = placed("wa_g0", [P, PACK, P, PACK], BF16, at_wa_g0)
         regroup(nc.scalar.copy, wa_g0[:], wa_raw0)
 
-        v_w0 = held("v_w0", [P, S], U32)
-        nc.vector.tensor_copy(v_w0[:], tab_w0[:].indirect(picks[:]))
+        v_w = {}
+
+        def gather_words(a, c0, c1, picked):
+            nc.vector.tensor_copy(picked[:], (tab_w0, tab_w1)[a][:].indirect(picks[:, c0 * CH // 16 : c1 * CH // 16]))
+            for c in range(c0, c1):
+                v_w[a, c] = picked[:, (c - c0) * CH : (c - c0 + 1) * CH]
+
+        gather_words(0, 0, OPENED, held("v_w0_low", [P, OPENED * CH], U32))
 
         def quantise(name, grouped):
-            codes = held(name + "_w", [P, PACK * P], U32)
-            scales = held(name + "_s", [P, PACK * P], U8)
+            slices = grouped.shape[1]
+            codes = held(name + "_w", [P, slices * P], U32)
+            scales = held(name + "_s", [P, slices * P], U8)
             nc.vector.quantize_mx(codes[:].bitcast(FP8X4), scales[:], grouped[:].rearrange("p t m j -> p (t m j)"))
-            return [(codes[:, t * P : (t + 1) * P].bitcast(FP8X4), scales[:, t * P : (t + 1) * P]) for t in range(PACK)]
+            return [(codes[:, t * P : (t + 1) * P].bitcast(FP8X4), scales[:, t * P : (t + 1) * P]) for t in range(slices)]
 
         wa_g1 = placed("wa_g1", [P, PACK, P, PACK], BF16, at_wa_g1)
         regroup(nc.scalar.copy, wa_g1[:], wa_raw1)
 
+        wa_q = [quantise("wa_q0", wa_g0)]
         w4_w = held("w4_w", [P, PASSES * 2 * H], U8)
         w4_s = held("w4_s", [P, PASSES * H], U8)
         nc.vector.tensor_copy(
@@ -152,22 +161,14 @@ def tile_list_allele_mixture_scores_kernel(
             [(w4_w[:, 2 * col : 2 * (col + P)].bitcast(FP4X4), w4_s[:, col : col + P]) for col in range(a * H, (a + 1) * H, P)]
             for a in range(PASSES)
         ]
-        wa_q = [quantise("wa_q0", wa_g0), quantise("wa_q1", wa_g1)]
+        gather_words(0, OPENED, CHUNKS, placed("v_w0_high", [P, (CHUNKS - OPENED) * CH], U32, at_wa_g0))
+        wa_q.append(quantise("wa_q1", wa_g1))
         w8_s = w4_s_raw
         for d in range(4):
             nc.sync.dma_start(w8_s[32 * d : 32 * d + 4, 0:N].bitcast(I32), w8_scales[0, 4 * d : 4 * d + 4, :].bitcast(I32))
 
-        v_w1 = {}
-
-        def gather_words(piece):
-            c0, c1 = GATHER_CUTS[piece : piece + 2]
-            picked = placed(f"v_w1_{c0}", [P, (c1 - c0) * CH], U32, at_wa_g1 + 4 * c0 * CH)
-            nc.vector.tensor_copy(picked[:], tab_w1[:].indirect(picks[:, c0 * CH // 16 : c1 * CH // 16]))
-            for c in range(c0, c1):
-                v_w1[c] = picked[:, (c - c0) * CH : (c - c0 + 1) * CH]
-
         def add_pass(bank, c, a, weights):
-            words = v_w0[:, c * CH : (c + 1) * CH] if a == 0 else v_w1[c]
+            words = v_w[a, c]
             for t in range(PACK):
                 codes, scales = weights[a][t]
                 nc.tensor.matmul_mx(
@@ -213,84 +214,131 @@ def tile_list_allele_mixture_scores_kernel(
         b_sb = held("b_sb", [P, PACK, S], F32)
         damp = held("damp", [P, PACK, S], F32)
 
-        roots = {}
+        squares, roots = {}, {}
 
-        def damping(c):
-            hw = h_w[:, c * CH : (c + 1) * CH].bitcast(FP8X4)
-            hs = h_s[:, c * CH : (c + 1) * CH]
-            d_bank = new_bank(f"d_bank{c}", (2, 0)[c % 2])[:].rearrange("p i m -> p (i m)")
-            nc.tensor.matmul_mx(d_bank, lhsT=hw, lhsT_scale=hs, rhs=w8_w[:].bitcast(FP8X4), rhs_scale=w8_s[:, 0:N], start=True, stop=True)
-            sq = ring.tile([P, PACK, P], F32, name="sq")
-            nc.scalar.activation(sq[:], d_bank.rearrange("p (m i) -> p i m", i=PACK), ACT.Square)
-            root = ring.tile([P, PACK, P], F32, name="root")
+        def h_of(c):
+            return h_w[:, c * CH : (c + 1) * CH].bitcast(FP8X4), h_s[:, c * CH : (c + 1) * CH]
+
+        def multiply_d(c):
+            hw, hs = h_of(c)
+            banks["d", c] = new_bank(f"d_bank{c}", (2, 0)[c % 2])[:].rearrange("p i m -> p (i m)")
+            nc.tensor.matmul_mx(
+                banks["d", c], lhsT=hw, lhsT_scale=hs, rhs=w8_w[:].bitcast(FP8X4), rhs_scale=w8_s[:, 0:N], start=True, stop=True
+            )
+
+        def square_d(c):
+            squares[c] = ring.tile([P, PACK, P], F32, name="sq")
+            nc.scalar.activation(squares[c][:], banks["d", c].rearrange("p (m i) -> p i m", i=PACK), ACT.Square)
+
+        def take_roots(c):
+            roots[c] = held(f"root{c}", [P, PACK, P], F32)
             for g in range(GROUPS):
                 factor = winv[:, g * CHUNKS + c : g * CHUNKS + c + 1]
                 nc.scalar.activation(
-                    root[:, :, g * GP : (g + 1) * GP], sq[:, :, g * GP : (g + 1) * GP], ACT.Abs_reciprocal_sqrt,
+                    roots[c][:, :, g * GP : (g + 1) * GP], squares[c][:, :, g * GP : (g + 1) * GP], ACT.Abs_reciprocal_sqrt,
                     bias=factor, scale=factor,
                 )
-            roots[c] = root
+
+        def multiply_b(c):
+            hw, hs = h_of(c)
+            banks["b", c] = new_bank(f"b_bank{c}", 4 + c % 2)
+            for i in range(PAGES):
+                nc.tensor.matmul_mx(
+                    banks["b", c][:, i, :], lhsT=wb_q[i][0], lhsT_scale=wb_q[i][1], rhs=hw, rhs_scale=hs, start=True, stop=True
+                )
+
+        def copy_b(c):
+            nc.scalar.copy(b_sb[:, 0:PAGES, c * CH : (c + 1) * CH], banks["b", c][:, 0:PAGES, :])
+
+        def turn_roots(c):
+            banks["r", c] = new_bank(f"r_bank{c}", (3, 1)[c % 2])
+            for i in range(PAGES):
+                nc.tensor.transpose(banks["r", c][:, i, :], roots[c][:, i, :], ident[:])
+
+        def square_roots(c):
+            nc.scalar.activation(damp[:, 0:PAGES, c * CH : (c + 1) * CH], banks["r", c][:, 0:PAGES, :], ACT.Square)
 
         def second_stage(c):
-            if c not in roots:
-                damping(c)
-            root = roots[c]
-            hw = h_w[:, c * CH : (c + 1) * CH].bitcast(FP8X4)
-            hs = h_s[:, c * CH : (c + 1) * CH]
-            b_bank = new_bank(f"b_bank{c}", 4 + c % 2)
-            for i in range(PACK):
-                nc.tensor.matmul_mx(
-                    b_bank[:, i, :], lhsT=wb_q[i][0], lhsT_scale=wb_q[i][1],
-                    rhs=hw, rhs_scale=hs, start=True, stop=True,
-                )
-            nc.scalar.copy(b_sb[:, :, c * CH : (c + 1) * CH], b_bank[:])
-            r_bank = new_bank(f"r_bank{c}", (3, 1)[c % 2])
-            for i in range(PACK):
-                nc.tensor.transpose(r_bank[:, i, :], root[:, i, :], ident[:])
-            nc.scalar.activation(damp[:, :, c * CH : (c + 1) * CH], r_bank[:], ACT.Square)
+            turn_roots(c)
+            if c + 1 < CHUNKS:
+                square_d(c + 1)
+            if c + 2 < CHUNKS:
+                multiply_d(c + 2)
+            copy_b(c)
+            square_roots(c)
+            if c + 1 < CHUNKS:
+                multiply_b(c + 1)
+                take_roots(c + 1)
+
+        def last_rows(c0):
+            cols = slice(c0 * CH, (c0 + PACK) * CH)
+            b_bank = new_bank(f"b_last{c0}", 6)[:].rearrange("p c n -> p (c n)")
+            nc.tensor.matmul_mx(
+                b_bank, lhsT=wb_q[PAGES][0], lhsT_scale=wb_q[PAGES][1],
+                rhs=h_w[:, cols].bitcast(FP8X4), rhs_scale=h_s[:, cols], start=True, stop=True,
+            )
+            nc.scalar.copy(b_sb[:, PAGES, cols], b_bank)
+            r_bank = new_bank(f"r_last{c0}", 7)
+            for c in range(PACK):
+                nc.tensor.transpose(r_bank[:, c, :], roots[c0 + c][:, PAGES, :], ident[:])
+            nc.scalar.activation(damp[:, PAGES, cols], r_bank[:].rearrange("p c n -> p (c n)"), ACT.Square)
+
+        def put(i, c0, c1):
+            page = pages[i % PAGES]
+            nc.vector.tensor_tensor(
+                page[:].indirect(bins[:, c0 * CH // 16 : c1 * CH // 16]),
+                b_sb[:, i, c0 * CH : c1 * CH], damp[:, i, c0 * CH : c1 * CH], MULT,
+            )
+            if c1 == CHUNKS:
+                nc.sync.dma_start(out.rearrange("(p i) t -> p i t", i=PACK)[:, i, :], page[:])
 
         def scatter(c):
-            for i in range(PACK):
+            for i in range(PAGES):
                 if c + 1 in SCATTER_CUTS[i]:
-                    c0 = max(cut for cut in SCATTER_CUTS[i] if cut <= c)
-                    nc.vector.tensor_tensor(
-                        pages[i][:].indirect(bins[:, c0 * CH // 16 : (c + 1) * CH // 16]),
-                        b_sb[:, i, c0 * CH : (c + 1) * CH], damp[:, i, c0 * CH : (c + 1) * CH], MULT,
-                    )
-                    if c == CHUNKS - 1:
-                        nc.sync.dma_start(out.rearrange("(p i) t -> p i t", i=PACK)[:, i, :], pages[i][:])
+                    put(i, max(cut for cut in SCATTER_CUTS[i] if cut <= c), c + 1)
 
-        for c in range(OPENED):
-            open_sum("av_bank", c, wa_q)
-            open_sum("x_bank", c, w4_q)
-        gather_words(0)
-        gather_words(1)
-        gather_words(2)
-        for c in range(OPENED):
+        for name, weights in (("av_bank", wa_q), ("x_bank", w4_q)):
+            for c in range(OPENED):
+                open_sum(name, c, weights)
+        for c0, c1 in zip(GATHER_CUTS, GATHER_CUTS[1:]):
+            gather_words(1, c0, c1, placed(f"v_w1_{c0}", [P, (c1 - c0) * CH], U32, at_wa_g1 + 4 * c0 * CH))
+        for c in range(2):
             project(c)
             first_stage(c)
-            if c in (1, 2):
-                quantise_h(c - 1)
-        pages.append(placed("page3", [P, T2], F32, at_x))
-        nc.vector.memset(pages[3][:].bitcast(I32), 0)
+        quantise_h(0)
+        wb_low = held("wb_low", [P, 2, P, PACK], BF16)
+        regroup(nc.vector.tensor_copy, wb_low[:], wb_raw, 0, 2)
+        wb_high = held("wb_high", [P, 2, P, PACK], BF16)
+        regroup(nc.scalar.copy, wb_high[:], wb_raw, 2, PACK)
+        project(2)
+        first_stage(2)
+        quantise_h(1)
+        project(3)
+        first_stage(3)
+        wb_q = quantise("wb_q0", wb_low) + quantise("wb_q1", wb_high)
+        multiply_d(0)
+        square_d(0)
+        take_roots(0)
         quantise_h(2)
-        wb_g = held("wb_g", [P, PACK, P, PACK], BF16)
-        regroup(nc.scalar.copy, wb_g[:], wb_raw)
+        pages.append(placed("page2", [P, T2], F32, at_x))
+        nc.vector.memset(pages[2][:].bitcast(I32), 0)
         project(4)
         first_stage(4)
         project(5)
+        multiply_b(0)
         first_stage(5)
-        damping(0)
-        wb_q = quantise("wb_q", wb_g)
-        quantise_h(3)
-        for c in range(6, CHUNKS):
-            project(c)
-            first_stage(c)
+        project(6)
+        multiply_d(1)
         second_stage(0)
-        second_stage(1)
+        quantise_h(3)
+        first_stage(6)
+        project(7)
+        first_stage(7)
         scatter(0)
         quantise_h(4)
         for c in range(1, CHUNKS):
-            if c + 1 < CHUNKS:
-                second_stage(c + 1)
+            second_stage(c)
             scatter(c)
+        for c0 in range(0, CHUNKS, PACK):
+            last_rows(c0)
+        put(PAGES, 0, CHUNKS)

@@ -27,8 +27,9 @@ GP = P // GROUPS
 OPENED = 4
 GATHER_CUTS = (0, 2, 4, 8)
 QUANTISE_CUTS = (0, 1, 2, 4, 6, 8)
-PAGES = PACK - 1
-SCATTER_CUTS = ((0, 1, 2, 4, 6, 8), (0, 1, 2, 4, 6, 8), (0, 1, 2, 4, 8))
+PAGES = PACK
+QUADRANTS = (0, 2, 1, 3)
+SCATTER_CUTS = ((0, 1, 2, 4, 6, 8), (0, 1, 2, 4, 6, 8), (0, 1, 2, 4, 5, 8), (0, 1, 2, 4, 5, 8))
 
 
 def tile_list_allele_mixture_scores_kernel(
@@ -50,9 +51,11 @@ def tile_list_allele_mixture_scores_kernel(
         def new_bank(name, bank):
             return psum.tile([P, PACK, CH], F32, name=name, tag=f"bank{bank}")
 
-        at_wa_g0 = 0
+        at_page2 = 0
+        at_wa_g0 = at_page2 + 4 * T2 - 64
         at_wa_g1 = at_wa_g0 + 2 * PACK * H
-        at_x = at_wa_g1 + 2 * PACK * H
+        at_w4 = at_wa_g1 + 4 * S
+        at_x = at_w4 + PASSES * 2 * H
         at_wroot = at_wa_g1 - 2 * GROUPS * CHUNKS
 
         picks = keep.tile([P, S // 16], U16, name="picks")
@@ -61,7 +64,7 @@ def tile_list_allele_mixture_scores_kernel(
         wgo_rows = held("wgo_rows", [P, CH], F32)
         w4_s_raw = held("w4_s_raw", [P, PASSES * H], U8)
         ident = held("ident", [P, P], F32)
-        pages = [held(f"page{i}", [P, T2], F32) for i in range(PAGES - 1)]
+        pages = [held(f"page{i}", [P, T2], F32) for i in range(2)]
 
         nc.gpsimd.memset(tab_s[:].bitcast(I32), 0)
         nc.gpsimd.memset(wgo_rows[:], 0.0)
@@ -71,8 +74,7 @@ def tile_list_allele_mixture_scores_kernel(
             nc.vector.memset(pages[0][:, lo:hi].bitcast(I32), 0)
         v_s = held("v_s", [P, PASSES * S], U8)
         nc.vector.memset(v_s[:].bitcast(I32), 0)
-        for page in pages[1:]:
-            nc.vector.memset(page[:].bitcast(I32), 0)
+        nc.vector.memset(pages[1][:].bitcast(I32), 0)
 
         def load_rows(tile, rows):
             nc.sync.dma_start(tile[:], rows.rearrange("(p j) c -> p j c", j=PACK))
@@ -88,7 +90,7 @@ def tile_list_allele_mixture_scores_kernel(
         load_words(tab_w0, tab_words[0])
         nc.scalar.dma_start(tab_s[0:P:4, :].bitcast(I32), tab_scales.bitcast(I32).rearrange("a q t -> q a t"))
         nc.scalar.dma_start(wgo_rows[0 : GROUPS * CHUNKS, :], wgo[0:P:GP, :])
-        for d in range(4):
+        for d in QUADRANTS:
             nc.scalar.dma_start(
                 w4_s_raw[32 * d : 32 * d + 4, :].bitcast(I32).rearrange("r (a c) -> r a c", a=PASSES),
                 w4_scales[:, 4 * d : 4 * d + 4, :].bitcast(I32).rearrange("a r c -> r a c"),
@@ -103,7 +105,7 @@ def tile_list_allele_mixture_scores_kernel(
 
         wa_raw1 = held("wa_raw1", [P, PACK, H], F32)
         load_rows(wa_raw1, wa[512:1024, :])
-        w4_raw = held("w4_raw", [P, PASSES * 2 * H], U8)
+        w4_raw = placed("w4_raw", [P, PASSES * 2 * H], U8, at_w4)
         nc.sync.dma_start(
             w4_raw[:].bitcast(I32).rearrange("p (a c) -> p a c", a=PASSES),
             w4_words.bitcast(I32).rearrange("a p c -> p a c"),
@@ -111,7 +113,7 @@ def tile_list_allele_mixture_scores_kernel(
 
         picked_s = held("picked_s", [P, S], U8)
         nc.vector.tensor_copy(picked_s[:], tab_s[:].indirect(picks[:]))
-        for d in range(4):
+        for d in QUADRANTS:
             nc.sync.dma_start(v_s[32 * d : 32 * d + 4, :].bitcast(I32), picked_s[32 * d : 32 * d + 32 : 4, :].bitcast(I32))
         tab_w1 = held("tab_w1", [P, T], U32)
         load_words(tab_w1, tab_words[1])
@@ -147,6 +149,8 @@ def tile_list_allele_mixture_scores_kernel(
         regroup(nc.scalar.copy, wa_g1[:], wa_raw1)
 
         wa_q = [quantise("wa_q0", wa_g0)]
+        pages.append(placed("page2", [P, T2], F32, at_page2))
+        nc.vector.memset(pages[2][:].bitcast(I32), 0)
         w4_w = held("w4_w", [P, PASSES * 2 * H], U8)
         w4_s = held("w4_s", [P, PASSES * H], U8)
         nc.vector.tensor_copy(
@@ -161,10 +165,10 @@ def tile_list_allele_mixture_scores_kernel(
             [(w4_w[:, 2 * col : 2 * (col + P)].bitcast(FP4X4), w4_s[:, col : col + P]) for col in range(a * H, (a + 1) * H, P)]
             for a in range(PASSES)
         ]
-        gather_words(0, OPENED, CHUNKS, placed("v_w0_high", [P, (CHUNKS - OPENED) * CH], U32, at_wa_g0))
+        gather_words(0, OPENED, CHUNKS, placed("v_w0_high", [P, (CHUNKS - OPENED) * CH], U32, at_w4))
         wa_q.append(quantise("wa_q1", wa_g1))
         w8_s = w4_s_raw
-        for d in range(4):
+        for d in QUADRANTS:
             nc.sync.dma_start(w8_s[32 * d : 32 * d + 4, 0:N].bitcast(I32), w8_scales[0, 4 * d : 4 * d + 4, :].bitcast(I32))
 
         def add_pass(bank, c, a, weights):
@@ -231,7 +235,7 @@ def tile_list_allele_mixture_scores_kernel(
             nc.scalar.activation(squares[c][:], banks["d", c].rearrange("p (m i) -> p i m", i=PACK), ACT.Square)
 
         def take_roots(c):
-            roots[c] = held(f"root{c}", [P, PACK, P], F32)
+            roots[c] = ring.tile([P, PACK, P], F32, name="root")
             for g in range(GROUPS):
                 factor = winv[:, g * CHUNKS + c : g * CHUNKS + c + 1]
                 nc.scalar.activation(
@@ -270,21 +274,8 @@ def tile_list_allele_mixture_scores_kernel(
                 multiply_b(c + 1)
                 take_roots(c + 1)
 
-        def last_rows(c0):
-            cols = slice(c0 * CH, (c0 + PACK) * CH)
-            b_bank = new_bank(f"b_last{c0}", 6)[:].rearrange("p c n -> p (c n)")
-            nc.tensor.matmul_mx(
-                b_bank, lhsT=wb_q[PAGES][0], lhsT_scale=wb_q[PAGES][1],
-                rhs=h_w[:, cols].bitcast(FP8X4), rhs_scale=h_s[:, cols], start=True, stop=True,
-            )
-            nc.scalar.copy(b_sb[:, PAGES, cols], b_bank)
-            r_bank = new_bank(f"r_last{c0}", 7)
-            for c in range(PACK):
-                nc.tensor.transpose(r_bank[:, c, :], roots[c0 + c][:, PAGES, :], ident[:])
-            nc.scalar.activation(damp[:, PAGES, cols], r_bank[:].rearrange("p c n -> p (c n)"), ACT.Square)
-
         def put(i, c0, c1):
-            page = pages[i % PAGES]
+            page = pages[i]
             nc.vector.tensor_tensor(
                 page[:].indirect(bins[:, c0 * CH // 16 : c1 * CH // 16]),
                 b_sb[:, i, c0 * CH : c1 * CH], damp[:, i, c0 * CH : c1 * CH], MULT,
@@ -320,8 +311,8 @@ def tile_list_allele_mixture_scores_kernel(
         square_d(0)
         take_roots(0)
         quantise_h(2)
-        pages.append(placed("page2", [P, T2], F32, at_x))
-        nc.vector.memset(pages[2][:].bitcast(I32), 0)
+        pages.append(placed("page3", [P, T2], F32, at_x))
+        nc.vector.memset(pages[3][:].bitcast(I32), 0)
         project(4)
         first_stage(4)
         project(5)
@@ -339,6 +330,3 @@ def tile_list_allele_mixture_scores_kernel(
         for c in range(1, CHUNKS):
             second_stage(c)
             scatter(c)
-        for c0 in range(0, CHUNKS, PACK):
-            last_rows(c0)
-        put(PAGES, 0, CHUNKS)

@@ -26,6 +26,7 @@ GROUPS = 8
 GP = P // GROUPS
 OPENED = 4
 GATHER_CUTS = (0, 2, 4, 8)
+X_BANKS = (0, 1, 2, 3, 0, 1, 0, 1)
 QUANTISE_CUTS = (0, 1, 2, 4, 6, 8)
 PAGES = PACK
 QUADRANTS = (0, 2, 1, 3)
@@ -103,8 +104,6 @@ def tile_list_allele_mixture_scores_kernel(
         nc.scalar.activation(wroot[:], w_bank[:, 0, 0 : GROUPS * CHUNKS], ACT.Abs_reciprocal_sqrt)
         nc.scalar.activation(winv[:], wroot[:], ACT.Square)
 
-        wa_raw1 = held("wa_raw1", [P, PACK, H], F32)
-        load_rows(wa_raw1, wa[512:1024, :])
         w4_raw = placed("w4_raw", [P, PASSES * 2 * H], U8, at_w4)
         nc.sync.dma_start(
             w4_raw[:].bitcast(I32).rearrange("p (a c) -> p a c", a=PASSES),
@@ -117,6 +116,8 @@ def tile_list_allele_mixture_scores_kernel(
             nc.sync.dma_start(v_s[32 * d : 32 * d + 4, :].bitcast(I32), picked_s[32 * d : 32 * d + 32 : 4, :].bitcast(I32))
         tab_w1 = held("tab_w1", [P, T], U32)
         load_words(tab_w1, tab_words[1])
+        wa_raw1 = held("wa_raw1", [P, PACK, H], F32)
+        load_rows(wa_raw1, wa[512:1024, :])
         wb_raw = held("wb_raw", [P, PACK, N], F32)
         load_rows(wb_raw, wb)
         w8_w = held("w8_w", [P, N], U32)
@@ -145,8 +146,6 @@ def tile_list_allele_mixture_scores_kernel(
             nc.vector.quantize_mx(codes[:].bitcast(FP8X4), scales[:], grouped[:].rearrange("p t m j -> p (t m j)"))
             return [(codes[:, t * P : (t + 1) * P].bitcast(FP8X4), scales[:, t * P : (t + 1) * P]) for t in range(slices)]
 
-        wa_g1 = placed("wa_g1", [P, PACK, P, PACK], BF16, at_wa_g1)
-        regroup(nc.scalar.copy, wa_g1[:], wa_raw1)
 
         wa_q = [quantise("wa_q0", wa_g0)]
         pages.append(placed("page2", [P, T2], F32, at_page2))
@@ -166,7 +165,6 @@ def tile_list_allele_mixture_scores_kernel(
             for a in range(PASSES)
         ]
         gather_words(0, OPENED, CHUNKS, placed("v_w0_high", [P, (CHUNKS - OPENED) * CH], U32, at_w4))
-        wa_q.append(quantise("wa_q1", wa_g1))
         w8_s = w4_s_raw
         for d in QUADRANTS:
             nc.sync.dma_start(w8_s[32 * d : 32 * d + 4, 0:N].bitcast(I32), w8_scales[0, 4 * d : 4 * d + 4, :].bitcast(I32))
@@ -189,7 +187,7 @@ def tile_list_allele_mixture_scores_kernel(
         x_sb = {}
 
         def open_sum(name, c, weights):
-            banks[name, c] = new_bank(f"{name}{c}", OPENED + c % OPENED if name == "av_bank" else c if c < OPENED else c % 2)
+            banks[name, c] = new_bank(f"{name}{c}", OPENED + c % OPENED if name == "av_bank" else X_BANKS[c])
             add_pass(banks[name, c], c, 0, weights)
 
         def project(c):
@@ -225,7 +223,7 @@ def tile_list_allele_mixture_scores_kernel(
 
         def multiply_d(c):
             hw, hs = h_of(c)
-            banks["d", c] = new_bank(f"d_bank{c}", (2, 0)[c % 2])[:].rearrange("p i m -> p (i m)")
+            banks["d", c] = new_bank(f"d_bank{c}", (2, 4)[c % 2])[:].rearrange("p i m -> p (i m)")
             nc.tensor.matmul_mx(
                 banks["d", c], lhsT=hw, lhsT_scale=hs, rhs=w8_w[:].bitcast(FP8X4), rhs_scale=w8_s[:, 0:N], start=True, stop=True
             )
@@ -245,7 +243,7 @@ def tile_list_allele_mixture_scores_kernel(
 
         def multiply_b(c):
             hw, hs = h_of(c)
-            banks["b", c] = new_bank(f"b_bank{c}", 4 + c % 2)
+            banks["b", c] = new_bank(f"b_bank{c}", c % 2)
             for i in range(PAGES):
                 nc.tensor.matmul_mx(
                     banks["b", c][:, i, :], lhsT=wb_q[i][0], lhsT_scale=wb_q[i][1], rhs=hw, rhs_scale=hs, start=True, stop=True
@@ -255,7 +253,7 @@ def tile_list_allele_mixture_scores_kernel(
             nc.scalar.copy(b_sb[:, 0:PAGES, c * CH : (c + 1) * CH], banks["b", c][:, 0:PAGES, :])
 
         def turn_roots(c):
-            banks["r", c] = new_bank(f"r_bank{c}", (3, 1)[c % 2])
+            banks["r", c] = new_bank(f"r_bank{c}", (3, 5)[c % 2])
             for i in range(PAGES):
                 nc.tensor.transpose(banks["r", c][:, i, :], roots[c][:, i, :], ident[:])
 
@@ -288,43 +286,57 @@ def tile_list_allele_mixture_scores_kernel(
                 if c + 1 in SCATTER_CUTS[i]:
                     put(i, max(cut for cut in SCATTER_CUTS[i] if cut <= c), c + 1)
 
-        for name, weights in (("av_bank", wa_q), ("x_bank", w4_q)):
-            for c in range(OPENED):
-                open_sum(name, c, weights)
+        for c in range(OPENED):
+            open_sum("x_bank", c, w4_q)
+        for c in range(2):
+            open_sum("av_bank", c, wa_q)
         for c0, c1 in zip(GATHER_CUTS, GATHER_CUTS[1:]):
-            gather_words(1, c0, c1, placed(f"v_w1_{c0}", [P, (c1 - c0) * CH], U32, at_wa_g1 + 4 * c0 * CH))
+            gather_words(1, c0, c1, held(f"v_w1_{c0}", [P, (c1 - c0) * CH], U32))
         for c in range(2):
             project(c)
-            first_stage(c)
+        wa_low = held("wa_low", [P, 2, P, PACK], BF16)
+        regroup(nc.vector.tensor_copy, wa_low[:], wa_raw1, 0, 2)
+        wa_high = placed("wa_high", [P, 2, P, PACK], BF16, at_wa_g1)
+        regroup(nc.scalar.copy, wa_high[:], wa_raw1, 2, PACK)
+        wa_q.append(quantise("wa_q1a", wa_low) + quantise("wa_q1b", wa_high))
+        for c in range(2, OPENED):
+            project(c)
+            open_sum("av_bank", c, wa_q)
+        first_stage(0)
+        project(4)
+        first_stage(1)
         quantise_h(0)
-        wb_low = held("wb_low", [P, 2, P, PACK], BF16)
-        regroup(nc.vector.tensor_copy, wb_low[:], wb_raw, 0, 2)
+        project(5)
         wb_high = held("wb_high", [P, 2, P, PACK], BF16)
         regroup(nc.scalar.copy, wb_high[:], wb_raw, 2, PACK)
-        project(2)
         first_stage(2)
         quantise_h(1)
-        project(3)
         first_stage(3)
-        wb_q = quantise("wb_q0", wb_low) + quantise("wb_q1", wb_high)
-        multiply_d(0)
-        square_d(0)
-        take_roots(0)
-        quantise_h(2)
+        wb_low = held("wb_low", [P, 2, P, PACK], BF16)
+        regroup(nc.vector.tensor_copy, wb_low[:], wb_raw, 0, 2)
+        project(6)
         pages.append(placed("page3", [P, T2], F32, at_x))
         nc.vector.memset(pages[3][:].bitcast(I32), 0)
-        project(4)
+        quantise_h(2)
+        multiply_d(0)
+        square_d(0)
         first_stage(4)
-        project(5)
-        multiply_b(0)
+        wb_q = quantise("wb_q0", wb_low) + quantise("wb_q1", wb_high)
+        project(7)
+        take_roots(0)
         first_stage(5)
-        project(6)
+        multiply_b(0)
+        turn_roots(0)
         multiply_d(1)
-        second_stage(0)
         quantise_h(3)
         first_stage(6)
-        project(7)
+        copy_b(0)
+        square_roots(0)
+        square_d(1)
         first_stage(7)
+        take_roots(1)
+        multiply_b(1)
+        multiply_d(2)
         scatter(0)
         quantise_h(4)
         for c in range(1, CHUNKS):

@@ -25,10 +25,11 @@ CHUNKS = S // CH
 GROUPS = 8
 GP = P // GROUPS
 OPENED = 4
+WEIGHED = 3
+FACTORS = GROUPS * (CHUNKS - WEIGHED)
 GATHER_CUTS = (0, 2, 4, 8)
 X_BANKS = (0, 1, 2, 3, 0, 1, 0, 1)
 QUANTISE_CUTS = (0, 1, 2, 4, 6, 8)
-PAGES = PACK
 QUADRANTS = (0, 2, 1, 3)
 SCATTER_CUTS = ((0, 1, 2, 4, 6, 8), (0, 1, 2, 4, 6, 8), (0, 1, 2, 4, 5, 8), (0, 1, 2, 4, 5, 8))
 
@@ -57,7 +58,7 @@ def tile_list_allele_mixture_scores_kernel(
         at_wa_g1 = at_wa_g0 + 2 * PACK * H
         at_w4 = at_wa_g1 + 4 * S
         at_x = at_w4 + PASSES * 2 * H
-        at_wroot = at_wa_g1 - 2 * GROUPS * CHUNKS
+        at_wroot = at_wa_g1 - 64
 
         picks = keep.tile([P, S // 16], U16, name="picks")
         bins = keep.tile([P, S // 16], U16, name="bins")
@@ -90,18 +91,18 @@ def tile_list_allele_mixture_scores_kernel(
         tab_w0 = held("tab_w0", [P, T], U32)
         load_words(tab_w0, tab_words[0])
         nc.scalar.dma_start(tab_s[0:P:4, :].bitcast(I32), tab_scales.bitcast(I32).rearrange("a q t -> q a t"))
-        nc.scalar.dma_start(wgo_rows[0 : GROUPS * CHUNKS, :], wgo[0:P:GP, :])
+        nc.scalar.dma_start(wgo_rows[0:FACTORS, :], wgo[0:P:GP, WEIGHED * CH : S])
         for d in QUADRANTS:
             nc.scalar.dma_start(
                 w4_s_raw[32 * d : 32 * d + 4, :].bitcast(I32).rearrange("r (a c) -> r a c", a=PASSES),
                 w4_scales[:, 4 * d : 4 * d + 4, :].bitcast(I32).rearrange("a r c -> r a c"),
             )
 
-        winv = held("winv", [P, GROUPS * CHUNKS], F32)
+        winv = held("winv", [P, FACTORS], F32)
         w_bank = new_bank("w_bank", 7)
         nc.tensor.transpose(w_bank[:, 0, :], wgo_rows[:], ident[:])
-        wroot = placed("wroot", [P, GROUPS * CHUNKS], F32, at_wroot)
-        nc.scalar.activation(wroot[:], w_bank[:, 0, 0 : GROUPS * CHUNKS], ACT.Abs_reciprocal_sqrt)
+        wroot = placed("wroot", [P, FACTORS], F32, at_wroot)
+        nc.scalar.activation(wroot[:], w_bank[:, 0, 0:FACTORS], ACT.Abs_reciprocal_sqrt)
         nc.scalar.activation(winv[:], wroot[:], ACT.Square)
 
         w4_raw = placed("w4_raw", [P, PASSES * 2 * H], U8, at_w4)
@@ -122,6 +123,8 @@ def tile_list_allele_mixture_scores_kernel(
         load_rows(wb_raw, wb)
         w8_w = held("w8_w", [P, N], U32)
         load_words(w8_w, w8_words[0])
+        wgo_cols = held("wgo_cols", [P, WEIGHED * CH], F32)
+        nc.sync.dma_start(wgo_cols[:], wgo[:, 0 : WEIGHED * CH])
 
 
         def regroup(copy, grouped, raw, t0=0, t1=PACK):
@@ -234,8 +237,12 @@ def tile_list_allele_mixture_scores_kernel(
 
         def take_roots(c):
             roots[c] = ring.tile([P, PACK, P], F32, name="root")
+            if c < WEIGHED:
+                nc.scalar.activation(roots[c][:], squares[c][:], ACT.Abs_reciprocal_sqrt, bias=1.0)
+                return
             for g in range(GROUPS):
-                factor = winv[:, g * CHUNKS + c : g * CHUNKS + c + 1]
+                at = g * (CHUNKS - WEIGHED) + c - WEIGHED
+                factor = winv[:, at : at + 1]
                 nc.scalar.activation(
                     roots[c][:, :, g * GP : (g + 1) * GP], squares[c][:, :, g * GP : (g + 1) * GP], ACT.Abs_reciprocal_sqrt,
                     bias=factor, scale=factor,
@@ -243,22 +250,27 @@ def tile_list_allele_mixture_scores_kernel(
 
         def multiply_b(c):
             hw, hs = h_of(c)
-            banks["b", c] = new_bank(f"b_bank{c}", c % 2)
-            for i in range(PAGES):
+            banks["b", c] = new_bank(f"b_bank{c}", (0, 1, 6)[c] if c < WEIGHED else c % 2)
+            for i in range(PACK):
                 nc.tensor.matmul_mx(
                     banks["b", c][:, i, :], lhsT=wb_q[i][0], lhsT_scale=wb_q[i][1], rhs=hw, rhs_scale=hs, start=True, stop=True
                 )
 
         def copy_b(c):
-            nc.scalar.copy(b_sb[:, 0:PAGES, c * CH : (c + 1) * CH], banks["b", c][:, 0:PAGES, :])
+            cols = slice(c * CH, (c + 1) * CH)
+            if c < WEIGHED:
+                factors = wgo_cols[:, cols].unsqueeze(1).to_broadcast([P, PACK, CH])
+                nc.vector.tensor_tensor(b_sb[:, :, cols], banks["b", c][:], factors, MULT)
+            else:
+                nc.scalar.copy(b_sb[:, :, cols], banks["b", c][:])
 
         def turn_roots(c):
             banks["r", c] = new_bank(f"r_bank{c}", (3, 5)[c % 2])
-            for i in range(PAGES):
+            for i in range(PACK):
                 nc.tensor.transpose(banks["r", c][:, i, :], roots[c][:, i, :], ident[:])
 
         def square_roots(c):
-            nc.scalar.activation(damp[:, 0:PAGES, c * CH : (c + 1) * CH], banks["r", c][:, 0:PAGES, :], ACT.Square)
+            nc.scalar.activation(damp[:, :, c * CH : (c + 1) * CH], banks["r", c][:], ACT.Square)
 
         def second_stage(c):
             turn_roots(c)
@@ -266,10 +278,12 @@ def tile_list_allele_mixture_scores_kernel(
                 square_d(c + 1)
             if c + 2 < CHUNKS:
                 multiply_d(c + 2)
-            copy_b(c)
+            if c >= WEIGHED:
+                copy_b(c)
             square_roots(c)
-            if c + 1 < CHUNKS:
+            if WEIGHED <= c + 1 < CHUNKS:
                 multiply_b(c + 1)
+            if c + 1 < CHUNKS:
                 take_roots(c + 1)
 
         def put(i, c0, c1):
@@ -282,7 +296,7 @@ def tile_list_allele_mixture_scores_kernel(
                 nc.sync.dma_start(out.rearrange("(p i) t -> p i t", i=PACK)[:, i, :], page[:])
 
         def scatter(c):
-            for i in range(PAGES):
+            for i in range(PACK):
                 if c + 1 in SCATTER_CUTS[i]:
                     put(i, max(cut for cut in SCATTER_CUTS[i] if cut <= c), c + 1)
 
@@ -325,20 +339,24 @@ def tile_list_allele_mixture_scores_kernel(
         project(7)
         take_roots(0)
         first_stage(5)
-        multiply_b(0)
         turn_roots(0)
+        multiply_b(0)
         multiply_d(1)
         quantise_h(3)
         first_stage(6)
         copy_b(0)
         square_roots(0)
         square_d(1)
+        multiply_b(1)
         first_stage(7)
         take_roots(1)
-        multiply_b(1)
-        multiply_d(2)
-        scatter(0)
+        copy_b(1)
         quantise_h(4)
+        multiply_d(2)
+        for c in range(2, WEIGHED):
+            multiply_b(c)
+            copy_b(c)
+        scatter(0)
         for c in range(1, CHUNKS):
             second_stage(c)
             scatter(c)

@@ -27,6 +27,7 @@ GP = P // GROUPS
 OPENED = 4
 WEIGHED = 3
 FACTORS = GROUPS * (CHUNKS - WEIGHED)
+SHARED = 1152
 GATHER_CUTS = (0, 2, 4, 8)
 X_BANKS = (0, 1, 2, 3, 0, 1, 0, 1)
 QUANTISE_CUTS = (0, 1, 2, 4, 6, 8)
@@ -53,11 +54,9 @@ def tile_list_allele_mixture_scores_kernel(
         def new_bank(name, bank):
             return psum.tile([P, PACK, CH], F32, name=name, tag=f"bank{bank}")
 
-        at_page2 = 0
-        at_wa_g0 = at_page2 + 4 * T2 - 64
+        at_wa_g0 = 0
         at_wa_g1 = at_wa_g0 + 2 * PACK * H
         at_w4 = at_wa_g1 + 4 * S
-        at_x = at_w4 + PASSES * 2 * H
         at_wroot = at_wa_g1 - 64
 
         picks = keep.tile([P, S // 16], U16, name="picks")
@@ -66,17 +65,19 @@ def tile_list_allele_mixture_scores_kernel(
         wgo_rows = held("wgo_rows", [P, CH], F32)
         w4_s_raw = held("w4_s_raw", [P, PASSES * H], U8)
         ident = held("ident", [P, P], F32)
-        pages = [held(f"page{i}", [P, T2], F32) for i in range(2)]
+        pages = [held(f"page{i}", [P, T2], F32) for i in range(PACK)]
 
         nc.gpsimd.memset(tab_s[:].bitcast(I32), 0)
         nc.gpsimd.memset(wgo_rows[:], 0.0)
         nc.gpsimd.memset(w4_s_raw[:].bitcast(I32), 0)
         make_identity(nc, ident[:])
-        for lo, hi in ((0, T2 // 2 + 1), (T2 // 2 + 1, T2 // 2 + 2), (T2 // 2 + 2, T2)):
-            nc.vector.memset(pages[0][:, lo:hi].bitcast(I32), 0)
         v_s = held("v_s", [P, PASSES * S], U8)
-        nc.vector.memset(v_s[:].bitcast(I32), 0)
-        nc.vector.memset(pages[1][:].bitcast(I32), 0)
+        nc.gpsimd.memset(v_s[:].bitcast(I32), 0)
+        nc.gpsimd.memset(pages[1][:].bitcast(I32), 0)
+        nc.gpsimd.memset(pages[2][:, SHARED:T2].bitcast(I32), 0)
+        for page, width in ((pages[0], T2), (pages[3], T2), (pages[2], SHARED)):
+            for lo, hi in ((0, width // 2 + 1), (width // 2 + 1, width)):
+                nc.vector.memset(page[:, lo:hi].bitcast(I32), 0)
 
         def load_rows(tile, rows):
             nc.sync.dma_start(tile[:], rows.rearrange("(p j) c -> p j c", j=PACK))
@@ -111,12 +112,12 @@ def tile_list_allele_mixture_scores_kernel(
             w4_words.bitcast(I32).rearrange("a p c -> p a c"),
         )
 
+        tab_w1 = held("tab_w1", [P, T], U32)
+        load_words(tab_w1, tab_words[1])
         picked_s = held("picked_s", [P, S], U8)
         nc.vector.tensor_copy(picked_s[:], tab_s[:].indirect(picks[:]))
         for d in QUADRANTS:
             nc.sync.dma_start(v_s[32 * d : 32 * d + 4, :].bitcast(I32), picked_s[32 * d : 32 * d + 32 : 4, :].bitcast(I32))
-        tab_w1 = held("tab_w1", [P, T], U32)
-        load_words(tab_w1, tab_words[1])
         wa_raw1 = held("wa_raw1", [P, PACK, H], F32)
         load_rows(wa_raw1, wa[512:1024, :])
         wb_raw = held("wb_raw", [P, PACK, N], F32)
@@ -151,8 +152,6 @@ def tile_list_allele_mixture_scores_kernel(
 
 
         wa_q = [quantise("wa_q0", wa_g0)]
-        pages.append(placed("page2", [P, T2], F32, at_page2))
-        nc.vector.memset(pages[2][:].bitcast(I32), 0)
         w4_w = held("w4_w", [P, PASSES * 2 * H], U8)
         w4_s = held("w4_s", [P, PASSES * H], U8)
         nc.vector.tensor_copy(
@@ -197,7 +196,7 @@ def tile_list_allele_mixture_scores_kernel(
             if ("x_bank", c) not in banks:
                 open_sum("x_bank", c, w4_q)
             add_pass(banks["x_bank", c], c, 1, w4_q)
-            x_sb[c] = placed(f"x{c}", [P, CH, PACK], F32, at_x + 4 * CH * PACK * c)
+            x_sb[c] = held(f"x{c}", [P, CH, PACK], F32)
             nc.scalar.copy(x_sb[c][:], banks["x_bank", c][:].rearrange("p t n -> p n t"))
 
         def first_stage(c):
@@ -329,8 +328,6 @@ def tile_list_allele_mixture_scores_kernel(
         wb_low = held("wb_low", [P, 2, P, PACK], BF16)
         regroup(nc.vector.tensor_copy, wb_low[:], wb_raw, 0, 2)
         project(6)
-        pages.append(placed("page3", [P, T2], F32, at_x))
-        nc.vector.memset(pages[3][:].bitcast(I32), 0)
         quantise_h(2)
         multiply_d(0)
         square_d(0)

@@ -25,14 +25,12 @@ CHUNKS = S // CH
 GROUPS = 8
 GP = P // GROUPS
 OPENED = 4
-WEIGHED = 3
-FACTORS = GROUPS * (CHUNKS - WEIGHED)
-SHARED = 1152
+FACTORS = GROUPS * CHUNKS
 GATHER_CUTS = (0, 2, 4, 8)
 X_BANKS = (0, 1, 2, 3, 0, 1, 0, 1)
 QUANTISE_CUTS = (0, 1, 2, 4, 6, 8)
 QUADRANTS = (0, 2, 1, 3)
-SCATTER_CUTS = ((0, 1, 2, 4, 6, 8), (0, 1, 2, 4, 6, 8), (0, 1, 2, 4, 5, 8), (0, 1, 2, 4, 5, 8))
+LAST_FROM = (6, 6, 5, 5)
 
 
 def tile_list_allele_mixture_scores_kernel(
@@ -54,9 +52,11 @@ def tile_list_allele_mixture_scores_kernel(
         def new_bank(name, bank):
             return psum.tile([P, PACK, CH], F32, name=name, tag=f"bank{bank}")
 
-        at_wa_g0 = 0
+        at_page2 = 0
+        at_wa_g0 = at_page2 + 4 * T2 - 64
         at_wa_g1 = at_wa_g0 + 2 * PACK * H
         at_w4 = at_wa_g1 + 4 * S
+        at_x = at_w4 + PASSES * 2 * H
         at_wroot = at_wa_g1 - 64
 
         picks = keep.tile([P, S // 16], U16, name="picks")
@@ -65,19 +65,17 @@ def tile_list_allele_mixture_scores_kernel(
         wgo_rows = held("wgo_rows", [P, CH], F32)
         w4_s_raw = held("w4_s_raw", [P, PASSES * H], U8)
         ident = held("ident", [P, P], F32)
-        pages = [held(f"page{i}", [P, T2], F32) for i in range(PACK)]
+        pages = [held(f"page{i}", [P, T2], F32) for i in range(2)]
 
         nc.gpsimd.memset(tab_s[:].bitcast(I32), 0)
         nc.gpsimd.memset(wgo_rows[:], 0.0)
         nc.gpsimd.memset(w4_s_raw[:].bitcast(I32), 0)
         make_identity(nc, ident[:])
+        for lo, hi in ((0, T2 // 2 + 1), (T2 // 2 + 1, T2 // 2 + 2), (T2 // 2 + 2, T2)):
+            nc.vector.memset(pages[0][:, lo:hi].bitcast(I32), 0)
         v_s = held("v_s", [P, PASSES * S], U8)
-        nc.gpsimd.memset(v_s[:].bitcast(I32), 0)
-        nc.gpsimd.memset(pages[1][:].bitcast(I32), 0)
-        nc.gpsimd.memset(pages[2][:, SHARED:T2].bitcast(I32), 0)
-        for page, width in ((pages[0], T2), (pages[3], T2), (pages[2], SHARED)):
-            for lo, hi in ((0, width // 2 + 1), (width // 2 + 1, width)):
-                nc.vector.memset(page[:, lo:hi].bitcast(I32), 0)
+        nc.vector.memset(v_s[:].bitcast(I32), 0)
+        nc.vector.memset(pages[1][:].bitcast(I32), 0)
 
         def load_rows(tile, rows):
             nc.sync.dma_start(tile[:], rows.rearrange("(p j) c -> p j c", j=PACK))
@@ -92,7 +90,7 @@ def tile_list_allele_mixture_scores_kernel(
         tab_w0 = held("tab_w0", [P, T], U32)
         load_words(tab_w0, tab_words[0])
         nc.scalar.dma_start(tab_s[0:P:4, :].bitcast(I32), tab_scales.bitcast(I32).rearrange("a q t -> q a t"))
-        nc.scalar.dma_start(wgo_rows[0:FACTORS, :], wgo[0:P:GP, WEIGHED * CH : S])
+        nc.scalar.dma_start(wgo_rows[0:FACTORS, :], wgo[0:P:GP, :])
         for d in QUADRANTS:
             nc.scalar.dma_start(
                 w4_s_raw[32 * d : 32 * d + 4, :].bitcast(I32).rearrange("r (a c) -> r a c", a=PASSES),
@@ -124,8 +122,6 @@ def tile_list_allele_mixture_scores_kernel(
         load_rows(wb_raw, wb)
         w8_w = held("w8_w", [P, N], U32)
         load_words(w8_w, w8_words[0])
-        wgo_cols = held("wgo_cols", [P, WEIGHED * CH], F32)
-        nc.sync.dma_start(wgo_cols[:], wgo[:, 0 : WEIGHED * CH])
 
 
         def regroup(copy, grouped, raw, t0=0, t1=PACK):
@@ -152,6 +148,8 @@ def tile_list_allele_mixture_scores_kernel(
 
 
         wa_q = [quantise("wa_q0", wa_g0)]
+        pages.append(placed("page2", [P, T2], F32, at_page2))
+        nc.vector.memset(pages[2][:].bitcast(I32), 0)
         w4_w = held("w4_w", [P, PASSES * 2 * H], U8)
         w4_s = held("w4_s", [P, PASSES * H], U8)
         nc.vector.tensor_copy(
@@ -196,7 +194,7 @@ def tile_list_allele_mixture_scores_kernel(
             if ("x_bank", c) not in banks:
                 open_sum("x_bank", c, w4_q)
             add_pass(banks["x_bank", c], c, 1, w4_q)
-            x_sb[c] = held(f"x{c}", [P, CH, PACK], F32)
+            x_sb[c] = placed(f"x{c}", [P, CH, PACK], F32, at_x + 4 * CH * PACK * c)
             nc.scalar.copy(x_sb[c][:], banks["x_bank", c][:].rearrange("p t n -> p n t"))
 
         def first_stage(c):
@@ -235,41 +233,37 @@ def tile_list_allele_mixture_scores_kernel(
             nc.scalar.activation(squares[c][:], banks["d", c].rearrange("p (m i) -> p i m", i=PACK), ACT.Square)
 
         def take_roots(c):
-            roots[c] = ring.tile([P, PACK, P], F32, name="root")
-            if c < WEIGHED:
-                nc.scalar.activation(roots[c][:], squares[c][:], ACT.Abs_reciprocal_sqrt, bias=1.0)
-                return
+            roots[c] = held(f"root{c}", [P, PACK, P], F32)
             for g in range(GROUPS):
-                at = g * (CHUNKS - WEIGHED) + c - WEIGHED
-                factor = winv[:, at : at + 1]
+                factor = winv[:, g * CHUNKS + c : g * CHUNKS + c + 1]
                 nc.scalar.activation(
                     roots[c][:, :, g * GP : (g + 1) * GP], squares[c][:, :, g * GP : (g + 1) * GP], ACT.Abs_reciprocal_sqrt,
                     bias=factor, scale=factor,
                 )
 
+        def prompt_rows(c):
+            return 1 + sum(c < LAST_FROM[i] for i in range(1, PACK))
+
         def multiply_b(c):
             hw, hs = h_of(c)
-            banks["b", c] = new_bank(f"b_bank{c}", (0, 1, 6)[c] if c < WEIGHED else c % 2)
-            for i in range(PACK):
+            banks["b", c] = new_bank(f"b_bank{c}", c % 2)
+            for i in range(prompt_rows(c)):
                 nc.tensor.matmul_mx(
                     banks["b", c][:, i, :], lhsT=wb_q[i][0], lhsT_scale=wb_q[i][1], rhs=hw, rhs_scale=hs, start=True, stop=True
                 )
 
         def copy_b(c):
-            cols = slice(c * CH, (c + 1) * CH)
-            if c < WEIGHED:
-                factors = wgo_cols[:, cols].unsqueeze(1).to_broadcast([P, PACK, CH])
-                nc.vector.tensor_tensor(b_sb[:, :, cols], banks["b", c][:], factors, MULT)
-            else:
-                nc.scalar.copy(b_sb[:, :, cols], banks["b", c][:])
+            rows = prompt_rows(c)
+            nc.scalar.copy(b_sb[:, 0:rows, c * CH : (c + 1) * CH], banks["b", c][:, 0:rows, :])
 
         def turn_roots(c):
             banks["r", c] = new_bank(f"r_bank{c}", (3, 5)[c % 2])
-            for i in range(PACK):
+            for i in range(prompt_rows(c)):
                 nc.tensor.transpose(banks["r", c][:, i, :], roots[c][:, i, :], ident[:])
 
         def square_roots(c):
-            nc.scalar.activation(damp[:, :, c * CH : (c + 1) * CH], banks["r", c][:], ACT.Square)
+            rows = prompt_rows(c)
+            nc.scalar.activation(damp[:, 0:rows, c * CH : (c + 1) * CH], banks["r", c][:, 0:rows, :], ACT.Square)
 
         def second_stage(c):
             turn_roots(c)
@@ -277,27 +271,37 @@ def tile_list_allele_mixture_scores_kernel(
                 square_d(c + 1)
             if c + 2 < CHUNKS:
                 multiply_d(c + 2)
-            if c >= WEIGHED:
-                copy_b(c)
+            copy_b(c)
             square_roots(c)
-            if WEIGHED <= c + 1 < CHUNKS:
-                multiply_b(c + 1)
             if c + 1 < CHUNKS:
+                multiply_b(c + 1)
                 take_roots(c + 1)
 
+        def late_rows(i):
+            c0 = LAST_FROM[i]
+            cols, count = slice(c0 * CH, S), CHUNKS - c0
+            b_bank = new_bank(f"b_late{i}", (6, 7, 2)[i - 1])
+            for c in range(c0, CHUNKS):
+                hw, hs = h_of(c)
+                nc.tensor.matmul_mx(
+                    b_bank[:, c - c0, :], lhsT=wb_q[i][0], lhsT_scale=wb_q[i][1], rhs=hw, rhs_scale=hs, start=True, stop=True
+                )
+            nc.scalar.copy(b_sb[:, i, cols], b_bank[:, 0:count, :].rearrange("p c n -> p (c n)"))
+            r_bank = new_bank(f"r_late{i}", (4, 3, 0)[i - 1])
+            for c in range(c0, CHUNKS):
+                nc.tensor.transpose(r_bank[:, c - c0, :], roots[c][:, i, :], ident[:])
+            nc.scalar.activation(damp[:, i, cols], r_bank[:, 0:count, :].rearrange("p c n -> p (c n)"), ACT.Square)
+
         def put(i, c0, c1):
-            page = pages[i]
             nc.vector.tensor_tensor(
-                page[:].indirect(bins[:, c0 * CH // 16 : c1 * CH // 16]),
+                pages[i][:].indirect(bins[:, c0 * CH // 16 : c1 * CH // 16]),
                 b_sb[:, i, c0 * CH : c1 * CH], damp[:, i, c0 * CH : c1 * CH], MULT,
             )
-            if c1 == CHUNKS:
-                nc.sync.dma_start(out.rearrange("(p i) t -> p i t", i=PACK)[:, i, :], page[:])
 
         def scatter(c):
             for i in range(PACK):
-                if c + 1 in SCATTER_CUTS[i]:
-                    put(i, max(cut for cut in SCATTER_CUTS[i] if cut <= c), c + 1)
+                if c < LAST_FROM[i]:
+                    put(i, c, c + 1)
 
         for c in range(OPENED):
             open_sum("x_bank", c, w4_q)
@@ -328,6 +332,8 @@ def tile_list_allele_mixture_scores_kernel(
         wb_low = held("wb_low", [P, 2, P, PACK], BF16)
         regroup(nc.vector.tensor_copy, wb_low[:], wb_raw, 0, 2)
         project(6)
+        pages.append(placed("page3", [P, T2], F32, at_x))
+        nc.vector.memset(pages[3][:].bitcast(I32), 0)
         quantise_h(2)
         multiply_d(0)
         square_d(0)
@@ -336,24 +342,25 @@ def tile_list_allele_mixture_scores_kernel(
         project(7)
         take_roots(0)
         first_stage(5)
-        turn_roots(0)
         multiply_b(0)
+        turn_roots(0)
         multiply_d(1)
         quantise_h(3)
         first_stage(6)
         copy_b(0)
         square_roots(0)
         square_d(1)
-        multiply_b(1)
         first_stage(7)
         take_roots(1)
-        copy_b(1)
-        quantise_h(4)
+        multiply_b(1)
         multiply_d(2)
-        for c in range(2, WEIGHED):
-            multiply_b(c)
-            copy_b(c)
         scatter(0)
+        quantise_h(4)
         for c in range(1, CHUNKS):
             second_stage(c)
             scatter(c)
+        for i in range(PACK):
+            if i > 0:
+                late_rows(i)
+            put(i, LAST_FROM[i], CHUNKS)
+            nc.sync.dma_start(out.rearrange("(p i) t -> p i t", i=PACK)[:, i, :], pages[i][:])

@@ -57,11 +57,12 @@ def tile_list_allele_mixture_scores_kernel(
         at_wa_g1 = at_wa_g0 + 2 * PACK * H
         at_w4 = at_wa_g1 + 4 * S
         at_x = at_w4 + PASSES * 2 * H
+        at_tab_s = at_x + 4 * PACK * S
         at_wroot = at_wa_g1 - 64
 
         picks = keep.tile([P, S // 16], U16, name="picks")
         bins = keep.tile([P, S // 16], U16, name="bins")
-        tab_s = held("tab_s", [P, T], U8)
+        tab_s = placed("tab_s", [P, T], U8, at_tab_s)
         wgo_rows = held("wgo_rows", [P, CH], F32)
         w4_s_raw = held("w4_s_raw", [P, PASSES * H], U8)
         ident = held("ident", [P, P], F32)
@@ -73,8 +74,6 @@ def tile_list_allele_mixture_scores_kernel(
         make_identity(nc, ident[:])
         for lo, hi in ((0, T2 // 2 + 1), (T2 // 2 + 1, T2 // 2 + 2), (T2 // 2 + 2, T2)):
             nc.vector.memset(pages[0][:, lo:hi].bitcast(I32), 0)
-        v_s = held("v_s", [P, PASSES * S], U8)
-        nc.vector.memset(v_s[:].bitcast(I32), 0)
         nc.vector.memset(pages[1][:].bitcast(I32), 0)
 
         def load_rows(tile, rows):
@@ -114,6 +113,7 @@ def tile_list_allele_mixture_scores_kernel(
         load_words(tab_w1, tab_words[1])
         picked_s = held("picked_s", [P, S], U8)
         nc.vector.tensor_copy(picked_s[:], tab_s[:].indirect(picks[:]))
+        v_s = placed("v_s", [P, PASSES * S], U8, at_tab_s)
         for d in QUADRANTS:
             nc.sync.dma_start(v_s[32 * d : 32 * d + 4, :].bitcast(I32), picked_s[32 * d : 32 * d + 32 : 4, :].bitcast(I32))
         wa_raw1 = held("wa_raw1", [P, PACK, H], F32)
@@ -324,13 +324,12 @@ def tile_list_allele_mixture_scores_kernel(
         first_stage(1)
         quantise_h(0)
         project(5)
-        wb_high = held("wb_high", [P, 2, P, PACK], BF16)
-        regroup(nc.scalar.copy, wb_high[:], wb_raw, 2, PACK)
+        wb_g = held("wb_g", [P, PACK, P, PACK], BF16)
+        regroup(nc.vector.tensor_copy, wb_g[:], wb_raw)
         first_stage(2)
+        wb_q = quantise("wb_q", wb_g)
         quantise_h(1)
         first_stage(3)
-        wb_low = held("wb_low", [P, 2, P, PACK], BF16)
-        regroup(nc.vector.tensor_copy, wb_low[:], wb_raw, 0, 2)
         project(6)
         pages.append(placed("page3", [P, T2], F32, at_x))
         nc.vector.memset(pages[3][:].bitcast(I32), 0)
@@ -338,7 +337,6 @@ def tile_list_allele_mixture_scores_kernel(
         multiply_d(0)
         square_d(0)
         first_stage(4)
-        wb_q = quantise("wb_q0", wb_low) + quantise("wb_q1", wb_high)
         project(7)
         take_roots(0)
         first_stage(5)

@@ -26,11 +26,13 @@ GROUPS = 8
 GP = P // GROUPS
 OPENED = 4
 FACTORS = GROUPS * CHUNKS
-GATHER_CUTS = (0, 2, 4, 8)
-X_BANKS = (0, 1, 2, 3, 0, 1, 0, 1)
+GATHER_CUTS = ((0, 4, 8), (0, 2, 4, 6, 8))
+SPARE = 64
 QUANTISE_CUTS = (0, 1, 2, 4, 6, 8)
 QUADRANTS = (0, 2, 1, 3)
-LAST_FROM = (6, 6, 5, 5)
+LAST_FROM = (7, 6, 5, 5)
+X_BANKS = (0, 1, 2, 3, 0, 1, 1, 1)
+B_BANK, D_BANK, R_BANK, W_BANK = 0, 2, 3, 7
 
 
 def tile_list_allele_mixture_scores_kernel(
@@ -40,7 +42,6 @@ def tile_list_allele_mixture_scores_kernel(
     with ExitStack() as ctx:
         keep = ctx.enter_context(tc.tile_pool(name="keep", bufs=1))
         laid = ctx.enter_context(tc.tile_pool(name="laid", bufs=1))
-        ring = ctx.enter_context(tc.tile_pool(name="ring", bufs=2))
         psum = ctx.enter_context(tc.psum_pool(name="psum", bufs=1))
 
         def held(name, shape, dtype):
@@ -52,43 +53,49 @@ def tile_list_allele_mixture_scores_kernel(
         def new_bank(name, bank):
             return psum.tile([P, PACK, CH], F32, name=name, tag=f"bank{bank}")
 
-        at_page2 = 0
-        at_wa_g0 = at_page2 + 4 * T2 - 64
-        at_wa_g1 = at_wa_g0 + 2 * PACK * H
-        at_w4 = at_wa_g1 + 4 * S
-        at_x = at_w4 + PASSES * 2 * H
-        at_tab_s = at_x + 4 * PACK * S
-        at_wroot = at_wa_g1 - 64
+        at_tab_s = 0
+        at_wa_g0 = at_tab_s + T
 
         picks = keep.tile([P, S // 16], U16, name="picks")
         bins = keep.tile([P, S // 16], U16, name="bins")
-        tab_s = placed("tab_s", [P, T], U8, at_tab_s)
+        tab_s = placed("tab_s", [P, T + SPARE], U8, at_tab_s)
+        weight_s = held("weight_s", [P, PASSES * H + N], U8)
+        w4_s_raw, w8_s = weight_s[:, 0 : PASSES * H], weight_s[:, PASSES * H :]
         wgo_rows = held("wgo_rows", [P, CH], F32)
-        w4_s_raw = held("w4_s_raw", [P, PASSES * H], U8)
         ident = held("ident", [P, P], F32)
-        pages = [held(f"page{i}", [P, T2], F32) for i in range(2)]
+        pages = [held(f"page{i}", [P, T2], F32) for i in range(PACK)]
 
-        nc.gpsimd.memset(tab_s[:].bitcast(I32), 0)
-        nc.gpsimd.memset(wgo_rows[:], 0.0)
-        nc.gpsimd.memset(w4_s_raw[:].bitcast(I32), 0)
+        nc.vector.memset(tab_s[:].bitcast(I32), 0)
+        nc.vector.memset(wgo_rows[:], 0.0)
+        nc.vector.memset(weight_s[:].bitcast(I32), 0)
         make_identity(nc, ident[:])
-        for lo, hi in ((0, T2 // 2 + 1), (T2 // 2 + 1, T2 // 2 + 2), (T2 // 2 + 2, T2)):
-            nc.vector.memset(pages[0][:, lo:hi].bitcast(I32), 0)
-        nc.vector.memset(pages[1][:].bitcast(I32), 0)
 
-        def load_rows(tile, rows):
+        def load_rows(name, rows):
+            tile = held(name, [P, PACK, rows.shape[1]], F32)
             nc.sync.dma_start(tile[:], rows.rearrange("(p j) c -> p j c", j=PACK))
+            return tile
 
-        def load_words(tile, words):
+        def load_words(name, words):
+            tile = held(name, [P, words.shape[1]], U32)
             nc.sync.dma_start(tile[:].bitcast(I32), words.rearrange("p t i -> p (t i)").bitcast(I32))
+            return tile
 
         nc.sync.dma_start(picks[:], offs)
+        w4_raw = held("w4_raw", [P, PASSES * 2 * H], U8)
+        nc.sync.dma_start(
+            w4_raw[:].bitcast(I32).rearrange("p (a c) -> p a c", a=PASSES),
+            w4_words.bitcast(I32).rearrange("a p c -> p a c"),
+        )
+        wa_raw0 = load_rows("wa_raw0", wa[0:512, :])
+        tab_w = [load_words(f"tab_w{a}", tab_words[a]) for a in range(PASSES)]
+        wa_raw1 = load_rows("wa_raw1", wa[512:1024, :])
+        for d in QUADRANTS:
+            nc.sync.dma_start(w8_s[32 * d : 32 * d + 4, :].bitcast(I32), w8_scales[0, 4 * d : 4 * d + 4, :].bitcast(I32))
+        w8_w = load_words("w8_w", w8_words[0])
+        wb_raw = load_rows("wb_raw", wb)
         nc.sync.dma_start(bins[:], offs2)
-        wa_raw0 = held("wa_raw0", [P, PACK, H], F32)
-        load_rows(wa_raw0, wa[0:512, :])
-        tab_w0 = held("tab_w0", [P, T], U32)
-        load_words(tab_w0, tab_words[0])
-        nc.scalar.dma_start(tab_s[0:P:4, :].bitcast(I32), tab_scales.bitcast(I32).rearrange("a q t -> q a t"))
+
+        nc.scalar.dma_start(tab_s[0:P:4, 0:T].bitcast(I32), tab_scales.bitcast(I32).rearrange("a q t -> q a t"))
         nc.scalar.dma_start(wgo_rows[0:FACTORS, :], wgo[0:P:GP, :])
         for d in QUADRANTS:
             nc.scalar.dma_start(
@@ -96,48 +103,40 @@ def tile_list_allele_mixture_scores_kernel(
                 w4_scales[:, 4 * d : 4 * d + 4, :].bitcast(I32).rearrange("a r c -> r a c"),
             )
 
+        for page in pages[0:2]:
+            nc.vector.memset(page[:].bitcast(I32), 0)
+        picked_s = held("picked_s", [P, S], U8)
+        nc.vector.tensor_copy(picked_s[:], tab_s[:].indirect(picks[:]))
+
         winv = held("winv", [P, FACTORS], F32)
-        w_bank = new_bank("w_bank", 7)
+        wroot = held("wroot", [P, FACTORS], F32)
+        w_bank = new_bank("w_bank", W_BANK)
         nc.tensor.transpose(w_bank[:, 0, :], wgo_rows[:], ident[:])
-        wroot = placed("wroot", [P, FACTORS], F32, at_wroot)
         nc.scalar.activation(wroot[:], w_bank[:, 0, 0:FACTORS], ACT.Abs_reciprocal_sqrt)
         nc.scalar.activation(winv[:], wroot[:], ACT.Square)
 
-        w4_raw = placed("w4_raw", [P, PASSES * 2 * H], U8, at_w4)
-        nc.sync.dma_start(
-            w4_raw[:].bitcast(I32).rearrange("p (a c) -> p a c", a=PASSES),
-            w4_words.bitcast(I32).rearrange("a p c -> p a c"),
+        w4_w = held("w4_w", [P, PASSES * 2 * H], U8)
+        w4_s = held("w4_s", [P, PASSES * H], U8)
+        nc.scalar.copy(
+            w4_w[:].bitcast(U16).rearrange("p (a t m) -> p a t m", a=PASSES, t=PACK),
+            w4_raw[:].bitcast(U16).rearrange("p (a m t) -> p a t m", a=PASSES, t=PACK),
         )
-
-        tab_w1 = held("tab_w1", [P, T], U32)
-        load_words(tab_w1, tab_words[1])
-        picked_s = held("picked_s", [P, S], U8)
-        nc.vector.tensor_copy(picked_s[:], tab_s[:].indirect(picks[:]))
         v_s = placed("v_s", [P, PASSES * S], U8, at_tab_s)
         for d in QUADRANTS:
-            nc.sync.dma_start(v_s[32 * d : 32 * d + 4, :].bitcast(I32), picked_s[32 * d : 32 * d + 32 : 4, :].bitcast(I32))
-        wa_raw1 = held("wa_raw1", [P, PACK, H], F32)
-        load_rows(wa_raw1, wa[512:1024, :])
-        wb_raw = held("wb_raw", [P, PACK, N], F32)
-        load_rows(wb_raw, wb)
-        w8_w = held("w8_w", [P, N], U32)
-        load_words(w8_w, w8_words[0])
+            nc.scalar.dma_start(v_s[32 * d : 32 * d + 4, :].bitcast(I32), picked_s[32 * d : 32 * d + 32 : 4, :].bitcast(I32))
+        nc.vector.tensor_copy(
+            w4_s[:].rearrange("p (a t m) -> p a t m", a=PASSES, t=PACK),
+            w4_s_raw.rearrange("p (a m t) -> p a t m", a=PASSES, t=PACK),
+        )
+        w4_q = [
+            [(w4_w[:, 2 * col : 2 * (col + P)].bitcast(FP4X4), w4_s[:, col : col + P]) for col in range(a * H, (a + 1) * H, P)]
+            for a in range(PASSES)
+        ]
+        nc.vector.memset(pages[2][:].bitcast(I32), 0)
 
-
-        def regroup(copy, grouped, raw, t0=0, t1=PACK):
-            copy(grouped.rearrange("p t m j -> p m j t"), raw[:].rearrange("p j (m t) -> p m j t", t=PACK)[:, :, :, t0:t1])
-
-        wa_g0 = placed("wa_g0", [P, PACK, P, PACK], BF16, at_wa_g0)
-        regroup(nc.scalar.copy, wa_g0[:], wa_raw0)
-
-        v_w = {}
-
-        def gather_words(a, c0, c1, picked):
-            nc.vector.tensor_copy(picked[:], (tab_w0, tab_w1)[a][:].indirect(picks[:, c0 * CH // 16 : c1 * CH // 16]))
-            for c in range(c0, c1):
-                v_w[a, c] = picked[:, (c - c0) * CH : (c - c0 + 1) * CH]
-
-        gather_words(0, 0, OPENED, held("v_w0_low", [P, OPENED * CH], U32))
+        def regroup(grouped, copy, raw, t0, t1):
+            copy(grouped[:].rearrange("p t m j -> p m j t"), raw[:].rearrange("p j (m t) -> p m j t", t=PACK)[:, :, :, t0:t1])
+            return grouped
 
         def quantise(name, grouped):
             slices = grouped.shape[1]
@@ -146,65 +145,48 @@ def tile_list_allele_mixture_scores_kernel(
             nc.vector.quantize_mx(codes[:].bitcast(FP8X4), scales[:], grouped[:].rearrange("p t m j -> p (t m j)"))
             return [(codes[:, t * P : (t + 1) * P].bitcast(FP8X4), scales[:, t * P : (t + 1) * P]) for t in range(slices)]
 
+        v_w = {}
 
-        wa_q = [quantise("wa_q0", wa_g0)]
-        pages.append(placed("page2", [P, T2], F32, at_page2))
-        nc.vector.memset(pages[2][:].bitcast(I32), 0)
-        w4_w = held("w4_w", [P, PASSES * 2 * H], U8)
-        w4_s = held("w4_s", [P, PASSES * H], U8)
-        nc.vector.tensor_copy(
-            w4_s[:].rearrange("p (a t m) -> p a t m", a=PASSES, t=PACK),
-            w4_s_raw[:].rearrange("p (a m t) -> p a t m", a=PASSES, t=PACK),
-        )
-        nc.vector.tensor_copy(
-            w4_w[:].bitcast(U16).rearrange("p (a t m) -> p a t m", a=PASSES, t=PACK),
-            w4_raw[:].bitcast(U16).rearrange("p (a m t) -> p a t m", a=PASSES, t=PACK),
-        )
-        w4_q = [
-            [(w4_w[:, 2 * col : 2 * (col + P)].bitcast(FP4X4), w4_s[:, col : col + P]) for col in range(a * H, (a + 1) * H, P)]
-            for a in range(PASSES)
-        ]
-        gather_words(0, OPENED, CHUNKS, placed("v_w0_high", [P, (CHUNKS - OPENED) * CH], U32, at_w4))
-        w8_s = w4_s_raw
-        for d in QUADRANTS:
-            nc.sync.dma_start(w8_s[32 * d : 32 * d + 4, 0:N].bitcast(I32), w8_scales[0, 4 * d : 4 * d + 4, :].bitcast(I32))
+        def gather_words(a, piece):
+            c0, c1 = GATHER_CUTS[a][piece : piece + 2]
+            picked = held(f"v_w{a}_{c0}", [P, (c1 - c0) * CH], U32)
+            nc.vector.tensor_copy(picked[:], tab_w[a][:].indirect(picks[:, c0 * CH // 16 : c1 * CH // 16]))
+            for c in range(c0, c1):
+                v_w[a, c] = picked[:, (c - c0) * CH : (c - c0 + 1) * CH]
 
-        def add_pass(bank, c, a, weights):
-            words = v_w[a, c]
+        banks = {}
+
+        def add_pass(name, c, a, weights):
+            if a == 0:
+                banks[name, c] = new_bank(f"{name}{c}", X_BANKS[c] if name == "x" else OPENED + c % OPENED)
             for t in range(PACK):
                 codes, scales = weights[a][t]
                 nc.tensor.matmul_mx(
-                    bank[:, t, :], lhsT=codes, lhsT_scale=scales,
-                    rhs=words.bitcast(FP8X4), rhs_scale=v_s[:, a * S + c * CH : a * S + (c + 1) * CH],
+                    banks[name, c][:, t, :], lhsT=codes, lhsT_scale=scales,
+                    rhs=v_w[a, c].bitcast(FP8X4), rhs_scale=v_s[:, a * S + c * CH : a * S + (c + 1) * CH],
                     start=(a == 0 and t == 0), stop=(a == PASSES - 1 and t == PACK - 1),
                 )
+
+        x_sb = {}
+
+        def project(c):
+            if c >= OPENED:
+                add_pass("x", c, 0, w4_q)
+            add_pass("x", c, 1, w4_q)
+            x_sb[c] = held(f"x{c}", [P, CH, PACK], F32)
+            nc.scalar.copy(x_sb[c][:], banks["x", c][:].rearrange("p t n -> p n t"))
 
         h_w = held("h_w", [P, S], U32)
         h_s = held("h_s", [P, S], U8)
         h_bf = held("h_bf", [P, S * PACK], BF16)
-        banks = {}
 
-        x_sb = {}
-
-        def open_sum(name, c, weights):
-            banks[name, c] = new_bank(f"{name}{c}", OPENED + c % OPENED if name == "av_bank" else X_BANKS[c])
-            add_pass(banks[name, c], c, 0, weights)
-
-        def project(c):
-            if ("x_bank", c) not in banks:
-                open_sum("x_bank", c, w4_q)
-            add_pass(banks["x_bank", c], c, 1, w4_q)
-            x_sb[c] = placed(f"x{c}", [P, CH, PACK], F32, at_x + 4 * CH * PACK * c)
-            nc.scalar.copy(x_sb[c][:], banks["x_bank", c][:].rearrange("p t n -> p n t"))
-
-        def first_stage(c):
-            if ("av_bank", c) not in banks:
-                open_sum("av_bank", c, wa_q)
-            av_bank = banks["av_bank", c]
-            add_pass(av_bank, c, 1, wa_q)
+        def make_h(c):
+            if c >= OPENED:
+                add_pass("av", c, 0, wa_q)
+            add_pass("av", c, 1, wa_q)
             nc.vector.tensor_tensor(
                 h_bf[:, c * CH * PACK : (c + 1) * CH * PACK].rearrange("p (n t) -> p n t", t=PACK),
-                av_bank[:].rearrange("p t n -> p n t"), x_sb[c][:], MULT,
+                banks["av", c][:].rearrange("p t n -> p n t"), x_sb[c][:], MULT,
             )
 
         def quantise_h(piece):
@@ -215,7 +197,6 @@ def tile_list_allele_mixture_scores_kernel(
 
         b_sb = held("b_sb", [P, PACK, S], F32)
         damp = held("damp", [P, PACK, S], F32)
-
         squares, roots = {}, {}
 
         def h_of(c):
@@ -223,13 +204,13 @@ def tile_list_allele_mixture_scores_kernel(
 
         def multiply_d(c):
             hw, hs = h_of(c)
-            banks["d", c] = new_bank(f"d_bank{c}", (2, 4)[c % 2])[:].rearrange("p i m -> p (i m)")
+            banks["d", c] = new_bank(f"d{c}", D_BANK)[:].rearrange("p i m -> p (i m)")
             nc.tensor.matmul_mx(
-                banks["d", c], lhsT=hw, lhsT_scale=hs, rhs=w8_w[:].bitcast(FP8X4), rhs_scale=w8_s[:, 0:N], start=True, stop=True
+                banks["d", c], lhsT=hw, lhsT_scale=hs, rhs=w8_w[:].bitcast(FP8X4), rhs_scale=w8_s, start=True, stop=True
             )
 
         def square_d(c):
-            squares[c] = ring.tile([P, PACK, P], F32, name="sq")
+            squares[c] = held(f"square{c}", [P, PACK, P], F32)
             nc.scalar.activation(squares[c][:], banks["d", c].rearrange("p (m i) -> p i m", i=PACK), ACT.Square)
 
         def take_roots(c):
@@ -241,29 +222,30 @@ def tile_list_allele_mixture_scores_kernel(
                     bias=factor, scale=factor,
                 )
 
-        def prompt_rows(c):
-            return 1 + sum(c < LAST_FROM[i] for i in range(1, PACK))
-
         def multiply_b(c):
             hw, hs = h_of(c)
-            banks["b", c] = new_bank(f"b_bank{c}", c % 2)
-            for i in range(prompt_rows(c)):
+            banks["b", c] = new_bank(f"b{c}", B_BANK)
+            for i in range(PACK):
                 nc.tensor.matmul_mx(
                     banks["b", c][:, i, :], lhsT=wb_q[i][0], lhsT_scale=wb_q[i][1], rhs=hw, rhs_scale=hs, start=True, stop=True
                 )
 
         def copy_b(c):
-            rows = prompt_rows(c)
-            nc.scalar.copy(b_sb[:, 0:rows, c * CH : (c + 1) * CH], banks["b", c][:, 0:rows, :])
+            nc.scalar.copy(b_sb[:, :, c * CH : (c + 1) * CH], banks["b", c][:])
 
         def turn_roots(c):
-            banks["r", c] = new_bank(f"r_bank{c}", (3, 5)[c % 2])
-            for i in range(prompt_rows(c)):
+            banks["r", c] = new_bank(f"r{c}", R_BANK)
+            for i in range(PACK):
                 nc.tensor.transpose(banks["r", c][:, i, :], roots[c][:, i, :], ident[:])
 
         def square_roots(c):
-            rows = prompt_rows(c)
-            nc.scalar.activation(damp[:, 0:rows, c * CH : (c + 1) * CH], banks["r", c][:, 0:rows, :], ACT.Square)
+            nc.scalar.activation(damp[:, :, c * CH : (c + 1) * CH], banks["r", c][:], ACT.Square)
+
+        def put(i, c0, c1):
+            nc.vector.tensor_tensor(
+                pages[i][:].indirect(bins[:, c0 * CH // 16 : c1 * CH // 16]),
+                b_sb[:, i, c0 * CH : c1 * CH], damp[:, i, c0 * CH : c1 * CH], MULT,
+            )
 
         def second_stage(c):
             turn_roots(c)
@@ -276,89 +258,57 @@ def tile_list_allele_mixture_scores_kernel(
             if c + 1 < CHUNKS:
                 multiply_b(c + 1)
                 take_roots(c + 1)
-
-        def late_rows(i):
-            c0 = LAST_FROM[i]
-            cols, count = slice(c0 * CH, S), CHUNKS - c0
-            b_bank = new_bank(f"b_late{i}", (6, 7, 2)[i - 1])
-            for c in range(c0, CHUNKS):
-                hw, hs = h_of(c)
-                nc.tensor.matmul_mx(
-                    b_bank[:, c - c0, :], lhsT=wb_q[i][0], lhsT_scale=wb_q[i][1], rhs=hw, rhs_scale=hs, start=True, stop=True
-                )
-            nc.scalar.copy(b_sb[:, i, cols], b_bank[:, 0:count, :].rearrange("p c n -> p (c n)"))
-            r_bank = new_bank(f"r_late{i}", (4, 3, 0)[i - 1])
-            for c in range(c0, CHUNKS):
-                nc.tensor.transpose(r_bank[:, c - c0, :], roots[c][:, i, :], ident[:])
-            nc.scalar.activation(damp[:, i, cols], r_bank[:, 0:count, :].rearrange("p c n -> p (c n)"), ACT.Square)
-
-        def put(i, c0, c1):
-            nc.vector.tensor_tensor(
-                pages[i][:].indirect(bins[:, c0 * CH // 16 : c1 * CH // 16]),
-                b_sb[:, i, c0 * CH : c1 * CH], damp[:, i, c0 * CH : c1 * CH], MULT,
-            )
-
-        def scatter(c):
             for i in range(PACK):
                 if c < LAST_FROM[i]:
                     put(i, c, c + 1)
 
+        wa_g0 = regroup(placed("wa_g0", [P, PACK, P, PACK], BF16, at_wa_g0), nc.scalar.copy, wa_raw0, 0, PACK)
+        gather_words(0, 0)
+        wa_q = [quantise("wa_q0", wa_g0)]
+        gather_words(0, 1)
         for c in range(OPENED):
-            open_sum("x_bank", c, w4_q)
-        for c in range(2):
-            open_sum("av_bank", c, wa_q)
-        for c0, c1 in zip(GATHER_CUTS, GATHER_CUTS[1:]):
-            gather_words(1, c0, c1, held(f"v_w1_{c0}", [P, (c1 - c0) * CH], U32))
-        for c in range(2):
-            project(c)
-        wa_low = held("wa_low", [P, 2, P, PACK], BF16)
-        regroup(nc.vector.tensor_copy, wa_low[:], wa_raw1, 0, 2)
-        wa_high = placed("wa_high", [P, 2, P, PACK], BF16, at_wa_g1)
-        regroup(nc.scalar.copy, wa_high[:], wa_raw1, 2, PACK)
-        wa_q.append(quantise("wa_q1a", wa_low) + quantise("wa_q1b", wa_high))
-        for c in range(2, OPENED):
-            project(c)
-            open_sum("av_bank", c, wa_q)
-        first_stage(0)
-        project(4)
-        first_stage(1)
-        quantise_h(0)
-        project(5)
-        wb_g = held("wb_g", [P, PACK, P, PACK], BF16)
-        regroup(nc.vector.tensor_copy, wb_g[:], wb_raw)
-        first_stage(2)
-        wb_q = quantise("wb_q", wb_g)
-        quantise_h(1)
-        first_stage(3)
-        project(6)
-        pages.append(placed("page3", [P, T2], F32, at_x))
+            add_pass("x", c, 0, w4_q)
+        for c in range(OPENED):
+            add_pass("av", c, 0, wa_q)
+        gather_words(1, 0)
+        gather_words(1, 1)
         nc.vector.memset(pages[3][:].bitcast(I32), 0)
-        quantise_h(2)
+        project(0)
+        project(1)
+        wa_low = regroup(held("wa_low", [P, 2, P, PACK], BF16), nc.vector.tensor_copy, wa_raw1, 0, 2)
+        wa_high = regroup(placed("wa_high", [P, 2, P, PACK], BF16, at_wa_g0), nc.scalar.copy, wa_raw1, 2, PACK)
+        gather_words(1, 2)
+        wa_q.append(quantise("wa_q1a", wa_low) + quantise("wa_q1b", wa_high))
+        gather_words(1, 3)
+        project(2)
+        project(3)
+        make_h(0)
+        make_h(1)
+        quantise_h(0)
         multiply_d(0)
+        make_h(2)
+        quantise_h(1)
+        project(4)
+        make_h(3)
         square_d(0)
-        first_stage(4)
-        project(7)
+        wb_g = regroup(held("wb_g", [P, PACK, P, PACK], BF16), nc.vector.tensor_copy, wb_raw, 0, PACK)
         take_roots(0)
-        first_stage(5)
-        multiply_b(0)
-        turn_roots(0)
         multiply_d(1)
+        project(5)
+        quantise_h(2)
+        wb_q = quantise("wb_q", wb_g)
+        make_h(4)
+        multiply_b(0)
+        make_h(5)
         quantise_h(3)
-        first_stage(6)
-        copy_b(0)
-        square_roots(0)
-        square_d(1)
-        first_stage(7)
-        take_roots(1)
-        multiply_b(1)
-        multiply_d(2)
-        scatter(0)
+        second_stage(0)
+        project(6)
+        make_h(6)
+        project(7)
+        make_h(7)
         quantise_h(4)
         for c in range(1, CHUNKS):
             second_stage(c)
-            scatter(c)
         for i in range(PACK):
-            if i > 0:
-                late_rows(i)
             put(i, LAST_FROM[i], CHUNKS)
             nc.sync.dma_start(out.rearrange("(p i) t -> p i t", i=PACK)[:, i, :], pages[i][:])

@@ -27,12 +27,14 @@ GP = P // GROUPS
 OPENED = 4
 FACTORS = GROUPS * CHUNKS
 GATHER_CUTS = ((0, 4, 8), (0, 2, 4, 6, 8))
-SPARE = 64
+HALF = N // 2
+ROW = S + H + HALF
 QUANTISE_CUTS = (0, 1, 2, 4, 6, 8)
 QUADRANTS = (0, 2, 1, 3)
 LAST_FROM = (7, 6, 5, 5)
-X_BANKS = (0, 1, 2, 3, 0, 1, 1, 1)
-B_BANK, D_BANK, R_BANK, W_BANK = 0, 2, 3, 7
+X_BANKS = (0, 2, 2, 2)
+D_BANK, R_BANK, W_BANK = 0, 1, 7
+B_BANKS = (2, 4, 4)
 
 
 def tile_list_allele_mixture_scores_kernel(
@@ -54,24 +56,31 @@ def tile_list_allele_mixture_scores_kernel(
             return psum.tile([P, PACK, CH], F32, name=name, tag=f"bank{bank}")
 
         at_tab_s = 0
-        at_wa_g0 = at_tab_s + T
+        at_w4_raw = at_tab_s + T
+        at_page3 = at_w4_raw + PASSES * 2 * H
+        at_wa_g0 = at_page3 + 4 * T2
+        x_bytes = 4 * 2 * CH * PACK
+        at_wa_raw1 = at_wa_g0 + 2 * PACK * H + x_bytes
+        at_wb_raw = at_wa_raw1 + 2 * x_bytes
+        at_x = (at_wa_raw1 - x_bytes, at_wa_raw1, at_wb_raw, at_wb_raw + x_bytes)
 
         picks = keep.tile([P, S // 16], U16, name="picks")
         bins = keep.tile([P, S // 16], U16, name="bins")
-        tab_s = placed("tab_s", [P, T + SPARE], U8, at_tab_s)
-        weight_s = held("weight_s", [P, PASSES * H + N], U8)
-        w4_s_raw, w8_s = weight_s[:, 0 : PASSES * H], weight_s[:, PASSES * H :]
+        tab_s = placed("tab_s", [P, T], U8, at_tab_s)
+        w4_s_raw = held("w4_s_raw", [P, H], U8)
+        rows_s = placed("rows_s", [P, ROW], U8, at_page3)
         wgo_rows = held("wgo_rows", [P, CH], F32)
         ident = held("ident", [P, P], F32)
-        pages = [held(f"page{i}", [P, T2], F32) for i in range(PACK)]
+        pages = [held("page0", [P, T2], F32)]
 
-        nc.vector.memset(tab_s[:].bitcast(I32), 0)
-        nc.vector.memset(wgo_rows[:], 0.0)
-        nc.vector.memset(weight_s[:].bitcast(I32), 0)
+        nc.gpsimd.memset(tab_s[:].bitcast(I32), 0)
+        nc.gpsimd.memset(w4_s_raw[:].bitcast(I32), 0)
+        nc.gpsimd.memset(wgo_rows[:], 0.0)
         make_identity(nc, ident[:])
+        for lo, hi in ((0, T2 // 2 + 1), (T2 // 2 + 1, T2 // 2 + 2), (T2 // 2 + 2, T2)):
+            nc.vector.memset(pages[0][:, lo:hi].bitcast(I32), 0)
 
-        def load_rows(name, rows):
-            tile = held(name, [P, PACK, rows.shape[1]], F32)
+        def load_rows(tile, rows):
             nc.sync.dma_start(tile[:], rows.rearrange("(p j) c -> p j c", j=PACK))
             return tile
 
@@ -81,32 +90,28 @@ def tile_list_allele_mixture_scores_kernel(
             return tile
 
         nc.sync.dma_start(picks[:], offs)
-        w4_raw = held("w4_raw", [P, PASSES * 2 * H], U8)
+        w4_raw = placed("w4_raw", [P, PASSES * 2 * H], U8, at_w4_raw)
         nc.sync.dma_start(
             w4_raw[:].bitcast(I32).rearrange("p (a c) -> p a c", a=PASSES),
             w4_words.bitcast(I32).rearrange("a p c -> p a c"),
         )
-        wa_raw0 = load_rows("wa_raw0", wa[0:512, :])
+        nc.sync.dma_start(rows_s[0:P:4, S + H : ROW].bitcast(I32), w8_scales[0].bitcast(I32))
+        nc.sync.dma_start(tab_s[0:P:4, :].bitcast(I32), tab_scales.bitcast(I32).rearrange("a q t -> q a t"))
+        nc.sync.dma_start(w4_s_raw[0:P:4, :].bitcast(I32), w4_scales.bitcast(I32).rearrange("a q c -> q a c"))
+        nc.sync.dma_start(wgo_rows[0:FACTORS, :], wgo[0:P:GP, :])
+        wa_raw0 = load_rows(held("wa_raw0", [P, PACK, H], F32), wa[0:512, :])
         tab_w = [load_words(f"tab_w{a}", tab_words[a]) for a in range(PASSES)]
-        wa_raw1 = load_rows("wa_raw1", wa[512:1024, :])
-        for d in QUADRANTS:
-            nc.sync.dma_start(w8_s[32 * d : 32 * d + 4, :].bitcast(I32), w8_scales[0, 4 * d : 4 * d + 4, :].bitcast(I32))
-        w8_w = load_words("w8_w", w8_words[0])
-        wb_raw = load_rows("wb_raw", wb)
-        nc.sync.dma_start(bins[:], offs2)
 
-        nc.scalar.dma_start(tab_s[0:P:4, 0:T].bitcast(I32), tab_scales.bitcast(I32).rearrange("a q t -> q a t"))
-        nc.scalar.dma_start(wgo_rows[0:FACTORS, :], wgo[0:P:GP, :])
-        for d in QUADRANTS:
-            nc.scalar.dma_start(
-                w4_s_raw[32 * d : 32 * d + 4, :].bitcast(I32).rearrange("r (a c) -> r a c", a=PASSES),
-                w4_scales[:, 4 * d : 4 * d + 4, :].bitcast(I32).rearrange("a r c -> r a c"),
-            )
-
-        for page in pages[0:2]:
-            nc.vector.memset(page[:].bitcast(I32), 0)
+        pages.append(held("page1", [P, T2], F32))
+        nc.vector.memset(pages[1][:].bitcast(I32), 0)
         picked_s = held("picked_s", [P, S], U8)
         nc.vector.tensor_copy(picked_s[:], tab_s[:].indirect(picks[:]))
+        nc.vector.tensor_copy(
+            rows_s[:, S : S + H].rearrange("p (t m) -> p t m", t=PACK), w4_s_raw[:].rearrange("p (m t) -> p t m", t=PACK)
+        )
+        nc.vector.tensor_copy(rows_s[:, 0:S].bitcast(I32), picked_s[:].bitcast(I32))
+        pages.append(held("page2", [P, T2], F32))
+        nc.vector.memset(pages[2][:].bitcast(I32), 0)
 
         winv = held("winv", [P, FACTORS], F32)
         wroot = held("wroot", [P, FACTORS], F32)
@@ -116,23 +121,24 @@ def tile_list_allele_mixture_scores_kernel(
         nc.scalar.activation(winv[:], wroot[:], ACT.Square)
 
         w4_w = held("w4_w", [P, PASSES * 2 * H], U8)
-        w4_s = held("w4_s", [P, PASSES * H], U8)
         nc.scalar.copy(
             w4_w[:].bitcast(U16).rearrange("p (a t m) -> p a t m", a=PASSES, t=PACK),
             w4_raw[:].bitcast(U16).rearrange("p (a m t) -> p a t m", a=PASSES, t=PACK),
         )
-        v_s = placed("v_s", [P, PASSES * S], U8, at_tab_s)
+        planes = placed("planes", [P, PASSES * ROW], U8, at_tab_s)
         for d in QUADRANTS:
-            nc.scalar.dma_start(v_s[32 * d : 32 * d + 4, :].bitcast(I32), picked_s[32 * d : 32 * d + 32 : 4, :].bitcast(I32))
-        nc.vector.tensor_copy(
-            w4_s[:].rearrange("p (a t m) -> p a t m", a=PASSES, t=PACK),
-            w4_s_raw.rearrange("p (a m t) -> p a t m", a=PASSES, t=PACK),
-        )
+            nc.sync.dma_start(planes[32 * d : 32 * d + 4, :].bitcast(I32), rows_s[32 * d : 32 * d + 32 : 4, :].bitcast(I32))
+        wa_raw1 = load_rows(placed("wa_raw1", [P, PACK, H], F32, at_wa_raw1), wa[512:1024, :])
+        w8_w = load_words("w8_w", w8_words[0])
+        wb_raw = load_rows(placed("wb_raw", [P, PACK, N], F32, at_wb_raw), wb)
+        nc.sync.dma_start(bins[:], offs2)
         w4_q = [
-            [(w4_w[:, 2 * col : 2 * (col + P)].bitcast(FP4X4), w4_s[:, col : col + P]) for col in range(a * H, (a + 1) * H, P)]
+            [
+                (w4_w[:, 2 * (a * H + col) : 2 * (a * H + col + P)].bitcast(FP4X4), planes[:, a * ROW + S + col : a * ROW + S + col + P])
+                for col in range(0, H, P)
+            ]
             for a in range(PASSES)
         ]
-        nc.vector.memset(pages[2][:].bitcast(I32), 0)
 
         def regroup(grouped, copy, raw, t0, t1):
             copy(grouped[:].rearrange("p t m j -> p m j t"), raw[:].rearrange("p j (m t) -> p m j t", t=PACK)[:, :, :, t0:t1])
@@ -147,34 +153,53 @@ def tile_list_allele_mixture_scores_kernel(
 
         v_w = {}
 
-        def gather_words(a, piece):
+        def gather_words(a, piece, at=None):
             c0, c1 = GATHER_CUTS[a][piece : piece + 2]
-            picked = held(f"v_w{a}_{c0}", [P, (c1 - c0) * CH], U32)
+            name, shape = f"v_w{a}_{c0}", [P, (c1 - c0) * CH]
+            picked = held(name, shape, U32) if at is None else placed(name, shape, U32, at)
             nc.vector.tensor_copy(picked[:], tab_w[a][:].indirect(picks[:, c0 * CH // 16 : c1 * CH // 16]))
             for c in range(c0, c1):
-                v_w[a, c] = picked[:, (c - c0) * CH : (c - c0 + 1) * CH]
+                v_w[a, c] = (picked, c0)
+
+        def picked_columns(a, c, count):
+            picked, c0 = v_w[a, c]
+            words = picked[:, (c - c0) * CH : (c - c0 + count) * CH]
+            return words.bitcast(FP8X4), planes[:, a * ROW + c * CH : a * ROW + (c + count) * CH]
 
         banks = {}
 
-        def add_pass(name, c, a, weights):
+        def add_av_pass(c, a):
             if a == 0:
-                banks[name, c] = new_bank(f"{name}{c}", X_BANKS[c] if name == "x" else OPENED + c % OPENED)
+                banks["av", c] = new_bank(f"av{c}", OPENED + c % OPENED)
+            words, word_scales = picked_columns(a, c, 1)
             for t in range(PACK):
-                codes, scales = weights[a][t]
+                codes, scales = wa_q[a][t]
                 nc.tensor.matmul_mx(
-                    banks[name, c][:, t, :], lhsT=codes, lhsT_scale=scales,
-                    rhs=v_w[a, c].bitcast(FP8X4), rhs_scale=v_s[:, a * S + c * CH : a * S + (c + 1) * CH],
+                    banks["av", c][:, t, :], lhsT=codes, lhsT_scale=scales, rhs=words, rhs_scale=word_scales,
                     start=(a == 0 and t == 0), stop=(a == PASSES - 1 and t == PACK - 1),
+                )
+
+        def add_x_pass(pair, u, a):
+            if a == 0:
+                bank = new_bank(f"x{pair}_{u}", X_BANKS[pair] + u)
+                banks["x", pair, u] = bank[:].rearrange("p (e h) n -> p e (h n)", e=2)
+            words, word_scales = picked_columns(a, 2 * pair, 2)
+            for e in range(2):
+                codes, scales = w4_q[a][2 * u + e]
+                nc.tensor.matmul_mx(
+                    banks["x", pair, u][:, e, :], lhsT=codes, lhsT_scale=scales, rhs=words, rhs_scale=word_scales,
+                    start=(a == 0 and e == 0), stop=(a == PASSES - 1 and e == 1),
                 )
 
         x_sb = {}
 
-        def project(c):
-            if c >= OPENED:
-                add_pass("x", c, 0, w4_q)
-            add_pass("x", c, 1, w4_q)
-            x_sb[c] = held(f"x{c}", [P, CH, PACK], F32)
-            nc.scalar.copy(x_sb[c][:], banks["x", c][:].rearrange("p t n -> p n t"))
+        def project(pair):
+            x_sb[pair] = placed(f"x{pair}", [P, 2, 2 * CH, 2], F32, at_x[pair])
+            for u in range(2):
+                if pair > 0:
+                    add_x_pass(pair, u, 0)
+                add_x_pass(pair, u, 1)
+                nc.scalar.copy(x_sb[pair][:, u, :, :], banks["x", pair, u].rearrange("p e n -> p n e"))
 
         h_w = held("h_w", [P, S], U32)
         h_s = held("h_s", [P, S], U8)
@@ -182,11 +207,13 @@ def tile_list_allele_mixture_scores_kernel(
 
         def make_h(c):
             if c >= OPENED:
-                add_pass("av", c, 0, wa_q)
-            add_pass("av", c, 1, wa_q)
+                add_av_pass(c, 0)
+            add_av_pass(c, 1)
             nc.vector.tensor_tensor(
-                h_bf[:, c * CH * PACK : (c + 1) * CH * PACK].rearrange("p (n t) -> p n t", t=PACK),
-                banks["av", c][:].rearrange("p t n -> p n t"), x_sb[c][:], MULT,
+                h_bf[:, c * CH * PACK : (c + 1) * CH * PACK].rearrange("p (n u e) -> p n u e", u=2, e=2),
+                banks["av", c][:].rearrange("p (u e) n -> p n u e", u=2),
+                x_sb[c // 2][:, :, c % 2 * CH : (c % 2 + 1) * CH, :].rearrange("p u n e -> p n u e"),
+                MULT,
             )
 
         def quantise_h(piece):
@@ -205,9 +232,12 @@ def tile_list_allele_mixture_scores_kernel(
         def multiply_d(c):
             hw, hs = h_of(c)
             banks["d", c] = new_bank(f"d{c}", D_BANK)[:].rearrange("p i m -> p (i m)")
-            nc.tensor.matmul_mx(
-                banks["d", c], lhsT=hw, lhsT_scale=hs, rhs=w8_w[:].bitcast(FP8X4), rhs_scale=w8_s, start=True, stop=True
-            )
+            for u in range(2):
+                nc.tensor.matmul_mx(
+                    banks["d", c][:, u * HALF : (u + 1) * HALF], lhsT=hw, lhsT_scale=hs,
+                    rhs=w8_w[:, u * HALF : (u + 1) * HALF].bitcast(FP8X4), rhs_scale=planes[:, u * ROW + S + H : (u + 1) * ROW],
+                    start=True, stop=True,
+                )
 
         def square_d(c):
             squares[c] = held(f"square{c}", [P, PACK, P], F32)
@@ -224,7 +254,7 @@ def tile_list_allele_mixture_scores_kernel(
 
         def multiply_b(c):
             hw, hs = h_of(c)
-            banks["b", c] = new_bank(f"b{c}", B_BANK)
+            banks["b", c] = new_bank(f"b{c}", B_BANKS[min(c, 2)])
             for i in range(PACK):
                 nc.tensor.matmul_mx(
                     banks["b", c][:, i, :], lhsT=wb_q[i][0], lhsT_scale=wb_q[i][1], rhs=hw, rhs_scale=hs, start=True, stop=True
@@ -258,6 +288,8 @@ def tile_list_allele_mixture_scores_kernel(
             if c + 1 < CHUNKS:
                 multiply_b(c + 1)
                 take_roots(c + 1)
+
+        def scatter(c):
             for i in range(PACK):
                 if c < LAST_FROM[i]:
                     put(i, c, c + 1)
@@ -266,49 +298,57 @@ def tile_list_allele_mixture_scores_kernel(
         gather_words(0, 0)
         wa_q = [quantise("wa_q0", wa_g0)]
         gather_words(0, 1)
-        for c in range(OPENED):
-            add_pass("x", c, 0, w4_q)
-        for c in range(OPENED):
-            add_pass("av", c, 0, wa_q)
+        for u in range(2):
+            add_x_pass(0, u, 0)
         gather_words(1, 0)
         gather_words(1, 1)
+        gather_words(1, 2)
+        pages.append(placed("page3", [P, T2], F32, at_page3))
         nc.vector.memset(pages[3][:].bitcast(I32), 0)
         project(0)
-        project(1)
+        for c in range(2):
+            add_av_pass(c, 0)
         wa_low = regroup(held("wa_low", [P, 2, P, PACK], BF16), nc.vector.tensor_copy, wa_raw1, 0, 2)
         wa_high = regroup(placed("wa_high", [P, 2, P, PACK], BF16, at_wa_g0), nc.scalar.copy, wa_raw1, 2, PACK)
-        gather_words(1, 2)
+        project(1)
+        for c in range(2, OPENED):
+            add_av_pass(c, 0)
         wa_q.append(quantise("wa_q1a", wa_low) + quantise("wa_q1b", wa_high))
-        gather_words(1, 3)
-        project(2)
-        project(3)
+        gather_words(1, 3, at_wa_g0)
+        wb_high = regroup(held("wb_high", [P, 2, P, PACK], BF16), nc.scalar.copy, wb_raw, 2, PACK)
         make_h(0)
         make_h(1)
         quantise_h(0)
         multiply_d(0)
+        wb_low = regroup(held("wb_low", [P, 2, P, PACK], BF16), nc.vector.tensor_copy, wb_raw, 0, 2)
         make_h(2)
         quantise_h(1)
-        project(4)
         make_h(3)
+        wb_q = quantise("wb_qa", wb_low) + quantise("wb_qb", wb_high)
         square_d(0)
-        wb_g = regroup(held("wb_g", [P, PACK, P, PACK], BF16), nc.vector.tensor_copy, wb_raw, 0, PACK)
         take_roots(0)
         multiply_d(1)
-        project(5)
+        project(2)
         quantise_h(2)
-        wb_q = quantise("wb_q", wb_g)
-        make_h(4)
         multiply_b(0)
+        make_h(4)
         make_h(5)
         quantise_h(3)
-        second_stage(0)
-        project(6)
+        turn_roots(0)
+        copy_b(0)
+        square_roots(0)
+        square_d(1)
+        multiply_d(2)
+        multiply_b(1)
+        take_roots(1)
+        scatter(0)
+        project(3)
         make_h(6)
-        project(7)
         make_h(7)
         quantise_h(4)
         for c in range(1, CHUNKS):
             second_stage(c)
+            scatter(c)
         for i in range(PACK):
             put(i, LAST_FROM[i], CHUNKS)
             nc.sync.dma_start(out.rearrange("(p i) t -> p i t", i=PACK)[:, i, :], pages[i][:])

@@ -26,15 +26,17 @@ GROUPS = 8
 GP = P // GROUPS
 OPENED = 4
 FACTORS = GROUPS * CHUNKS
-GATHER_CUTS = ((0, 4, 8), (0, 2, 4, 6, 8))
+GATHER_CUTS = ((0, 2, 8), (0, 2, 4, 6, 8))
 HALF = N // 2
 ROW = S + H + HALF
 QUANTISE_CUTS = (0, 1, 2, 4, 6, 8)
+UNDER_LAST_PAGE = 3
 QUADRANTS = (0, 2, 1, 3)
 LAST_FROM = (7, 6, 5, 5)
-X_BANKS = (0, 2, 2, 2)
-D_BANK, R_BANK, W_BANK = 0, 1, 7
-B_BANKS = (2, 4, 4)
+X_BANKS = (0, 2, 4, 2)
+AV_BANKS = (4, 5, 6, 7, 0, 1, 6, 7)
+D_BANKS, R_BANKS = (2, 5), (3, 0)
+B_BANK, W_BANK = 4, 7
 
 
 def tile_list_allele_mixture_scores_kernel(
@@ -57,18 +59,18 @@ def tile_list_allele_mixture_scores_kernel(
 
         at_tab_s = 0
         at_w4_raw = at_tab_s + T
-        at_page3 = at_w4_raw + PASSES * 2 * H
+        at_page2 = at_w4_raw + PASSES * 2 * H
+        at_page3 = at_page2 + 4 * T2
         at_wa_g0 = at_page3 + 4 * T2
-        x_bytes = 4 * 2 * CH * PACK
-        at_wa_raw1 = at_wa_g0 + 2 * PACK * H + x_bytes
-        at_wb_raw = at_wa_raw1 + 2 * x_bytes
-        at_x = (at_wa_raw1 - x_bytes, at_wa_raw1, at_wb_raw, at_wb_raw + x_bytes)
+        at_wb_raw = at_wa_g0 + 2 * PACK * H
+        at_root0 = at_wb_raw + 4 * PACK * N + 2 * N
+        x_words = 2 * CH * PACK
 
         picks = keep.tile([P, S // 16], U16, name="picks")
         bins = keep.tile([P, S // 16], U16, name="bins")
         tab_s = placed("tab_s", [P, T], U8, at_tab_s)
         w4_s_raw = held("w4_s_raw", [P, H], U8)
-        rows_s = placed("rows_s", [P, ROW], U8, at_page3)
+        rows_s = held("rows_s", [P, ROW], U8)
         wgo_rows = held("wgo_rows", [P, CH], F32)
         ident = held("ident", [P, P], F32)
         pages = [held("page0", [P, T2], F32)]
@@ -81,7 +83,7 @@ def tile_list_allele_mixture_scores_kernel(
             nc.vector.memset(pages[0][:, lo:hi].bitcast(I32), 0)
 
         def load_rows(tile, rows):
-            nc.sync.dma_start(tile[:], rows.rearrange("(p j) c -> p j c", j=PACK))
+            nc.sync.dma_start(tile, rows.rearrange("(p j) c -> p j c", j=PACK))
             return tile
 
         def load_words(name, words):
@@ -98,19 +100,21 @@ def tile_list_allele_mixture_scores_kernel(
         nc.sync.dma_start(rows_s[0:P:4, S + H : ROW].bitcast(I32), w8_scales[0].bitcast(I32))
         nc.sync.dma_start(tab_s[0:P:4, :].bitcast(I32), tab_scales.bitcast(I32).rearrange("a q t -> q a t"))
         nc.sync.dma_start(w4_s_raw[0:P:4, :].bitcast(I32), w4_scales.bitcast(I32).rearrange("a q c -> q a c"))
+        wa_raw0 = load_rows(held("wa_raw0", [P, PACK, H], F32)[:], wa[0:512, :])
         nc.sync.dma_start(wgo_rows[0:FACTORS, :], wgo[0:P:GP, :])
-        wa_raw0 = load_rows(held("wa_raw0", [P, PACK, H], F32), wa[0:512, :])
-        tab_w = [load_words(f"tab_w{a}", tab_words[a]) for a in range(PASSES)]
+        tab_w = [load_words("tab_w0", tab_words[0]), held("tab_w1", [P, T], U32)]
+        late_words = tab_words[1].rearrange("p t i -> p (t i)").bitcast(I32)
+        nc.sync.dma_start(tab_w[1][:, : T // 2].bitcast(I32), late_words[:, : T // 2])
 
         pages.append(held("page1", [P, T2], F32))
         nc.vector.memset(pages[1][:].bitcast(I32), 0)
-        picked_s = held("picked_s", [P, S], U8)
+        picked_s = placed("picked_s", [P, S], U8, at_page2)
         nc.vector.tensor_copy(picked_s[:], tab_s[:].indirect(picks[:]))
         nc.vector.tensor_copy(
             rows_s[:, S : S + H].rearrange("p (t m) -> p t m", t=PACK), w4_s_raw[:].rearrange("p (m t) -> p t m", t=PACK)
         )
         nc.vector.tensor_copy(rows_s[:, 0:S].bitcast(I32), picked_s[:].bitcast(I32))
-        pages.append(held("page2", [P, T2], F32))
+        pages.append(placed("page2", [P, T2], F32, at_page2))
         nc.vector.memset(pages[2][:].bitcast(I32), 0)
 
         winv = held("winv", [P, FACTORS], F32)
@@ -128,9 +132,11 @@ def tile_list_allele_mixture_scores_kernel(
         planes = placed("planes", [P, PASSES * ROW], U8, at_tab_s)
         for d in QUADRANTS:
             nc.sync.dma_start(planes[32 * d : 32 * d + 4, :].bitcast(I32), rows_s[32 * d : 32 * d + 32 : 4, :].bitcast(I32))
-        wa_raw1 = load_rows(placed("wa_raw1", [P, PACK, H], F32, at_wa_raw1), wa[512:1024, :])
+        nc.sync.dma_start(tab_w[1][:, T // 2 :].bitcast(I32), late_words[:, T // 2 :])
+        stage = held("stage", [P, 3 * x_words], F32)
+        wa_raw1 = load_rows(stage[:, : PACK * H].rearrange("p (j c) -> p j c", j=PACK), wa[512:1024, :])
         w8_w = load_words("w8_w", w8_words[0])
-        wb_raw = load_rows(placed("wb_raw", [P, PACK, N], F32, at_wb_raw), wb)
+        wb_raw = load_rows(placed("wb_raw", [P, PACK, N], F32, at_wb_raw)[:], wb)
         nc.sync.dma_start(bins[:], offs2)
         w4_q = [
             [
@@ -141,7 +147,7 @@ def tile_list_allele_mixture_scores_kernel(
         ]
 
         def regroup(grouped, copy, raw, t0, t1):
-            copy(grouped[:].rearrange("p t m j -> p m j t"), raw[:].rearrange("p j (m t) -> p m j t", t=PACK)[:, :, :, t0:t1])
+            copy(grouped[:].rearrange("p t m j -> p m j t"), raw.rearrange("p j (m t) -> p m j t", t=PACK)[:, :, :, t0:t1])
             return grouped
 
         def quantise(name, grouped):
@@ -170,7 +176,7 @@ def tile_list_allele_mixture_scores_kernel(
 
         def add_av_pass(c, a):
             if a == 0:
-                banks["av", c] = new_bank(f"av{c}", OPENED + c % OPENED)
+                banks["av", c] = new_bank(f"av{c}", AV_BANKS[c])
             words, word_scales = picked_columns(a, c, 1)
             for t in range(PACK):
                 codes, scales = wa_q[a][t]
@@ -194,23 +200,31 @@ def tile_list_allele_mixture_scores_kernel(
         x_sb = {}
 
         def project(pair):
-            x_sb[pair] = placed(f"x{pair}", [P, 2, 2 * CH, 2], F32, at_x[pair])
+            room = stage[:, pair * x_words : (pair + 1) * x_words] if pair < 3 else placed("x3", [P, x_words], F32, at_root0 + 2 * N)[:]
+            x_sb[pair] = room.rearrange("p (u n e) -> p u n e", u=2, e=2)
             for u in range(2):
-                if pair > 0:
+                if pair > 1:
                     add_x_pass(pair, u, 0)
                 add_x_pass(pair, u, 1)
                 nc.scalar.copy(x_sb[pair][:, u, :, :], banks["x", pair, u].rearrange("p e n -> p n e"))
 
         h_w = held("h_w", [P, S], U32)
         h_s = held("h_s", [P, S], U8)
-        h_bf = held("h_bf", [P, S * PACK], BF16)
+        h_bf = {}
+        for piece in range(len(QUANTISE_CUTS) - 1):
+            c0, c1 = QUANTISE_CUTS[piece : piece + 2]
+            name, shape = f"h_bf{piece}", [P, (c1 - c0) * CH * PACK]
+            tile = placed(name, shape, BF16, at_page3) if piece == UNDER_LAST_PAGE else held(name, shape, BF16)
+            for c in range(c0, c1):
+                h_bf[c] = (tile, c0)
 
         def make_h(c):
             if c >= OPENED:
                 add_av_pass(c, 0)
             add_av_pass(c, 1)
+            tile, c0 = h_bf[c]
             nc.vector.tensor_tensor(
-                h_bf[:, c * CH * PACK : (c + 1) * CH * PACK].rearrange("p (n u e) -> p n u e", u=2, e=2),
+                tile[:, (c - c0) * CH * PACK : (c - c0 + 1) * CH * PACK].rearrange("p (n u e) -> p n u e", u=2, e=2),
                 banks["av", c][:].rearrange("p (u e) n -> p n u e", u=2),
                 x_sb[c // 2][:, :, c % 2 * CH : (c % 2 + 1) * CH, :].rearrange("p u n e -> p n u e"),
                 MULT,
@@ -219,7 +233,7 @@ def tile_list_allele_mixture_scores_kernel(
         def quantise_h(piece):
             c0, c1 = QUANTISE_CUTS[piece : piece + 2]
             nc.vector.quantize_mx(
-                h_w[:, c0 * CH : c1 * CH].bitcast(FP8X4), h_s[:, c0 * CH : c1 * CH], h_bf[:, c0 * CH * PACK : c1 * CH * PACK]
+                h_w[:, c0 * CH : c1 * CH].bitcast(FP8X4), h_s[:, c0 * CH : c1 * CH], h_bf[c0][0][:]
             )
 
         b_sb = held("b_sb", [P, PACK, S], F32)
@@ -231,7 +245,7 @@ def tile_list_allele_mixture_scores_kernel(
 
         def multiply_d(c):
             hw, hs = h_of(c)
-            banks["d", c] = new_bank(f"d{c}", D_BANK)[:].rearrange("p i m -> p (i m)")
+            banks["d", c] = new_bank(f"d{c}", D_BANKS[min(c, 1)])[:].rearrange("p i m -> p (i m)")
             for u in range(2):
                 nc.tensor.matmul_mx(
                     banks["d", c][:, u * HALF : (u + 1) * HALF], lhsT=hw, lhsT_scale=hs,
@@ -240,11 +254,13 @@ def tile_list_allele_mixture_scores_kernel(
                 )
 
         def square_d(c):
-            squares[c] = held(f"square{c}", [P, PACK, P], F32)
+            name, shape = f"square{c}", [P, PACK, P]
+            squares[c] = placed(name, shape, F32, at_root0 - 2 * N) if c == 1 else held(name, shape, F32)
             nc.scalar.activation(squares[c][:], banks["d", c].rearrange("p (m i) -> p i m", i=PACK), ACT.Square)
 
         def take_roots(c):
-            roots[c] = held(f"root{c}", [P, PACK, P], F32)
+            name, shape = f"root{c}", [P, PACK, P]
+            roots[c] = placed(name, shape, F32, at_root0) if c == 0 else held(name, shape, F32)
             for g in range(GROUPS):
                 factor = winv[:, g * CHUNKS + c : g * CHUNKS + c + 1]
                 nc.scalar.activation(
@@ -254,7 +270,7 @@ def tile_list_allele_mixture_scores_kernel(
 
         def multiply_b(c):
             hw, hs = h_of(c)
-            banks["b", c] = new_bank(f"b{c}", B_BANKS[min(c, 2)])
+            banks["b", c] = new_bank(f"b{c}", B_BANK)
             for i in range(PACK):
                 nc.tensor.matmul_mx(
                     banks["b", c][:, i, :], lhsT=wb_q[i][0], lhsT_scale=wb_q[i][1], rhs=hw, rhs_scale=hs, start=True, stop=True
@@ -264,7 +280,7 @@ def tile_list_allele_mixture_scores_kernel(
             nc.scalar.copy(b_sb[:, :, c * CH : (c + 1) * CH], banks["b", c][:])
 
         def turn_roots(c):
-            banks["r", c] = new_bank(f"r{c}", R_BANK)
+            banks["r", c] = new_bank(f"r{c}", R_BANKS[min(c, 1)])
             for i in range(PACK):
                 nc.tensor.transpose(banks["r", c][:, i, :], roots[c][:, i, :], ident[:])
 
@@ -298,45 +314,44 @@ def tile_list_allele_mixture_scores_kernel(
         gather_words(0, 0)
         wa_q = [quantise("wa_q0", wa_g0)]
         gather_words(0, 1)
-        for u in range(2):
-            add_x_pass(0, u, 0)
+        for pair in range(2):
+            for u in range(2):
+                add_x_pass(pair, u, 0)
+            for c in range(2 * pair, 2 * pair + 2):
+                add_av_pass(c, 0)
         gather_words(1, 0)
         gather_words(1, 1)
         gather_words(1, 2)
-        pages.append(placed("page3", [P, T2], F32, at_page3))
-        nc.vector.memset(pages[3][:].bitcast(I32), 0)
-        project(0)
-        for c in range(2):
-            add_av_pass(c, 0)
         wa_low = regroup(held("wa_low", [P, 2, P, PACK], BF16), nc.vector.tensor_copy, wa_raw1, 0, 2)
         wa_high = regroup(placed("wa_high", [P, 2, P, PACK], BF16, at_wa_g0), nc.scalar.copy, wa_raw1, 2, PACK)
+        project(0)
         project(1)
-        for c in range(2, OPENED):
-            add_av_pass(c, 0)
         wa_q.append(quantise("wa_q1a", wa_low) + quantise("wa_q1b", wa_high))
         gather_words(1, 3, at_wa_g0)
-        wb_high = regroup(held("wb_high", [P, 2, P, PACK], BF16), nc.scalar.copy, wb_raw, 2, PACK)
         make_h(0)
         make_h(1)
+        project(2)
         quantise_h(0)
         multiply_d(0)
+        wb_high = regroup(held("wb_high", [P, 2, P, PACK], BF16), nc.scalar.copy, wb_raw, 2, PACK)
         wb_low = regroup(held("wb_low", [P, 2, P, PACK], BF16), nc.vector.tensor_copy, wb_raw, 0, 2)
         make_h(2)
         quantise_h(1)
+        multiply_d(1)
         make_h(3)
         wb_q = quantise("wb_qa", wb_low) + quantise("wb_qb", wb_high)
         square_d(0)
         take_roots(0)
-        multiply_d(1)
-        project(2)
         quantise_h(2)
         multiply_b(0)
         make_h(4)
         make_h(5)
-        quantise_h(3)
         turn_roots(0)
         copy_b(0)
         square_roots(0)
+        quantise_h(3)
+        pages.append(placed("page3", [P, T2], F32, at_page3))
+        nc.gpsimd.memset(pages[3][:].bitcast(I32), 0)
         square_d(1)
         multiply_d(2)
         multiply_b(1)

@@ -32,7 +32,7 @@ ROW = S + H + HALF
 QUANTISE_CUTS = (0, 1, 2, 4, 6, 8)
 UNDER_LAST_PAGE = 3
 QUADRANTS = (0, 2, 1, 3)
-LAST_FROM = (7, 6, 5, 5)
+LAST_FROM = (5, 5, 5, 5)
 X_BANKS = (0, 2, 4, 2)
 AV_BANKS = (4, 5, 6, 7, 0, 1, 6, 7)
 D_BANKS, R_BANKS = (2, 5), (3, 0)

@@ -351,7 +351,7 @@ def tile_list_allele_mixture_scores_kernel(
         square_roots(0)
         quantise_h(3)
         pages.append(placed("page3", [P, T2], F32, at_page3))
-        nc.gpsimd.memset(pages[3][:].bitcast(I32), 0)
+        nc.vector.memset(pages[3][:].bitcast(I32), 0)
         square_d(1)
         multiply_d(2)
         multiply_b(1)

@@ -30,13 +30,14 @@ GATHER_CUTS = ((0, 2, 8), (0, 2, 4, 6, 8))
 HALF = N // 2
 ROW = S + H + HALF
 QUANTISE_CUTS = (0, 1, 2, 4, 6, 8)
-UNDER_LAST_PAGE = 3
+DEEP_FROM = 2
+UNDER_LAST_PAGE = 2
 QUADRANTS = (0, 2, 1, 3)
 LAST_FROM = (5, 5, 5, 5)
-X_BANKS = (0, 2, 4, 2)
-AV_BANKS = (4, 5, 6, 7, 0, 1, 6, 7)
-D_BANKS, R_BANKS = (2, 5), (3, 0)
-B_BANK, W_BANK = 4, 7
+X_BANKS = ((0, 1), (2, 3), (4, 5), (4, 3))
+AV_BANKS = (4, 5, 6, 7, 0, 2, 4, 3)
+D_BANKS, R_BANKS, B_BANKS = (2, 6), (3, 0), (4, 5)
+W_BANK = 7
 
 
 def tile_list_allele_mixture_scores_kernel(
@@ -147,7 +148,7 @@ def tile_list_allele_mixture_scores_kernel(
         ]
 
         def regroup(grouped, copy, raw, t0, t1):
-            copy(grouped[:].rearrange("p t m j -> p m j t"), raw.rearrange("p j (m t) -> p m j t", t=PACK)[:, :, :, t0:t1])
+            copy(grouped[:, :, :, :].rearrange("p t m j -> p m j t"), raw.rearrange("p j (m t) -> p m j t", t=PACK)[:, :, :, t0:t1])
             return grouped
 
         def quantise(name, grouped):
@@ -187,7 +188,7 @@ def tile_list_allele_mixture_scores_kernel(
 
         def add_x_pass(pair, u, a):
             if a == 0:
-                bank = new_bank(f"x{pair}_{u}", X_BANKS[pair] + u)
+                bank = new_bank(f"x{pair}_{u}", X_BANKS[pair][u])
                 banks["x", pair, u] = bank[:].rearrange("p (e h) n -> p e (h n)", e=2)
             words, word_scales = picked_columns(a, 2 * pair, 2)
             for e in range(2):
@@ -199,10 +200,10 @@ def tile_list_allele_mixture_scores_kernel(
 
         x_sb = {}
 
-        def project(pair):
+        def project(pair, halves=(0, 1)):
             room = stage[:, pair * x_words : (pair + 1) * x_words] if pair < 3 else placed("x3", [P, x_words], F32, at_root0 + 2 * N)[:]
             x_sb[pair] = room.rearrange("p (u n e) -> p u n e", u=2, e=2)
-            for u in range(2):
+            for u in halves:
                 if pair > 1:
                     add_x_pass(pair, u, 0)
                 add_x_pass(pair, u, 1)
@@ -255,8 +256,11 @@ def tile_list_allele_mixture_scores_kernel(
 
         def square_d(c):
             name, shape = f"square{c}", [P, PACK, P]
-            squares[c] = placed(name, shape, F32, at_root0 - 2 * N) if c == 1 else held(name, shape, F32)
-            nc.scalar.activation(squares[c][:], banks["d", c].rearrange("p (m i) -> p i m", i=PACK), ACT.Square)
+            if c == 0:
+                squares[c] = stage[:, 3 * x_words - N :].rearrange("p (i m) -> p i m", i=PACK)
+            else:
+                squares[c] = (placed(name, shape, F32, at_root0 - 2 * N) if c == 1 else held(name, shape, F32))[:]
+            nc.scalar.activation(squares[c], banks["d", c].rearrange("p (m i) -> p i m", i=PACK), ACT.Square)
 
         def take_roots(c):
             name, shape = f"root{c}", [P, PACK, P]
@@ -270,7 +274,7 @@ def tile_list_allele_mixture_scores_kernel(
 
         def multiply_b(c):
             hw, hs = h_of(c)
-            banks["b", c] = new_bank(f"b{c}", B_BANK)
+            banks["b", c] = new_bank(f"b{c}", B_BANKS[min(c, 1)])
             for i in range(PACK):
                 nc.tensor.matmul_mx(
                     banks["b", c][:, i, :], lhsT=wb_q[i][0], lhsT_scale=wb_q[i][1], rhs=hw, rhs_scale=hs, start=True, stop=True
@@ -300,10 +304,13 @@ def tile_list_allele_mixture_scores_kernel(
             if c + 2 < CHUNKS:
                 multiply_d(c + 2)
             copy_b(c)
-            square_roots(c)
+            if c < DEEP_FROM:
+                square_roots(c)
             if c + 1 < CHUNKS:
                 multiply_b(c + 1)
                 take_roots(c + 1)
+            if c >= DEEP_FROM:
+                square_roots(c)
 
         def scatter(c):
             for i in range(PACK):
@@ -330,19 +337,22 @@ def tile_list_allele_mixture_scores_kernel(
         gather_words(1, 3, at_wa_g0)
         make_h(0)
         make_h(1)
-        project(2)
         quantise_h(0)
         multiply_d(0)
         wb_high = regroup(held("wb_high", [P, 2, P, PACK], BF16), nc.scalar.copy, wb_raw, 2, PACK)
+        project(2, (0,))
         wb_low = regroup(held("wb_low", [P, 2, P, PACK], BF16), nc.vector.tensor_copy, wb_raw, 0, 2)
         make_h(2)
+        wb_q = quantise("wb_qa", wb_low) + quantise("wb_qb", wb_high)
         quantise_h(1)
         multiply_d(1)
         make_h(3)
-        wb_q = quantise("wb_qa", wb_low) + quantise("wb_qb", wb_high)
         square_d(0)
         take_roots(0)
+        project(2, (1,))
         quantise_h(2)
+        pages.append(placed("page3", [P, T2], F32, at_page3))
+        nc.vector.memset(pages[3][:].bitcast(I32), 0)
         multiply_b(0)
         make_h(4)
         make_h(5)
@@ -350,8 +360,6 @@ def tile_list_allele_mixture_scores_kernel(
         copy_b(0)
         square_roots(0)
         quantise_h(3)
-        pages.append(placed("page3", [P, T2], F32, at_page3))
-        nc.vector.memset(pages[3][:].bitcast(I32), 0)
         square_d(1)
         multiply_d(2)
         multiply_b(1)

@@ -29,15 +29,14 @@ FACTORS = GROUPS * CHUNKS
 GATHER_CUTS = ((0, 2, 8), (0, 2, 4, 6, 8))
 HALF = N // 2
 ROW = S + H + HALF
-QUANTISE_CUTS = (0, 1, 2, 4, 6, 8)
+QUANTISE_CUTS = (0, 1, 4, 6, 8)
 DEEP_FROM = 2
-UNDER_LAST_PAGE = 2
 QUADRANTS = (0, 2, 1, 3)
 LAST_FROM = (5, 5, 5, 5)
 X_BANKS = ((0, 1), (2, 3), (4, 5), (4, 3))
 AV_BANKS = (4, 5, 6, 7, 0, 2, 4, 3)
 D_BANKS, R_BANKS, B_BANKS = (2, 6), (3, 0), (4, 5)
-W_BANK = 7
+EARLY_R_BANK, W_BANK = 1, 7
 
 
 def tile_list_allele_mixture_scores_kernel(
@@ -109,14 +108,15 @@ def tile_list_allele_mixture_scores_kernel(
 
         pages.append(held("page1", [P, T2], F32))
         nc.vector.memset(pages[1][:].bitcast(I32), 0)
-        picked_s = placed("picked_s", [P, S], U8, at_page2)
+        picked_s = placed("picked_s", [P, S], U8, at_page3 - S // 2)
         nc.vector.tensor_copy(picked_s[:], tab_s[:].indirect(picks[:]))
         nc.vector.tensor_copy(
             rows_s[:, S : S + H].rearrange("p (t m) -> p t m", t=PACK), w4_s_raw[:].rearrange("p (m t) -> p t m", t=PACK)
         )
         nc.vector.tensor_copy(rows_s[:, 0:S].bitcast(I32), picked_s[:].bitcast(I32))
-        pages.append(placed("page2", [P, T2], F32, at_page2))
-        nc.vector.memset(pages[2][:].bitcast(I32), 0)
+        for i, at in ((2, at_page2), (3, at_page3)):
+            pages.append(placed(f"page{i}", [P, T2], F32, at))
+            nc.vector.memset(pages[i][:].bitcast(I32), 0)
 
         winv = held("winv", [P, FACTORS], F32)
         wroot = held("wroot", [P, FACTORS], F32)
@@ -134,7 +134,7 @@ def tile_list_allele_mixture_scores_kernel(
         for d in QUADRANTS:
             nc.sync.dma_start(planes[32 * d : 32 * d + 4, :].bitcast(I32), rows_s[32 * d : 32 * d + 32 : 4, :].bitcast(I32))
         nc.sync.dma_start(tab_w[1][:, T // 2 :].bitcast(I32), late_words[:, T // 2 :])
-        stage = held("stage", [P, 3 * x_words], F32)
+        stage = held("stage", [P, 3 * x_words + HALF], F32)
         wa_raw1 = load_rows(stage[:, : PACK * H].rearrange("p (j c) -> p j c", j=PACK), wa[512:1024, :])
         w8_w = load_words("w8_w", w8_words[0])
         wb_raw = load_rows(placed("wb_raw", [P, PACK, N], F32, at_wb_raw)[:], wb)
@@ -202,12 +202,12 @@ def tile_list_allele_mixture_scores_kernel(
 
         def project(pair, halves=(0, 1)):
             room = stage[:, pair * x_words : (pair + 1) * x_words] if pair < 3 else placed("x3", [P, x_words], F32, at_root0 + 2 * N)[:]
-            x_sb[pair] = room.rearrange("p (u n e) -> p u n e", u=2, e=2)
+            x_sb[pair] = room.rearrange("p (u n e f) -> p u n e f", u=2, e=2, f=2)
             for u in halves:
                 if pair > 1:
                     add_x_pass(pair, u, 0)
                 add_x_pass(pair, u, 1)
-                nc.scalar.copy(x_sb[pair][:, u, :, :], banks["x", pair, u].rearrange("p e n -> p n e"))
+                nc.scalar.copy(x_sb[pair][:, u, :, :, :], banks["x", pair, u].rearrange("p e (n f) -> p n e f", f=2))
 
         h_w = held("h_w", [P, S], U32)
         h_s = held("h_s", [P, S], U8)
@@ -215,7 +215,7 @@ def tile_list_allele_mixture_scores_kernel(
         for piece in range(len(QUANTISE_CUTS) - 1):
             c0, c1 = QUANTISE_CUTS[piece : piece + 2]
             name, shape = f"h_bf{piece}", [P, (c1 - c0) * CH * PACK]
-            tile = placed(name, shape, BF16, at_page3) if piece == UNDER_LAST_PAGE else held(name, shape, BF16)
+            tile = held(name, shape, BF16)
             for c in range(c0, c1):
                 h_bf[c] = (tile, c0)
 
@@ -225,9 +225,9 @@ def tile_list_allele_mixture_scores_kernel(
             add_av_pass(c, 1)
             tile, c0 = h_bf[c]
             nc.vector.tensor_tensor(
-                tile[:, (c - c0) * CH * PACK : (c - c0 + 1) * CH * PACK].rearrange("p (n u e) -> p n u e", u=2, e=2),
-                banks["av", c][:].rearrange("p (u e) n -> p n u e", u=2),
-                x_sb[c // 2][:, :, c % 2 * CH : (c % 2 + 1) * CH, :].rearrange("p u n e -> p n u e"),
+                tile[:, (c - c0) * CH * PACK : (c - c0 + 1) * CH * PACK].rearrange("p (n f u e) -> p n u e f", f=2, u=2, e=2),
+                banks["av", c][:].rearrange("p (u e) (n f) -> p n u e f", u=2, f=2),
+                x_sb[c // 2][:, :, c % 2 * CH // 2 : (c % 2 + 1) * CH // 2, :, :].rearrange("p u n e f -> p n u e f"),
                 MULT,
             )
 
@@ -254,21 +254,24 @@ def tile_list_allele_mixture_scores_kernel(
                     start=True, stop=True,
                 )
 
-        def square_d(c):
+        def square_d(c, i0=0, i1=PACK):
             name, shape = f"square{c}", [P, PACK, P]
             if c == 0:
-                squares[c] = stage[:, 3 * x_words - N :].rearrange("p (i m) -> p i m", i=PACK)
+                squares[c] = stage[:, 3 * x_words - HALF :].rearrange("p (i m) -> p i m", i=PACK)
             else:
                 squares[c] = (placed(name, shape, F32, at_root0 - 2 * N) if c == 1 else held(name, shape, F32))[:]
-            nc.scalar.activation(squares[c], banks["d", c].rearrange("p (m i) -> p i m", i=PACK), ACT.Square)
+            nc.scalar.activation(
+                squares[c][:, i0:i1, :], banks["d", c].rearrange("p (m i) -> p i m", i=PACK)[:, i0:i1, :], ACT.Square
+            )
 
-        def take_roots(c):
+        def take_roots(c, i0=0, i1=PACK):
             name, shape = f"root{c}", [P, PACK, P]
-            roots[c] = placed(name, shape, F32, at_root0) if c == 0 else held(name, shape, F32)
+            if i0 == 0:
+                roots[c] = placed(name, shape, F32, at_root0) if c == 0 else held(name, shape, F32)
             for g in range(GROUPS):
                 factor = winv[:, g * CHUNKS + c : g * CHUNKS + c + 1]
                 nc.scalar.activation(
-                    roots[c][:, :, g * GP : (g + 1) * GP], squares[c][:, :, g * GP : (g + 1) * GP], ACT.Abs_reciprocal_sqrt,
+                    roots[c][:, i0:i1, g * GP : (g + 1) * GP], squares[c][:, i0:i1, g * GP : (g + 1) * GP], ACT.Abs_reciprocal_sqrt,
                     bias=factor, scale=factor,
                 )
 
@@ -280,16 +283,16 @@ def tile_list_allele_mixture_scores_kernel(
                     banks["b", c][:, i, :], lhsT=wb_q[i][0], lhsT_scale=wb_q[i][1], rhs=hw, rhs_scale=hs, start=True, stop=True
                 )
 
-        def copy_b(c):
-            nc.scalar.copy(b_sb[:, :, c * CH : (c + 1) * CH], banks["b", c][:])
+        def copy_b(c, i0=0, i1=PACK):
+            nc.scalar.copy(b_sb[:, i0:i1, c * CH : (c + 1) * CH], banks["b", c][:, i0:i1, :])
 
-        def turn_roots(c):
-            banks["r", c] = new_bank(f"r{c}", R_BANKS[min(c, 1)])
-            for i in range(PACK):
-                nc.tensor.transpose(banks["r", c][:, i, :], roots[c][:, i, :], ident[:])
+        def turn_roots(c, i0=0, i1=PACK):
+            banks["r", c, i0] = new_bank(f"r{c}_{i0}", R_BANKS[min(c, 1)] if i1 == PACK else EARLY_R_BANK)
+            for i in range(i0, i1):
+                nc.tensor.transpose(banks["r", c, i0][:, i, :], roots[c][:, i, :], ident[:])
 
-        def square_roots(c):
-            nc.scalar.activation(damp[:, :, c * CH : (c + 1) * CH], banks["r", c][:], ACT.Square)
+        def square_roots(c, i0=0, i1=PACK):
+            nc.scalar.activation(damp[:, i0:i1, c * CH : (c + 1) * CH], banks["r", c, i0][:, i0:i1, :], ACT.Square)
 
         def put(i, c0, c1):
             nc.vector.tensor_tensor(
@@ -344,34 +347,37 @@ def tile_list_allele_mixture_scores_kernel(
         wb_low = regroup(held("wb_low", [P, 2, P, PACK], BF16), nc.vector.tensor_copy, wb_raw, 0, 2)
         make_h(2)
         wb_q = quantise("wb_qa", wb_low) + quantise("wb_qb", wb_high)
-        quantise_h(1)
-        multiply_d(1)
         make_h(3)
-        square_d(0)
-        take_roots(0)
+        square_d(0, 0, 2)
+        square_d(0, 2, PACK)
+        take_roots(0, 0, 2)
+        turn_roots(0, 0, 2)
         project(2, (1,))
-        quantise_h(2)
-        pages.append(placed("page3", [P, T2], F32, at_page3))
-        nc.vector.memset(pages[3][:].bitcast(I32), 0)
         multiply_b(0)
         make_h(4)
+        quantise_h(1)
+        multiply_d(1)
         make_h(5)
-        turn_roots(0)
-        copy_b(0)
-        square_roots(0)
-        quantise_h(3)
+        copy_b(0, 0, 2)
+        square_roots(0, 0, 2)
+        take_roots(0, 2, PACK)
+        turn_roots(0, 2, PACK)
+        copy_b(0, 2, PACK)
+        square_roots(0, 2, PACK)
         square_d(1)
         multiply_d(2)
         multiply_b(1)
         take_roots(1)
         scatter(0)
+        quantise_h(2)
         project(3)
         make_h(6)
         make_h(7)
-        quantise_h(4)
         for c in range(1, CHUNKS):
             second_stage(c)
             scatter(c)
+            if c == 1:
+                quantise_h(3)
         for i in range(PACK):
             put(i, LAST_FROM[i], CHUNKS)
             nc.sync.dma_start(out.rearrange("(p i) t -> p i t", i=PACK)[:, i, :], pages[i][:])

@@ -31,8 +31,9 @@ HALF = N // 2
 ROW = S + H + HALF
 QUANTISE_CUTS = (0, 1, 4, 6, 8)
 DEEP_FROM = 2
+ONE_PORT_WORDS = 3 * T2 // 8 + 1
 QUADRANTS = (0, 2, 1, 3)
-LAST_FROM = (5, 5, 5, 5)
+LAST_FROM = (6, 6, 5, 4)
 X_BANKS = ((0, 1), (2, 3), (4, 5), (4, 3))
 AV_BANKS = (4, 5, 6, 7, 0, 2, 4, 3)
 D_BANKS, R_BANKS, B_BANKS = (2, 6), (3, 0), (4, 5)
@@ -76,10 +77,11 @@ def tile_list_allele_mixture_scores_kernel(
         pages = [held("page0", [P, T2], F32)]
 
         nc.gpsimd.memset(tab_s[:].bitcast(I32), 0)
-        nc.gpsimd.memset(w4_s_raw[:].bitcast(I32), 0)
-        nc.gpsimd.memset(wgo_rows[:], 0.0)
-        make_identity(nc, ident[:])
-        for lo, hi in ((0, T2 // 2 + 1), (T2 // 2 + 1, T2 // 2 + 2), (T2 // 2 + 2, T2)):
+        nc.vector.memset(ident[:], 0.0)
+        make_identity(nc, ident[:], nomemset=True)
+        nc.vector.memset(w4_s_raw[:].bitcast(I32), 0)
+        nc.vector.memset(wgo_rows[:], 0.0)
+        for lo, hi in ((0, ONE_PORT_WORDS), (ONE_PORT_WORDS, ONE_PORT_WORDS + 1), (ONE_PORT_WORDS + 1, T2)):
             nc.vector.memset(pages[0][:, lo:hi].bitcast(I32), 0)
 
         def load_rows(tile, rows):

@@ -26,14 +26,14 @@ GROUPS = 8
 GP = P // GROUPS
 OPENED = 4
 FACTORS = GROUPS * CHUNKS
-GATHER_CUTS = ((0, 2, 8), (0, 2, 4, 6, 8))
+GATHER_CUTS = ((0, 2, 8), (0, 4, 8))
 HALF = N // 2
 ROW = S + H + HALF
 QUANTISE_CUTS = (0, 1, 4, 6, 8)
 DEEP_FROM = 2
 ONE_PORT_WORDS = 3 * T2 // 8 + 1
 QUADRANTS = (0, 2, 1, 3)
-LAST_FROM = (6, 6, 5, 4)
+PUT_CUTS = ((0, 1, 2, 3, 4, 6, 8), (0, 1, 2, 3, 5, 6, 8), (0, 1, 2, 3, 5, 8), (0, 1, 2, 3, 4, 8))
 X_BANKS = ((0, 1), (2, 3), (4, 5), (4, 3))
 AV_BANKS = (4, 5, 6, 7, 0, 2, 4, 3)
 D_BANKS, R_BANKS, B_BANKS = (2, 6), (3, 0), (4, 5)
@@ -304,23 +304,23 @@ def tile_list_allele_mixture_scores_kernel(
 
         def second_stage(c):
             turn_roots(c)
-            if c + 1 < CHUNKS:
-                square_d(c + 1)
+            square_d(c + 1)
             if c + 2 < CHUNKS:
                 multiply_d(c + 2)
             copy_b(c)
             if c < DEEP_FROM:
                 square_roots(c)
-            if c + 1 < CHUNKS:
-                multiply_b(c + 1)
-                take_roots(c + 1)
+            multiply_b(c + 1)
+            take_roots(c + 1)
             if c >= DEEP_FROM:
                 square_roots(c)
 
         def scatter(c):
-            for i in range(PACK):
-                if c < LAST_FROM[i]:
-                    put(i, c, c + 1)
+            for i, cuts in enumerate(PUT_CUTS):
+                if c + 1 in cuts:
+                    put(i, cuts[cuts.index(c + 1) - 1], c + 1)
+                if c + 1 == CHUNKS:
+                    nc.sync.dma_start(out.rearrange("(p i) t -> p i t", i=PACK)[:, i, :], pages[i][:])
 
         wa_g0 = regroup(placed("wa_g0", [P, PACK, P, PACK], BF16, at_wa_g0), nc.scalar.copy, wa_raw0, 0, PACK)
         gather_words(0, 0)
@@ -332,14 +332,12 @@ def tile_list_allele_mixture_scores_kernel(
             for c in range(2 * pair, 2 * pair + 2):
                 add_av_pass(c, 0)
         gather_words(1, 0)
-        gather_words(1, 1)
-        gather_words(1, 2)
         wa_low = regroup(held("wa_low", [P, 2, P, PACK], BF16), nc.vector.tensor_copy, wa_raw1, 0, 2)
         wa_high = regroup(placed("wa_high", [P, 2, P, PACK], BF16, at_wa_g0), nc.scalar.copy, wa_raw1, 2, PACK)
         project(0)
         project(1)
         wa_q.append(quantise("wa_q1a", wa_low) + quantise("wa_q1b", wa_high))
-        gather_words(1, 3, at_wa_g0)
+        gather_words(1, 1, at_wa_g0)
         make_h(0)
         make_h(1)
         quantise_h(0)
@@ -375,11 +373,13 @@ def tile_list_allele_mixture_scores_kernel(
         project(3)
         make_h(6)
         make_h(7)
-        for c in range(1, CHUNKS):
+        for c in range(1, CHUNKS - 1):
             second_stage(c)
             scatter(c)
             if c == 1:
                 quantise_h(3)
-        for i in range(PACK):
-            put(i, LAST_FROM[i], CHUNKS)
-            nc.sync.dma_start(out.rearrange("(p i) t -> p i t", i=PACK)[:, i, :], pages[i][:])
+        for i in range(0, PACK, 2):
+            turn_roots(CHUNKS - 1, i, i + 2)
+            copy_b(CHUNKS - 1, i, i + 2)
+            square_roots(CHUNKS - 1, i, i + 2)
+        scatter(CHUNKS - 1)

@@ -26,14 +26,14 @@ GROUPS = 8
 GP = P // GROUPS
 OPENED = 4
 FACTORS = GROUPS * CHUNKS
-GATHER_CUTS = ((0, 2, 8), (0, 4, 8))
+GATHER_CUTS = ((0, 2, 8), (0, 2, 4, 6, 8))
 HALF = N // 2
 ROW = S + H + HALF
 QUANTISE_CUTS = (0, 1, 4, 6, 8)
 DEEP_FROM = 2
 ONE_PORT_WORDS = 3 * T2 // 8 + 1
 QUADRANTS = (0, 2, 1, 3)
-PUT_CUTS = ((0, 1, 2, 3, 4, 6, 8), (0, 1, 2, 3, 5, 6, 8), (0, 1, 2, 3, 5, 8), (0, 1, 2, 3, 4, 8))
+LAST_FROM = (6, 6, 5, 4)
 X_BANKS = ((0, 1), (2, 3), (4, 5), (4, 3))
 AV_BANKS = (4, 5, 6, 7, 0, 2, 4, 3)
 D_BANKS, R_BANKS, B_BANKS = (2, 6), (3, 0), (4, 5)
@@ -295,32 +295,31 @@ def tile_list_allele_mixture_scores_kernel(
 
         def square_roots(c, i0=0, i1=PACK):
             nc.scalar.activation(damp[:, i0:i1, c * CH : (c + 1) * CH], banks["r", c, i0][:, i0:i1, :], ACT.Square)
+            scores = damp[:, i0:i1, c * CH : (c + 1) * CH]
+            nc.gpsimd.tensor_tensor(scores, scores, b_sb[:, i0:i1, c * CH : (c + 1) * CH], MULT)
 
         def put(i, c0, c1):
-            nc.vector.tensor_tensor(
-                pages[i][:].indirect(bins[:, c0 * CH // 16 : c1 * CH // 16]),
-                b_sb[:, i, c0 * CH : c1 * CH], damp[:, i, c0 * CH : c1 * CH], MULT,
-            )
+            nc.vector.tensor_copy(pages[i][:].indirect(bins[:, c0 * CH // 16 : c1 * CH // 16]), damp[:, i, c0 * CH : c1 * CH])
 
         def second_stage(c):
             turn_roots(c)
-            square_d(c + 1)
+            if c + 1 < CHUNKS:
+                square_d(c + 1)
             if c + 2 < CHUNKS:
                 multiply_d(c + 2)
             copy_b(c)
             if c < DEEP_FROM:
                 square_roots(c)
-            multiply_b(c + 1)
-            take_roots(c + 1)
+            if c + 1 < CHUNKS:
+                multiply_b(c + 1)
+                take_roots(c + 1)
             if c >= DEEP_FROM:
                 square_roots(c)
 
         def scatter(c):
-            for i, cuts in enumerate(PUT_CUTS):
-                if c + 1 in cuts:
-                    put(i, cuts[cuts.index(c + 1) - 1], c + 1)
-                if c + 1 == CHUNKS:
-                    nc.sync.dma_start(out.rearrange("(p i) t -> p i t", i=PACK)[:, i, :], pages[i][:])
+            for i in range(PACK):
+                if c < LAST_FROM[i]:
+                    put(i, c, c + 1)
 
         wa_g0 = regroup(placed("wa_g0", [P, PACK, P, PACK], BF16, at_wa_g0), nc.scalar.copy, wa_raw0, 0, PACK)
         gather_words(0, 0)
@@ -332,12 +331,14 @@ def tile_list_allele_mixture_scores_kernel(
             for c in range(2 * pair, 2 * pair + 2):
                 add_av_pass(c, 0)
         gather_words(1, 0)
+        gather_words(1, 1)
+        gather_words(1, 2)
         wa_low = regroup(held("wa_low", [P, 2, P, PACK], BF16), nc.vector.tensor_copy, wa_raw1, 0, 2)
         wa_high = regroup(placed("wa_high", [P, 2, P, PACK], BF16, at_wa_g0), nc.scalar.copy, wa_raw1, 2, PACK)
         project(0)
         project(1)
         wa_q.append(quantise("wa_q1a", wa_low) + quantise("wa_q1b", wa_high))
-        gather_words(1, 1, at_wa_g0)
+        gather_words(1, 3, at_wa_g0)
         make_h(0)
         make_h(1)
         quantise_h(0)
@@ -373,13 +374,11 @@ def tile_list_allele_mixture_scores_kernel(
         project(3)
         make_h(6)
         make_h(7)
-        for c in range(1, CHUNKS - 1):
+        for c in range(1, CHUNKS):
             second_stage(c)
             scatter(c)
             if c == 1:
                 quantise_h(3)
-        for i in range(0, PACK, 2):
-            turn_roots(CHUNKS - 1, i, i + 2)
-            copy_b(CHUNKS - 1, i, i + 2)
-            square_roots(CHUNKS - 1, i, i + 2)
-        scatter(CHUNKS - 1)
+        for i in range(PACK):
+            put(i, LAST_FROM[i], CHUNKS)
+            nc.sync.dma_start(out.rearrange("(p i) t -> p i t", i=PACK)[:, i, :], pages[i][:])

@@ -24,20 +24,20 @@ CH = 128
 CHUNKS = S // CH
 GROUPS = 8
 GP = P // GROUPS
-OPENED = 4
 FACTORS = GROUPS * CHUNKS
-GATHER_CUTS = ((0, 2, 8), (0, 2, 4, 6, 8))
+GATHERS = ((0, 0, 4), (0, 4, 8), (1, 0, 2), (1, 2, 4), (1, 4, 8))
+OPENED = 2
+SHARED = 96
 HALF = N // 2
-ROW = S + H + HALF
+FIRST = S // 2
+ROW = FIRST + H + HALF
 QUANTISE_CUTS = (0, 1, 4, 6, 8)
-DEEP_FROM = 2
-ONE_PORT_WORDS = 3 * T2 // 8 + 1
 QUADRANTS = (0, 2, 1, 3)
-LAST_FROM = (6, 6, 5, 4)
-X_BANKS = ((0, 1), (2, 3), (4, 5), (4, 3))
-AV_BANKS = (4, 5, 6, 7, 0, 2, 4, 3)
-D_BANKS, R_BANKS, B_BANKS = (2, 6), (3, 0), (4, 5)
-EARLY_R_BANK, W_BANK = 1, 7
+LAST_FROM = (7, 6, 5, 4)
+X_BANKS = (0, 1, 2, 3, 4, 5, 2, 4)
+AV_BANKS = (0, 1, 4, 5, 0, 1, 0, 1)
+D_BANKS, TURN_BANKS = (6, 7), (3, 2)
+W_BANK, EARLY_B_BANKS = 7, (6, 4)
 
 
 def tile_list_allele_mixture_scores_kernel(
@@ -59,30 +59,33 @@ def tile_list_allele_mixture_scores_kernel(
             return psum.tile([P, PACK, CH], F32, name=name, tag=f"bank{bank}")
 
         at_tab_s = 0
-        at_w4_raw = at_tab_s + T
-        at_page2 = at_w4_raw + PASSES * 2 * H
-        at_page3 = at_page2 + 4 * T2
-        at_wa_g0 = at_page3 + 4 * T2
-        at_wb_raw = at_wa_g0 + 2 * PACK * H
-        at_root0 = at_wb_raw + 4 * PACK * N + 2 * N
-        x_words = 2 * CH * PACK
+        at_page3 = at_tab_s + T - 64
+        at_planes = at_page3 + 4 * T2
+        at_late_s = at_planes + PASSES * ROW
+        at_picked_s = at_late_s + S - FIRST - 64
+        at_page2 = at_picked_s + FIRST - 64
+        chunk_words = CH * PACK
 
         picks = keep.tile([P, S // 16], U16, name="picks")
         bins = keep.tile([P, S // 16], U16, name="bins")
         tab_s = placed("tab_s", [P, T], U8, at_tab_s)
-        w4_s_raw = held("w4_s_raw", [P, H], U8)
+        w4_s_raw = placed("w4_s_raw", [P, H], U8, at_planes + PASSES * 2 * H)
+        picked_s = placed("picked_s", [P, FIRST], U8, at_picked_s)
         rows_s = held("rows_s", [P, ROW], U8)
+        late_planes = placed("late_planes", [P, PASSES * (S - FIRST)], U8, at_tab_s)
         wgo_rows = held("wgo_rows", [P, CH], F32)
         ident = held("ident", [P, P], F32)
         pages = [held("page0", [P, T2], F32)]
 
         nc.gpsimd.memset(tab_s[:].bitcast(I32), 0)
-        nc.vector.memset(ident[:], 0.0)
+        for words in (w4_s_raw[:].bitcast(I32), wgo_rows[:].bitcast(I32), pages[0][:].bitcast(I32)):
+            last = words.shape[1] - 1
+            nc.vector.memset(words[:, :last], 0)
+            nc.vector.memset(words[:, last:], 0)
+        nc.gpsimd.memset(ident[:], 0.0)
         make_identity(nc, ident[:], nomemset=True)
-        nc.vector.memset(w4_s_raw[:].bitcast(I32), 0)
-        nc.vector.memset(wgo_rows[:], 0.0)
-        for lo, hi in ((0, ONE_PORT_WORDS), (ONE_PORT_WORDS, ONE_PORT_WORDS + 1), (ONE_PORT_WORDS + 1, T2)):
-            nc.vector.memset(pages[0][:, lo:hi].bitcast(I32), 0)
+        pages.append(held("page1", [P, T2], F32))
+        nc.gpsimd.memset(pages[1][:].bitcast(I32), 0)
 
         def load_rows(tile, rows):
             nc.sync.dma_start(tile, rows.rearrange("(p j) c -> p j c", j=PACK))
@@ -94,31 +97,30 @@ def tile_list_allele_mixture_scores_kernel(
             return tile
 
         nc.sync.dma_start(picks[:], offs)
-        w4_raw = placed("w4_raw", [P, PASSES * 2 * H], U8, at_w4_raw)
+        w4_raw = placed("w4_raw", [P, PASSES * 2 * H], U8, at_planes)
         nc.sync.dma_start(
             w4_raw[:].bitcast(I32).rearrange("p (a c) -> p a c", a=PASSES),
             w4_words.bitcast(I32).rearrange("a p c -> p a c"),
         )
-        nc.sync.dma_start(rows_s[0:P:4, S + H : ROW].bitcast(I32), w8_scales[0].bitcast(I32))
+        nc.sync.dma_start(rows_s[0:P:4, FIRST + H : ROW].bitcast(I32), w8_scales[0].bitcast(I32))
         nc.sync.dma_start(tab_s[0:P:4, :].bitcast(I32), tab_scales.bitcast(I32).rearrange("a q t -> q a t"))
         nc.sync.dma_start(w4_s_raw[0:P:4, :].bitcast(I32), w4_scales.bitcast(I32).rearrange("a q c -> q a c"))
-        wa_raw0 = load_rows(held("wa_raw0", [P, PACK, H], F32)[:], wa[0:512, :])
+        tab_w = [held(f"tab_w{a}", [P, T], U32) for a in range(PASSES)]
+        table = [tab_words[a].rearrange("p t i -> p (t i)").bitcast(I32) for a in range(PASSES)]
+        nc.sync.dma_start(tab_w[0][:].bitcast(I32), table[0])
         nc.sync.dma_start(wgo_rows[0:FACTORS, :], wgo[0:P:GP, :])
-        tab_w = [load_words("tab_w0", tab_words[0]), held("tab_w1", [P, T], U32)]
-        late_words = tab_words[1].rearrange("p t i -> p (t i)").bitcast(I32)
-        nc.sync.dma_start(tab_w[1][:, : T // 2].bitcast(I32), late_words[:, : T // 2])
+        nc.sync.dma_start(tab_w[1][:].bitcast(I32), table[1])
 
-        pages.append(held("page1", [P, T2], F32))
-        nc.vector.memset(pages[1][:].bitcast(I32), 0)
-        picked_s = placed("picked_s", [P, S], U8, at_page3 - S // 2)
-        nc.vector.tensor_copy(picked_s[:], tab_s[:].indirect(picks[:]))
+        nc.vector.tensor_copy(picked_s[:], tab_s[:].indirect(picks[:, : FIRST // 16]))
         nc.vector.tensor_copy(
-            rows_s[:, S : S + H].rearrange("p (t m) -> p t m", t=PACK), w4_s_raw[:].rearrange("p (m t) -> p t m", t=PACK)
+            rows_s[:, FIRST : FIRST + H].rearrange("p (t m) -> p t m", t=PACK), w4_s_raw[:].rearrange("p (m t) -> p t m", t=PACK)
         )
-        nc.vector.tensor_copy(rows_s[:, 0:S].bitcast(I32), picked_s[:].bitcast(I32))
+        nc.vector.tensor_copy(rows_s[:, 0:FIRST].bitcast(I32), picked_s[:].bitcast(I32))
+        late_s = placed("late_s", [P, S - FIRST], U8, at_late_s)
+        nc.vector.tensor_copy(late_s[:], tab_s[:].indirect(picks[:, FIRST // 16 :]))
         for i, at in ((2, at_page2), (3, at_page3)):
             pages.append(placed(f"page{i}", [P, T2], F32, at))
-            nc.vector.memset(pages[i][:].bitcast(I32), 0)
+            nc.gpsimd.memset(pages[i][:].bitcast(I32), 0)
 
         winv = held("winv", [P, FACTORS], F32)
         wroot = held("wroot", [P, FACTORS], F32)
@@ -132,102 +134,111 @@ def tile_list_allele_mixture_scores_kernel(
             w4_w[:].bitcast(U16).rearrange("p (a t m) -> p a t m", a=PASSES, t=PACK),
             w4_raw[:].bitcast(U16).rearrange("p (a m t) -> p a t m", a=PASSES, t=PACK),
         )
-        planes = placed("planes", [P, PASSES * ROW], U8, at_tab_s)
-        for d in QUADRANTS:
-            nc.sync.dma_start(planes[32 * d : 32 * d + 4, :].bitcast(I32), rows_s[32 * d : 32 * d + 32 : 4, :].bitcast(I32))
-        nc.sync.dma_start(tab_w[1][:, T // 2 :].bitcast(I32), late_words[:, T // 2 :])
-        stage = held("stage", [P, 3 * x_words + HALF], F32)
-        wa_raw1 = load_rows(stage[:, : PACK * H].rearrange("p (j c) -> p j c", j=PACK), wa[512:1024, :])
+
+        def move(target, rows):
+            for d in QUADRANTS:
+                nc.sync.dma_start(target[32 * d : 32 * d + 4, :].bitcast(I32), rows[32 * d : 32 * d + 32 : 4, :].bitcast(I32))
+
+        planes = placed("planes", [P, PASSES * ROW], U8, at_planes)
+        move(planes, rows_s)
+        wa_raw0 = load_rows(held("wa_raw0", [P, PACK, H], F32)[:], wa[0:512, :])
+        move(late_planes, late_s)
+        stage = held("stage", [P, PACK * H], F32)
+        wa_raw1 = load_rows(stage[:].rearrange("p (j c) -> p j c", j=PACK), wa[512:1024, :])
+        wb_raw = load_rows(held("wb_raw", [P, PACK, N], F32)[:], wb)
         w8_w = load_words("w8_w", w8_words[0])
-        wb_raw = load_rows(placed("wb_raw", [P, PACK, N], F32, at_wb_raw)[:], wb)
         nc.sync.dma_start(bins[:], offs2)
         w4_q = [
             [
-                (w4_w[:, 2 * (a * H + col) : 2 * (a * H + col + P)].bitcast(FP4X4), planes[:, a * ROW + S + col : a * ROW + S + col + P])
+                (w4_w[:, 2 * (a * H + col) : 2 * (a * H + col + P)].bitcast(FP4X4), planes[:, a * ROW + FIRST + col : a * ROW + FIRST + col + P])
                 for col in range(0, H, P)
             ]
             for a in range(PASSES)
         ]
 
-        def regroup(grouped, copy, raw, t0, t1):
-            copy(grouped[:, :, :, :].rearrange("p t m j -> p m j t"), raw.rearrange("p j (m t) -> p m j t", t=PACK)[:, :, :, t0:t1])
+        def regroup(name, raw, t0, shares):
+            grouped = held(name, [P, 2, P, PACK], BF16)
+            for copy, m0, m1 in shares:
+                copy(
+                    grouped[:, :, m0:m1, :].rearrange("p t m j -> p m j t"),
+                    raw.rearrange("p j (m t) -> p m j t", t=PACK)[:, m0:m1, :, t0 : t0 + 2],
+                )
             return grouped
 
         def quantise(name, grouped):
-            slices = grouped.shape[1]
-            codes = held(name + "_w", [P, slices * P], U32)
-            scales = held(name + "_s", [P, slices * P], U8)
+            codes = held(name + "_w", [P, 2 * P], U32)
+            scales = held(name + "_s", [P, 2 * P], U8)
             nc.vector.quantize_mx(codes[:].bitcast(FP8X4), scales[:], grouped[:].rearrange("p t m j -> p (t m j)"))
-            return [(codes[:, t * P : (t + 1) * P].bitcast(FP8X4), scales[:, t * P : (t + 1) * P]) for t in range(slices)]
+            return [(codes[:, t * P : (t + 1) * P].bitcast(FP8X4), scales[:, t * P : (t + 1) * P]) for t in range(2)]
 
         v_w = {}
 
-        def gather_words(a, piece, at=None):
-            c0, c1 = GATHER_CUTS[a][piece : piece + 2]
-            name, shape = f"v_w{a}_{c0}", [P, (c1 - c0) * CH]
-            picked = held(name, shape, U32) if at is None else placed(name, shape, U32, at)
-            nc.vector.tensor_copy(picked[:], tab_w[a][:].indirect(picks[:, c0 * CH // 16 : c1 * CH // 16]))
-            for c in range(c0, c1):
-                v_w[a, c] = (picked, c0)
+        def gather_words():
+            for a, c0, c1 in GATHERS:
+                picked = held(f"v_w{a}_{c0}", [P, (c1 - c0) * CH], U32)
+                nc.vector.tensor_copy(picked[:], tab_w[a][:].indirect(picks[:, c0 * CH // 16 : c1 * CH // 16]))
+                for c in range(c0, c1):
+                    v_w[a, c] = (picked, c0)
 
         def picked_columns(a, c, count):
             picked, c0 = v_w[a, c]
             words = picked[:, (c - c0) * CH : (c - c0 + count) * CH]
-            return words.bitcast(FP8X4), planes[:, a * ROW + c * CH : a * ROW + (c + count) * CH]
+            if c * CH < FIRST:
+                return words.bitcast(FP8X4), planes[:, a * ROW + c * CH : a * ROW + (c + count) * CH]
+            at = a * (S - FIRST) + c * CH - FIRST
+            return words.bitcast(FP8X4), late_planes[:, at : at + count * CH]
 
         banks = {}
+
+        def add_pass(bank, weights, c, a):
+            words, word_scales = picked_columns(a, c, 1)
+            for t in range(PACK):
+                codes, scales = weights[a][t]
+                nc.tensor.matmul_mx(
+                    bank[:, t, :], lhsT=codes, lhsT_scale=scales, rhs=words, rhs_scale=word_scales,
+                    start=(a == 0 and t == 0), stop=(a == PASSES - 1 and t == PACK - 1),
+                )
 
         def add_av_pass(c, a):
             if a == 0:
                 banks["av", c] = new_bank(f"av{c}", AV_BANKS[c])
-            words, word_scales = picked_columns(a, c, 1)
-            for t in range(PACK):
-                codes, scales = wa_q[a][t]
-                nc.tensor.matmul_mx(
-                    banks["av", c][:, t, :], lhsT=codes, lhsT_scale=scales, rhs=words, rhs_scale=word_scales,
-                    start=(a == 0 and t == 0), stop=(a == PASSES - 1 and t == PACK - 1),
-                )
-
-        def add_x_pass(pair, u, a):
-            if a == 0:
-                bank = new_bank(f"x{pair}_{u}", X_BANKS[pair][u])
-                banks["x", pair, u] = bank[:].rearrange("p (e h) n -> p e (h n)", e=2)
-            words, word_scales = picked_columns(a, 2 * pair, 2)
-            for e in range(2):
-                codes, scales = w4_q[a][2 * u + e]
-                nc.tensor.matmul_mx(
-                    banks["x", pair, u][:, e, :], lhsT=codes, lhsT_scale=scales, rhs=words, rhs_scale=word_scales,
-                    start=(a == 0 and e == 0), stop=(a == PASSES - 1 and e == 1),
-                )
+            add_pass(banks["av", c], wa_q, c, a)
 
         x_sb = {}
 
-        def project(pair, halves=(0, 1)):
-            room = stage[:, pair * x_words : (pair + 1) * x_words] if pair < 3 else placed("x3", [P, x_words], F32, at_root0 + 2 * N)[:]
-            x_sb[pair] = room.rearrange("p (u n e f) -> p u n e f", u=2, e=2, f=2)
-            for u in halves:
-                if pair > 1:
-                    add_x_pass(pair, u, 0)
-                add_x_pass(pair, u, 1)
-                nc.scalar.copy(x_sb[pair][:, u, :, :, :], banks["x", pair, u].rearrange("p e (n f) -> p n e f", f=2))
+        def x_room(pair):
+            if pair < 2:
+                return held(f"x_pair{pair}", [P, 2 * chunk_words], F32)[:]
+            return stage[:, (pair - 2) * 2 * chunk_words : (pair - 1) * 2 * chunk_words]
+
+        def project_pair(pair):
+            x_sb[pair] = x_room(pair).rearrange("p (u n e f) -> p u n e f", u=2, e=2, f=2)
+            for u in range(2):
+                bank = new_bank(f"x{pair}_{u}", X_BANKS[2 * pair + u])[:].rearrange("p (e h) n -> p e (h n)", e=2)
+                for a in range(PASSES):
+                    words, word_scales = picked_columns(a, 2 * pair, 2)
+                    for e in range(2):
+                        codes, scales = w4_q[a][2 * u + e]
+                        nc.tensor.matmul_mx(
+                            bank[:, e, :], lhsT=codes, lhsT_scale=scales, rhs=words, rhs_scale=word_scales,
+                            start=(a == 0 and e == 0), stop=(a == PASSES - 1 and e == 1),
+                        )
+                nc.scalar.copy(x_sb[pair][:, u, :, :, :], bank.rearrange("p e (n f) -> p n e f", f=2))
 
         h_w = held("h_w", [P, S], U32)
         h_s = held("h_s", [P, S], U8)
         h_bf = {}
-        for piece in range(len(QUANTISE_CUTS) - 1):
-            c0, c1 = QUANTISE_CUTS[piece : piece + 2]
-            name, shape = f"h_bf{piece}", [P, (c1 - c0) * CH * PACK]
-            tile = held(name, shape, BF16)
+        for c0, c1 in zip(QUANTISE_CUTS, QUANTISE_CUTS[1:]):
+            tile = held(f"h_bf{c0}", [P, (c1 - c0) * chunk_words], BF16)
             for c in range(c0, c1):
-                h_bf[c] = (tile, c0)
+                h_bf[c] = (tile, tile[:, (c - c0) * chunk_words : (c - c0 + 1) * chunk_words])
 
         def make_h(c):
             if c >= OPENED:
                 add_av_pass(c, 0)
             add_av_pass(c, 1)
-            tile, c0 = h_bf[c]
             nc.vector.tensor_tensor(
-                tile[:, (c - c0) * CH * PACK : (c - c0 + 1) * CH * PACK].rearrange("p (n f u e) -> p n u e f", f=2, u=2, e=2),
+                h_bf[c][1].rearrange("p (n f u e) -> p n u e f", f=2, u=2, e=2),
                 banks["av", c][:].rearrange("p (u e) (n f) -> p n u e f", u=2, f=2),
                 x_sb[c // 2][:, :, c % 2 * CH // 2 : (c % 2 + 1) * CH // 2, :, :].rearrange("p u n e f -> p n u e f"),
                 MULT,
@@ -235,12 +246,10 @@ def tile_list_allele_mixture_scores_kernel(
 
         def quantise_h(piece):
             c0, c1 = QUANTISE_CUTS[piece : piece + 2]
-            nc.vector.quantize_mx(
-                h_w[:, c0 * CH : c1 * CH].bitcast(FP8X4), h_s[:, c0 * CH : c1 * CH], h_bf[c0][0][:]
-            )
+            nc.vector.quantize_mx(h_w[:, c0 * CH : c1 * CH].bitcast(FP8X4), h_s[:, c0 * CH : c1 * CH], h_bf[c0][0][:])
 
         b_sb = held("b_sb", [P, PACK, S], F32)
-        damp = held("damp", [P, PACK, S], F32)
+        scores = held("scores", [P, PACK, S], F32)
         squares, roots = {}, {}
 
         def h_of(c):
@@ -252,54 +261,50 @@ def tile_list_allele_mixture_scores_kernel(
             for u in range(2):
                 nc.tensor.matmul_mx(
                     banks["d", c][:, u * HALF : (u + 1) * HALF], lhsT=hw, lhsT_scale=hs,
-                    rhs=w8_w[:, u * HALF : (u + 1) * HALF].bitcast(FP8X4), rhs_scale=planes[:, u * ROW + S + H : (u + 1) * ROW],
+                    rhs=w8_w[:, u * HALF : (u + 1) * HALF].bitcast(FP8X4), rhs_scale=planes[:, u * ROW + FIRST + H : (u + 1) * ROW],
                     start=True, stop=True,
                 )
 
         def square_d(c, i0=0, i1=PACK):
-            name, shape = f"square{c}", [P, PACK, P]
-            if c == 0:
-                squares[c] = stage[:, 3 * x_words - HALF :].rearrange("p (i m) -> p i m", i=PACK)
-            else:
-                squares[c] = (placed(name, shape, F32, at_root0 - 2 * N) if c == 1 else held(name, shape, F32))[:]
+            squares[c, i0] = held(f"square{c}_{i0}", [P, i1 - i0, P], F32)
             nc.scalar.activation(
-                squares[c][:, i0:i1, :], banks["d", c].rearrange("p (m i) -> p i m", i=PACK)[:, i0:i1, :], ACT.Square
+                squares[c, i0][:], banks["d", c].rearrange("p (m i) -> p i m", i=PACK)[:, i0:i1, :], ACT.Square
             )
 
         def take_roots(c, i0=0, i1=PACK):
-            name, shape = f"root{c}", [P, PACK, P]
             if i0 == 0:
-                roots[c] = placed(name, shape, F32, at_root0) if c == 0 else held(name, shape, F32)
+                roots[c] = held(f"root{c}", [P, PACK, P], F32)
             for g in range(GROUPS):
                 factor = winv[:, g * CHUNKS + c : g * CHUNKS + c + 1]
                 nc.scalar.activation(
-                    roots[c][:, i0:i1, g * GP : (g + 1) * GP], squares[c][:, i0:i1, g * GP : (g + 1) * GP], ACT.Abs_reciprocal_sqrt,
+                    roots[c][:, i0:i1, g * GP : (g + 1) * GP], squares[c, i0][:, :, g * GP : (g + 1) * GP], ACT.Abs_reciprocal_sqrt,
                     bias=factor, scale=factor,
                 )
 
-        def multiply_b(c):
+        def multiply_b(c, i0=0, i1=PACK):
             hw, hs = h_of(c)
-            banks["b", c] = new_bank(f"b{c}", B_BANKS[min(c, 1)])
-            for i in range(PACK):
+            banks["b", c, i0] = new_bank(f"b{c}_{i0}", TURN_BANKS[(c + 1) % 2] if c else EARLY_B_BANKS[i0 // 2])
+            for i in range(i0, i1):
                 nc.tensor.matmul_mx(
-                    banks["b", c][:, i, :], lhsT=wb_q[i][0], lhsT_scale=wb_q[i][1], rhs=hw, rhs_scale=hs, start=True, stop=True
+                    banks["b", c, i0][:, i, :], lhsT=wb_q[i][0], lhsT_scale=wb_q[i][1], rhs=hw, rhs_scale=hs, start=True, stop=True
                 )
 
         def copy_b(c, i0=0, i1=PACK):
-            nc.scalar.copy(b_sb[:, i0:i1, c * CH : (c + 1) * CH], banks["b", c][:, i0:i1, :])
+            nc.scalar.copy(b_sb[:, i0:i1, c * CH : (c + 1) * CH], banks["b", c, i0][:, i0:i1, :])
 
         def turn_roots(c, i0=0, i1=PACK):
-            banks["r", c, i0] = new_bank(f"r{c}_{i0}", R_BANKS[min(c, 1)] if i1 == PACK else EARLY_R_BANK)
+            banks["r", c, i0] = new_bank(f"r{c}_{i0}", TURN_BANKS[c % 2 if i1 == PACK else 1])
             for i in range(i0, i1):
                 nc.tensor.transpose(banks["r", c, i0][:, i, :], roots[c][:, i, :], ident[:])
 
-        def square_roots(c, i0=0, i1=PACK):
-            nc.scalar.activation(damp[:, i0:i1, c * CH : (c + 1) * CH], banks["r", c, i0][:, i0:i1, :], ACT.Square)
-            scores = damp[:, i0:i1, c * CH : (c + 1) * CH]
-            nc.gpsimd.tensor_tensor(scores, scores, b_sb[:, i0:i1, c * CH : (c + 1) * CH], MULT)
+        def weigh(c, i0=0, i1=PACK):
+            nc.scalar.activation(scores[:, i0:i1, c * CH : (c + 1) * CH], banks["r", c, i0][:, i0:i1, :], ACT.Square)
 
         def put(i, c0, c1):
-            nc.vector.tensor_copy(pages[i][:].indirect(bins[:, c0 * CH // 16 : c1 * CH // 16]), damp[:, i, c0 * CH : c1 * CH])
+            nc.vector.tensor_tensor(
+                pages[i][:].indirect(bins[:, c0 * CH // 16 : c1 * CH // 16]),
+                b_sb[:, i, c0 * CH : c1 * CH], scores[:, i, c0 * CH : c1 * CH], MULT,
+            )
 
         def second_stage(c):
             turn_roots(c)
@@ -308,77 +313,68 @@ def tile_list_allele_mixture_scores_kernel(
             if c + 2 < CHUNKS:
                 multiply_d(c + 2)
             copy_b(c)
-            if c < DEEP_FROM:
-                square_roots(c)
+            weigh(c)
             if c + 1 < CHUNKS:
                 multiply_b(c + 1)
                 take_roots(c + 1)
-            if c >= DEEP_FROM:
-                square_roots(c)
 
         def scatter(c):
             for i in range(PACK):
                 if c < LAST_FROM[i]:
                     put(i, c, c + 1)
 
-        wa_g0 = regroup(placed("wa_g0", [P, PACK, P, PACK], BF16, at_wa_g0), nc.scalar.copy, wa_raw0, 0, PACK)
-        gather_words(0, 0)
-        wa_q = [quantise("wa_q0", wa_g0)]
-        gather_words(0, 1)
-        for pair in range(2):
-            for u in range(2):
-                add_x_pass(pair, u, 0)
-            for c in range(2 * pair, 2 * pair + 2):
-                add_av_pass(c, 0)
-        gather_words(1, 0)
-        gather_words(1, 1)
-        gather_words(1, 2)
-        wa_low = regroup(held("wa_low", [P, 2, P, PACK], BF16), nc.vector.tensor_copy, wa_raw1, 0, 2)
-        wa_high = regroup(placed("wa_high", [P, 2, P, PACK], BF16, at_wa_g0), nc.scalar.copy, wa_raw1, 2, PACK)
-        project(0)
-        project(1)
-        wa_q.append(quantise("wa_q1a", wa_low) + quantise("wa_q1b", wa_high))
-        gather_words(1, 3, at_wa_g0)
+        by_vector, by_scalar = [(nc.vector.tensor_copy, 0, P)], [(nc.scalar.copy, 0, P)]
+        gather_words()
+        project_pair(0)
+        project_pair(1)
+        wa0_low = regroup("wa0_low", wa_raw0, 0, by_vector)
+        wa0_high = regroup("wa0_high", wa_raw0, 2, by_vector)
+        wa_q = [quantise("wa_q0a", wa0_low) + quantise("wa_q0b", wa0_high)]
+        wa1_low = regroup("wa1_low", wa_raw1, 0, by_vector)
+        wa1_high = regroup("wa1_high", wa_raw1, 2, [(nc.scalar.copy, 0, SHARED), (nc.vector.tensor_copy, SHARED, P)])
+        project_pair(2)
+        for c in range(OPENED):
+            add_av_pass(c, 0)
+        wa_q.append(quantise("wa_q1a", wa1_low) + quantise("wa_q1b", wa1_high))
         make_h(0)
         make_h(1)
         quantise_h(0)
         multiply_d(0)
-        wb_high = regroup(held("wb_high", [P, 2, P, PACK], BF16), nc.scalar.copy, wb_raw, 2, PACK)
-        project(2, (0,))
-        wb_low = regroup(held("wb_low", [P, 2, P, PACK], BF16), nc.vector.tensor_copy, wb_raw, 0, 2)
+        wb_low = regroup("wb_low", wb_raw, 0, by_scalar)
+        wb_high = regroup("wb_high", wb_raw, 2, by_scalar)
         make_h(2)
-        wb_q = quantise("wb_qa", wb_low) + quantise("wb_qb", wb_high)
         make_h(3)
+        wb_q = quantise("wb_qa", wb_low)
+        quantise_h(1)
         square_d(0, 0, 2)
         square_d(0, 2, PACK)
         take_roots(0, 0, 2)
         turn_roots(0, 0, 2)
-        project(2, (1,))
-        multiply_b(0)
         make_h(4)
-        quantise_h(1)
-        multiply_d(1)
+        wb_q = wb_q + quantise("wb_qb", wb_high)
         make_h(5)
+        quantise_h(2)
+        multiply_b(0, 0, 2)
+        weigh(0, 0, 2)
         copy_b(0, 0, 2)
-        square_roots(0, 0, 2)
         take_roots(0, 2, PACK)
         turn_roots(0, 2, PACK)
+        multiply_b(0, 2, PACK)
+        multiply_d(1)
         copy_b(0, 2, PACK)
-        square_roots(0, 2, PACK)
+        weigh(0, 2, PACK)
         square_d(1)
+        project_pair(3)
         multiply_d(2)
         multiply_b(1)
         take_roots(1)
         scatter(0)
-        quantise_h(2)
-        project(3)
         make_h(6)
         make_h(7)
+        quantise_h(3)
         for c in range(1, CHUNKS):
             second_stage(c)
             scatter(c)
-            if c == 1:
-                quantise_h(3)
         for i in range(PACK):
             put(i, LAST_FROM[i], CHUNKS)
             nc.sync.dma_start(out.rearrange("(p i) t -> p i t", i=PACK)[:, i, :], pages[i][:])

@@ -31,7 +31,7 @@ SHARED = 96
 HALF = N // 2
 FIRST = S // 2
 ROW = FIRST + H + HALF
-QUANTISE_CUTS = (0, 1, 4, 6, 8)
+QUANTISE_CUTS = (0, 1, 4, 6, 7, 8)
 QUADRANTS = (0, 2, 1, 3)
 LAST_FROM = (7, 6, 5, 4)
 X_BANKS = (0, 1, 2, 3, 4, 5, 2, 4)
@@ -78,7 +78,7 @@ def tile_list_allele_mixture_scores_kernel(
         pages = [held("page0", [P, T2], F32)]
 
         nc.gpsimd.memset(tab_s[:].bitcast(I32), 0)
-        for words in (w4_s_raw[:].bitcast(I32), wgo_rows[:].bitcast(I32), pages[0][:].bitcast(I32)):
+        for words in (w4_s_raw[:].bitcast(I32), wgo_rows[FACTORS:, :].bitcast(I32), pages[0][:].bitcast(I32)):
             last = words.shape[1] - 1
             nc.vector.memset(words[:, :last], 0)
             nc.vector.memset(words[:, last:], 0)
@@ -103,12 +103,12 @@ def tile_list_allele_mixture_scores_kernel(
             w4_words.bitcast(I32).rearrange("a p c -> p a c"),
         )
         nc.sync.dma_start(rows_s[0:P:4, FIRST + H : ROW].bitcast(I32), w8_scales[0].bitcast(I32))
+        nc.sync.dma_start(wgo_rows[0:FACTORS, :], wgo[0:P:GP, :])
         nc.sync.dma_start(tab_s[0:P:4, :].bitcast(I32), tab_scales.bitcast(I32).rearrange("a q t -> q a t"))
         nc.sync.dma_start(w4_s_raw[0:P:4, :].bitcast(I32), w4_scales.bitcast(I32).rearrange("a q c -> q a c"))
         tab_w = [held(f"tab_w{a}", [P, T], U32) for a in range(PASSES)]
         table = [tab_words[a].rearrange("p t i -> p (t i)").bitcast(I32) for a in range(PASSES)]
         nc.sync.dma_start(tab_w[0][:].bitcast(I32), table[0])
-        nc.sync.dma_start(wgo_rows[0:FACTORS, :], wgo[0:P:GP, :])
         nc.sync.dma_start(tab_w[1][:].bitcast(I32), table[1])
 
         nc.vector.tensor_copy(picked_s[:], tab_s[:].indirect(picks[:, : FIRST // 16]))
@@ -145,7 +145,7 @@ def tile_list_allele_mixture_scores_kernel(
         move(late_planes, late_s)
         stage = held("stage", [P, PACK * H], F32)
         wa_raw1 = load_rows(stage[:].rearrange("p (j c) -> p j c", j=PACK), wa[512:1024, :])
-        wb_raw = load_rows(held("wb_raw", [P, PACK, N], F32)[:], wb)
+        wb_raw = [load_rows(held(f"wb_raw{u}", [P, PACK, HALF], F32)[:], wb[:, u * HALF : (u + 1) * HALF]) for u in range(2)]
         w8_w = load_words("w8_w", w8_words[0])
         nc.sync.dma_start(bins[:], offs2)
         w4_q = [
@@ -156,14 +156,11 @@ def tile_list_allele_mixture_scores_kernel(
             for a in range(PASSES)
         ]
 
-        def regroup(name, raw, t0, shares):
-            grouped = held(name, [P, 2, P, PACK], BF16)
-            for copy, m0, m1 in shares:
-                copy(
-                    grouped[:, :, m0:m1, :].rearrange("p t m j -> p m j t"),
-                    raw.rearrange("p j (m t) -> p m j t", t=PACK)[:, m0:m1, :, t0 : t0 + 2],
-                )
-            return grouped
+        def regroup(grouped, copy, raw, t0, m0=0, m1=P, first=0):
+            copy(
+                grouped[:, :, m0:m1, :].rearrange("p t m j -> p m j t"),
+                raw.rearrange("p j (m t) -> p m j t", t=PACK)[:, m0 - first : m1 - first, :, t0 : t0 + 2],
+            )
 
         def quantise(name, grouped):
             codes = held(name + "_w", [P, 2 * P], U32)
@@ -206,13 +203,9 @@ def tile_list_allele_mixture_scores_kernel(
 
         x_sb = {}
 
-        def x_room(pair):
-            if pair < 2:
-                return held(f"x_pair{pair}", [P, 2 * chunk_words], F32)[:]
-            return stage[:, (pair - 2) * 2 * chunk_words : (pair - 1) * 2 * chunk_words]
-
         def project_pair(pair):
-            x_sb[pair] = x_room(pair).rearrange("p (u n e f) -> p u n e f", u=2, e=2, f=2)
+            room = stage[:, : 2 * chunk_words] if pair == 2 else held(f"x_pair{pair}", [P, 2 * chunk_words], F32)[:]
+            x_sb[pair] = room.rearrange("p (u n e f) -> p u n e f", u=2, e=2, f=2)
             for u in range(2):
                 bank = new_bank(f"x{pair}_{u}", X_BANKS[2 * pair + u])[:].rearrange("p (e h) n -> p e (h n)", e=2)
                 for a in range(PASSES):
@@ -323,37 +316,40 @@ def tile_list_allele_mixture_scores_kernel(
                 if c < LAST_FROM[i]:
                     put(i, c, c + 1)
 
-        by_vector, by_scalar = [(nc.vector.tensor_copy, 0, P)], [(nc.scalar.copy, 0, P)]
+        grouped = {(name, t0): held(f"{name}_{t0}", [P, 2, P, PACK], BF16) for name in ("wa0", "wa1", "wb") for t0 in (0, 2)}
         gather_words()
         project_pair(0)
         project_pair(1)
-        wa0_low = regroup("wa0_low", wa_raw0, 0, by_vector)
-        wa0_high = regroup("wa0_high", wa_raw0, 2, by_vector)
-        wa_q = [quantise("wa_q0a", wa0_low) + quantise("wa_q0b", wa0_high)]
-        wa1_low = regroup("wa1_low", wa_raw1, 0, by_vector)
-        wa1_high = regroup("wa1_high", wa_raw1, 2, [(nc.scalar.copy, 0, SHARED), (nc.vector.tensor_copy, SHARED, P)])
-        project_pair(2)
+        for t0 in (0, 2):
+            regroup(grouped["wa0", t0], nc.vector.tensor_copy, wa_raw0, t0)
+        wa_q = [quantise("wa_q0a", grouped["wa0", 0]) + quantise("wa_q0b", grouped["wa0", 2])]
         for c in range(OPENED):
             add_av_pass(c, 0)
-        wa_q.append(quantise("wa_q1a", wa1_low) + quantise("wa_q1b", wa1_high))
+        regroup(grouped["wa1", 0], nc.vector.tensor_copy, wa_raw1, 0)
+        regroup(grouped["wa1", 2], nc.scalar.copy, wa_raw1, 2, 0, SHARED)
+        regroup(grouped["wa1", 2], nc.vector.tensor_copy, wa_raw1, 2, SHARED, P)
+        project_pair(2)
+        wa_q.append(quantise("wa_q1a", grouped["wa1", 0]) + quantise("wa_q1b", grouped["wa1", 2]))
+        for t0 in (0, 2):
+            regroup(grouped["wb", t0], nc.vector.tensor_copy, wb_raw[0], t0, 0, P // 2)
+        for t0 in (0, 2):
+            regroup(grouped["wb", t0], nc.scalar.copy, wb_raw[1], t0, P // 2, P, P // 2)
         make_h(0)
         make_h(1)
         quantise_h(0)
         multiply_d(0)
-        wb_low = regroup("wb_low", wb_raw, 0, by_scalar)
-        wb_high = regroup("wb_high", wb_raw, 2, by_scalar)
         make_h(2)
         make_h(3)
-        wb_q = quantise("wb_qa", wb_low)
+        wb_q = quantise("wb_qa", grouped["wb", 0])
         quantise_h(1)
+        make_h(4)
+        make_h(5)
+        wb_q = wb_q + quantise("wb_qb", grouped["wb", 2])
+        quantise_h(2)
         square_d(0, 0, 2)
         square_d(0, 2, PACK)
         take_roots(0, 0, 2)
         turn_roots(0, 0, 2)
-        make_h(4)
-        wb_q = wb_q + quantise("wb_qb", wb_high)
-        make_h(5)
-        quantise_h(2)
         multiply_b(0, 0, 2)
         weigh(0, 0, 2)
         copy_b(0, 0, 2)
@@ -372,6 +368,7 @@ def tile_list_allele_mixture_scores_kernel(
         make_h(6)
         make_h(7)
         quantise_h(3)
+        quantise_h(4)
         for c in range(1, CHUNKS):
             second_stage(c)
             scatter(c)

@@ -33,7 +33,7 @@ FIRST = S // 2
 ROW = FIRST + H + HALF
 QUANTISE_CUTS = (0, 1, 4, 6, 7, 8)
 QUADRANTS = (0, 2, 1, 3)
-LAST_FROM = (7, 6, 5, 4)
+PIECES = ((0, 1, 2, 3, 4, 6, 7, 8), (0, 1, 2, 3, 4, 6, 7, 8), (0, 1, 2, 4, 8), (0, 1, 2, 4, 8))
 X_BANKS = (0, 1, 2, 3, 4, 5, 2, 4)
 AV_BANKS = (0, 1, 4, 5, 0, 1, 0, 1)
 D_BANKS, TURN_BANKS = (6, 7), (3, 2)
@@ -313,8 +313,8 @@ def tile_list_allele_mixture_scores_kernel(
 
         def scatter(c):
             for i in range(PACK):
-                if c < LAST_FROM[i]:
-                    put(i, c, c + 1)
+                if c in PIECES[i][1:-1]:
+                    put(i, PIECES[i][PIECES[i].index(c) - 1], c)
 
         grouped = {(name, t0): held(f"{name}_{t0}", [P, 2, P, PACK], BF16) for name in ("wa0", "wa1", "wb") for t0 in (0, 2)}
         gather_words()
@@ -364,14 +364,14 @@ def tile_list_allele_mixture_scores_kernel(
         multiply_d(2)
         multiply_b(1)
         take_roots(1)
-        scatter(0)
+        scatter(1)
         make_h(6)
         make_h(7)
         quantise_h(3)
         quantise_h(4)
         for c in range(1, CHUNKS):
             second_stage(c)
-            scatter(c)
+            scatter(c + 1)
         for i in range(PACK):
-            put(i, LAST_FROM[i], CHUNKS)
+            put(i, PIECES[i][-2], CHUNKS)
             nc.sync.dma_start(out.rearrange("(p i) t -> p i t", i=PACK)[:, i, :], pages[i][:])

@@ -78,11 +78,10 @@ def tile_list_allele_mixture_scores_kernel(
         pages = [held("page0", [P, T2], F32)]
 
         nc.gpsimd.memset(tab_s[:].bitcast(I32), 0)
-        for words in (w4_s_raw[:].bitcast(I32), wgo_rows[FACTORS:, :].bitcast(I32), pages[0][:].bitcast(I32)):
+        for words in (ident[:].bitcast(I32), w4_s_raw[:].bitcast(I32), wgo_rows[FACTORS:, :].bitcast(I32), pages[0][:].bitcast(I32)):
             last = words.shape[1] - 1
             nc.vector.memset(words[:, :last], 0)
             nc.vector.memset(words[:, last:], 0)
-        nc.gpsimd.memset(ident[:], 0.0)
         make_identity(nc, ident[:], nomemset=True)
         pages.append(held("page1", [P, T2], F32))
         nc.gpsimd.memset(pages[1][:].bitcast(I32), 0)
@@ -143,8 +142,8 @@ def tile_list_allele_mixture_scores_kernel(
         move(planes, rows_s)
         wa_raw0 = load_rows(held("wa_raw0", [P, PACK, H], F32)[:], wa[0:512, :])
         move(late_planes, late_s)
-        stage = held("stage", [P, PACK * H], F32)
-        wa_raw1 = load_rows(stage[:].rearrange("p (j c) -> p j c", j=PACK), wa[512:1024, :])
+        stage = held("stage", [P, chunk_words + PACK * H], F32)
+        wa_raw1 = load_rows(stage[:, chunk_words:].rearrange("p (j c) -> p j c", j=PACK), wa[512:1024, :])
         wb_raw = [load_rows(held(f"wb_raw{u}", [P, PACK, HALF], F32)[:], wb[:, u * HALF : (u + 1) * HALF]) for u in range(2)]
         w8_w = load_words("w8_w", w8_words[0])
         nc.sync.dma_start(bins[:], offs2)
@@ -203,10 +202,11 @@ def tile_list_allele_mixture_scores_kernel(
 
         x_sb = {}
 
-        def project_pair(pair):
-            room = stage[:, : 2 * chunk_words] if pair == 2 else held(f"x_pair{pair}", [P, 2 * chunk_words], F32)[:]
+        def project_pair(pair, halves=(0, 1)):
+            at = (pair - 1) * 2 * chunk_words
+            room = stage[:, at : at + 2 * chunk_words] if pair in (1, 2) else held(f"x_pair{pair}", [P, 2 * chunk_words], F32)[:]
             x_sb[pair] = room.rearrange("p (u n e f) -> p u n e f", u=2, e=2, f=2)
-            for u in range(2):
+            for u in halves:
                 bank = new_bank(f"x{pair}_{u}", X_BANKS[2 * pair + u])[:].rearrange("p (e h) n -> p e (h n)", e=2)
                 for a in range(PASSES):
                     words, word_scales = picked_columns(a, 2 * pair, 2)
@@ -319,7 +319,7 @@ def tile_list_allele_mixture_scores_kernel(
         grouped = {(name, t0): held(f"{name}_{t0}", [P, 2, P, PACK], BF16) for name in ("wa0", "wa1", "wb") for t0 in (0, 2)}
         gather_words()
         project_pair(0)
-        project_pair(1)
+        project_pair(1, (0,))
         for t0 in (0, 2):
             regroup(grouped["wa0", t0], nc.vector.tensor_copy, wa_raw0, t0)
         wa_q = [quantise("wa_q0a", grouped["wa0", 0]) + quantise("wa_q0b", grouped["wa0", 2])]
@@ -328,6 +328,7 @@ def tile_list_allele_mixture_scores_kernel(
         regroup(grouped["wa1", 0], nc.vector.tensor_copy, wa_raw1, 0)
         regroup(grouped["wa1", 2], nc.scalar.copy, wa_raw1, 2, 0, SHARED)
         regroup(grouped["wa1", 2], nc.vector.tensor_copy, wa_raw1, 2, SHARED, P)
+        project_pair(1, (1,))
         project_pair(2)
         wa_q.append(quantise("wa_q1a", grouped["wa1", 0]) + quantise("wa_q1b", grouped["wa1", 2]))
         for t0 in (0, 2):

@@ -25,7 +25,7 @@ CHUNKS = S // CH
 GROUPS = 8
 GP = P // GROUPS
 FACTORS = GROUPS * CHUNKS
-GATHERS = ((0, 0, 4), (0, 4, 8), (1, 0, 2), (1, 2, 4), (1, 4, 8))
+GATHERS = ((0, 0, 4), (0, 4, 8), (1, 0, 2), (1, 2, 4), (1, 4, 6), (1, 6, 8))
 OPENED = 2
 SHARED = 96
 HALF = N // 2
@@ -64,6 +64,7 @@ def tile_list_allele_mixture_scores_kernel(
         at_late_s = at_planes + PASSES * ROW
         at_picked_s = at_late_s + S - FIRST - 64
         at_page2 = at_picked_s + FIRST - 64
+        at_grouped = at_page2 + 4 * T2
         chunk_words = CH * PACK
 
         picks = keep.tile([P, S // 16], U16, name="picks")
@@ -169,9 +170,10 @@ def tile_list_allele_mixture_scores_kernel(
 
         v_w = {}
 
-        def gather_words():
-            for a, c0, c1 in GATHERS:
-                picked = held(f"v_w{a}_{c0}", [P, (c1 - c0) * CH], U32)
+        def gather_words(pieces, at=None):
+            for a, c0, c1 in pieces:
+                name, shape = f"v_w{a}_{c0}", [P, (c1 - c0) * CH]
+                picked = held(name, shape, U32) if at is None else placed(name, shape, U32, at)
                 nc.vector.tensor_copy(picked[:], tab_w[a][:].indirect(picks[:, c0 * CH // 16 : c1 * CH // 16]))
                 for c in range(c0, c1):
                     v_w[a, c] = (picked, c0)
@@ -204,7 +206,7 @@ def tile_list_allele_mixture_scores_kernel(
 
         def project_pair(pair, halves=(0, 1)):
             at = (pair - 1) * 2 * chunk_words
-            room = stage[:, at : at + 2 * chunk_words] if pair in (1, 2) else held(f"x_pair{pair}", [P, 2 * chunk_words], F32)[:]
+            room = stage[:, at : at + 2 * chunk_words] if pair == 2 else held(f"x_pair{pair}", [P, 2 * chunk_words], F32)[:]
             x_sb[pair] = room.rearrange("p (u n e f) -> p u n e f", u=2, e=2, f=2)
             for u in halves:
                 bank = new_bank(f"x{pair}_{u}", X_BANKS[2 * pair + u])[:].rearrange("p (e h) n -> p e (h n)", e=2)
@@ -316,10 +318,11 @@ def tile_list_allele_mixture_scores_kernel(
                 if c in PIECES[i][1:-1]:
                     put(i, PIECES[i][PIECES[i].index(c) - 1], c)
 
-        grouped = {(name, t0): held(f"{name}_{t0}", [P, 2, P, PACK], BF16) for name in ("wa0", "wa1", "wb") for t0 in (0, 2)}
-        gather_words()
+        grouped = {(name, t0): held(f"{name}_{t0}", [P, 2, P, PACK], BF16) for name, t0 in (("wa0", 0), ("wa0", 2), ("wa1", 2), ("wb", 0), ("wb", 2))}
+        grouped["wa1", 0] = placed("wa1_0", [P, 2, P, PACK], BF16, at_grouped)
+        gather_words(GATHERS[:-1])
         project_pair(0)
-        project_pair(1, (0,))
+        project_pair(1)
         for t0 in (0, 2):
             regroup(grouped["wa0", t0], nc.vector.tensor_copy, wa_raw0, t0)
         wa_q = [quantise("wa_q0a", grouped["wa0", 0]) + quantise("wa_q0b", grouped["wa0", 2])]
@@ -328,11 +331,11 @@ def tile_list_allele_mixture_scores_kernel(
         regroup(grouped["wa1", 0], nc.vector.tensor_copy, wa_raw1, 0)
         regroup(grouped["wa1", 2], nc.scalar.copy, wa_raw1, 2, 0, SHARED)
         regroup(grouped["wa1", 2], nc.vector.tensor_copy, wa_raw1, 2, SHARED, P)
-        project_pair(1, (1,))
         project_pair(2)
         wa_q.append(quantise("wa_q1a", grouped["wa1", 0]) + quantise("wa_q1b", grouped["wa1", 2]))
-        for t0 in (0, 2):
-            regroup(grouped["wb", t0], nc.vector.tensor_copy, wb_raw[0], t0, 0, P // 2)
+        gather_words(GATHERS[-1:], at_grouped)
+        regroup(grouped["wb", 0], nc.vector.tensor_copy, wb_raw[0], 0, 0, P // 2)
+        regroup(grouped["wb", 2], nc.scalar.copy, wb_raw[0], 2, 0, P // 2)
         for t0 in (0, 2):
             regroup(grouped["wb", t0], nc.scalar.copy, wb_raw[1], t0, P // 2, P, P // 2)
         make_h(0)

from contextlib import ExitStack

import concourse.mybir as mybir
from concourse.masks import make_identity

K, T, S, T2, H, N = 1024, 2048, 1024, 2048, 512, 512
FLOPS = 2 * (2 * K * H * S + 2 * H * N * S)

F32 = mybir.dt.float32
BF16 = mybir.dt.bfloat16
I32 = mybir.dt.int32
U32 = mybir.dt.uint32
U16 = mybir.dt.uint16
U8 = mybir.dt.uint8
FP8X4 = mybir.dt.float8_e4m3fn_x4
FP4X4 = mybir.dt.float4_e2m1fn_x4
ACT = mybir.ActivationFunctionType
MULT = mybir.AluOpType.mult

P = 128
PACK = 4
PASSES = K // (P * PACK)
CH = 128
CHUNKS = S // CH
GROUPS = 8
GP = P // GROUPS
FACTORS = GROUPS * CHUNKS
GATHERS = ((0, 0, 4), (0, 4, 8), (1, 0, 2), (1, 2, 4), (1, 4, 6), (1, 6, 8))
OPENED = 2
SHARED = 96
HALF = N // 2
FIRST = S // 2
ROW = FIRST + H + HALF
QUANTISE_CUTS = (0, 1, 4, 6, 7, 8)
QUADRANTS = (0, 2, 1, 3)
PIECES = ((0, 1, 2, 3, 4, 6, 7, 8), (0, 1, 2, 3, 4, 6, 7, 8), (0, 1, 2, 4, 8), (0, 1, 2, 4, 8))
X_BANKS = (0, 1, 2, 3, 4, 5, 2, 4)
AV_BANKS = (0, 1, 4, 5, 0, 1, 0, 1)
D_BANKS, TURN_BANKS = (6, 7), (3, 2)
W_BANK, EARLY_B_BANKS = 7, (6, 4)


def tile_list_allele_mixture_scores_kernel(
    tc, tab_words, tab_scales, w4_words, w4_scales, wa, wb, w8_words, w8_scales, wgo, offs, offs2, out
):
    nc = tc.nc
    with ExitStack() as ctx:
        keep = ctx.enter_context(tc.tile_pool(name="keep", bufs=1))
        laid = ctx.enter_context(tc.tile_pool(name="laid", bufs=1))
        psum = ctx.enter_context(tc.psum_pool(name="psum", bufs=1))

        def held(name, shape, dtype):
            return keep.tile(shape, dtype, name=name, align_bytes=64)

        def placed(name, shape, dtype, offset):
            return laid.tile(shape, dtype, name=name, align_bytes=64, offset=offset)

        def new_bank(name, bank):
            return psum.tile([P, PACK, CH], F32, name=name, tag=f"bank{bank}")

        at_tab_s = 0
        at_page3 = at_tab_s + T - 64
        at_planes = at_page3 + 4 * T2
        at_late_s = at_planes + PASSES * ROW
        at_picked_s = at_late_s + S - FIRST - 64
        at_page2 = at_picked_s + FIRST - 64
        at_grouped = at_page2 + 4 * T2
        chunk_words = CH * PACK

        picks = keep.tile([P, S // 16], U16, name="picks")
        bins = keep.tile([P, S // 16], U16, name="bins")
        tab_s = placed("tab_s", [P, T], U8, at_tab_s)
        w4_s_raw = placed("w4_s_raw", [P, H], U8, at_planes + PASSES * 2 * H)
        picked_s = placed("picked_s", [P, FIRST], U8, at_picked_s)
        rows_s = held("rows_s", [P, ROW], U8)
        late_planes = placed("late_planes", [P, PASSES * (S - FIRST)], U8, at_tab_s)
        wgo_rows = held("wgo_rows", [P, CH], F32)
        ident = held("ident", [P, P], F32)
        pages = [held("page0", [P, T2], F32)]

        nc.gpsimd.memset(tab_s[:].bitcast(I32), 0)
        for words in (ident[:].bitcast(I32), w4_s_raw[:].bitcast(I32), wgo_rows[FACTORS:, :].bitcast(I32), pages[0][:].bitcast(I32)):
            last = words.shape[1] - 1
            nc.vector.memset(words[:, :last], 0)
            nc.vector.memset(words[:, last:], 0)
        make_identity(nc, ident[:], nomemset=True)
        pages.append(held("page1", [P, T2], F32))
        nc.gpsimd.memset(pages[1][:].bitcast(I32), 0)

        def load_rows(tile, rows):
            nc.sync.dma_start(tile, rows.rearrange("(p j) c -> p j c", j=PACK))
            return tile

        def load_words(name, words):
            tile = held(name, [P, words.shape[1]], U32)
            nc.sync.dma_start(tile[:].bitcast(I32), words.rearrange("p t i -> p (t i)").bitcast(I32))
            return tile

        nc.sync.dma_start(picks[:], offs)
        w4_raw = placed("w4_raw", [P, PASSES * 2 * H], U8, at_planes)
        nc.sync.dma_start(
            w4_raw[:].bitcast(I32).rearrange("p (a c) -> p a c", a=PASSES),
            w4_words.bitcast(I32).rearrange("a p c -> p a c"),
        )
        nc.sync.dma_start(rows_s[0:P:4, FIRST + H : ROW].bitcast(I32), w8_scales[0].bitcast(I32))
        nc.sync.dma_start(wgo_rows[0:FACTORS, :], wgo[0:P:GP, :])
        nc.sync.dma_start(tab_s[0:P:4, :].bitcast(I32), tab_scales.bitcast(I32).rearrange("a q t -> q a t"))
        nc.sync.dma_start(w4_s_raw[0:P:4, :].bitcast(I32), w4_scales.bitcast(I32).rearrange("a q c -> q a c"))
        tab_w = [held(f"tab_w{a}", [P, T], U32) for a in range(PASSES)]
        table = [tab_words[a].rearrange("p t i -> p (t i)").bitcast(I32) for a in range(PASSES)]
        nc.sync.dma_start(tab_w[0][:].bitcast(I32), table[0])
        nc.sync.dma_start(tab_w[1][:].bitcast(I32), table[1])

        nc.vector.tensor_copy(picked_s[:], tab_s[:].indirect(picks[:, : FIRST // 16]))
        nc.vector.tensor_copy(
            rows_s[:, FIRST : FIRST + H].rearrange("p (t m) -> p t m", t=PACK), w4_s_raw[:].rearrange("p (m t) -> p t m", t=PACK)
        )
        nc.vector.tensor_copy(rows_s[:, 0:FIRST].bitcast(I32), picked_s[:].bitcast(I32))
        late_s = placed("late_s", [P, S - FIRST], U8, at_late_s)
        nc.vector.tensor_copy(late_s[:], tab_s[:].indirect(picks[:, FIRST // 16 :]))
        for i, at in ((2, at_page2), (3, at_page3)):
            pages.append(placed(f"page{i}", [P, T2], F32, at))
            nc.gpsimd.memset(pages[i][:].bitcast(I32), 0)

        winv = held("winv", [P, FACTORS], F32)
        wroot = held("wroot", [P, FACTORS], F32)
        w_bank = new_bank("w_bank", W_BANK)
        nc.tensor.transpose(w_bank[:, 0, :], wgo_rows[:], ident[:])
        nc.scalar.activation(wroot[:], w_bank[:, 0, 0:FACTORS], ACT.Abs_reciprocal_sqrt)
        nc.scalar.activation(winv[:], wroot[:], ACT.Square)

        w4_w = held("w4_w", [P, PASSES * 2 * H], U8)
        nc.scalar.copy(
            w4_w[:].bitcast(U16).rearrange("p (a t m) -> p a t m", a=PASSES, t=PACK),
            w4_raw[:].bitcast(U16).rearrange("p (a m t) -> p a t m", a=PASSES, t=PACK),
        )

        def move(target, rows):
            for d in QUADRANTS:
                nc.sync.dma_start(target[32 * d : 32 * d + 4, :].bitcast(I32), rows[32 * d : 32 * d + 32 : 4, :].bitcast(I32))

        planes = placed("planes", [P, PASSES * ROW], U8, at_planes)
        move(planes, rows_s)
        wa_raw0 = load_rows(held("wa_raw0", [P, PACK, H], F32)[:], wa[0:512, :])
        move(late_planes, late_s)
        stage = held("stage", [P, chunk_words + PACK * H], F32)
        wa_raw1 = load_rows(stage[:, chunk_words:].rearrange("p (j c) -> p j c", j=PACK), wa[512:1024, :])
        wb_raw = [load_rows(held(f"wb_raw{u}", [P, PACK, HALF], F32)[:], wb[:, u * HALF : (u + 1) * HALF]) for u in range(2)]
        w8_w = load_words("w8_w", w8_words[0])
        nc.sync.dma_start(bins[:], offs2)
        w4_q = [
            [
                (w4_w[:, 2 * (a * H + col) : 2 * (a * H + col + P)].bitcast(FP4X4), planes[:, a * ROW + FIRST + col : a * ROW + FIRST + col + P])
                for col in range(0, H, P)
            ]
            for a in range(PASSES)
        ]

        def regroup(grouped, copy, raw, t0, m0=0, m1=P, first=0):
            copy(
                grouped[:, :, m0:m1, :].rearrange("p t m j -> p m j t"),
                raw.rearrange("p j (m t) -> p m j t", t=PACK)[:, m0 - first : m1 - first, :, t0 : t0 + 2],
            )

        def quantise(name, grouped):
            codes = held(name + "_w", [P, 2 * P], U32)
            scales = held(name + "_s", [P, 2 * P], U8)
            nc.vector.quantize_mx(codes[:].bitcast(FP8X4), scales[:], grouped[:].rearrange("p t m j -> p (t m j)"))
            return [(codes[:, t * P : (t + 1) * P].bitcast(FP8X4), scales[:, t * P : (t + 1) * P]) for t in range(2)]

        v_w = {}

        def gather_words(pieces, at=None):
            for a, c0, c1 in pieces:
                name, shape = f"v_w{a}_{c0}", [P, (c1 - c0) * CH]
                picked = held(name, shape, U32) if at is None else placed(name, shape, U32, at)
                nc.vector.tensor_copy(picked[:], tab_w[a][:].indirect(picks[:, c0 * CH // 16 : c1 * CH // 16]))
                for c in range(c0, c1):
                    v_w[a, c] = (picked, c0)

        def picked_columns(a, c, count):
            picked, c0 = v_w[a, c]
            words = picked[:, (c - c0) * CH : (c - c0 + count) * CH]
            if c * CH < FIRST:
                return words.bitcast(FP8X4), planes[:, a * ROW + c * CH : a * ROW + (c + count) * CH]
            at = a * (S - FIRST) + c * CH - FIRST
            return words.bitcast(FP8X4), late_planes[:, at : at + count * CH]

        banks = {}

        def add_pass(bank, weights, c, a):
            words, word_scales = picked_columns(a, c, 1)
            for t in range(PACK):
                codes, scales = weights[a][t]
                nc.tensor.matmul_mx(
                    bank[:, t, :], lhsT=codes, lhsT_scale=scales, rhs=words, rhs_scale=word_scales,
                    start=(a == 0 and t == 0), stop=(a == PASSES - 1 and t == PACK - 1),
                )

        def add_av_pass(c, a):
            if a == 0:
                banks["av", c] = new_bank(f"av{c}", AV_BANKS[c])
            add_pass(banks["av", c], wa_q, c, a)

        x_sb = {}

        def project_pair(pair, halves=(0, 1)):
            at = (pair - 1) * 2 * chunk_words
            room = stage[:, at : at + 2 * chunk_words] if pair == 2 else held(f"x_pair{pair}", [P, 2 * chunk_words], F32)[:]
            x_sb[pair] = room.rearrange("p (u n e f) -> p u n e f", u=2, e=2, f=2)
            for u in halves:
                bank = new_bank(f"x{pair}_{u}", X_BANKS[2 * pair + u])[:].rearrange("p (e h) n -> p e (h n)", e=2)
                for a in range(PASSES):
                    words, word_scales = picked_columns(a, 2 * pair, 2)
                    for e in range(2):
                        codes, scales = w4_q[a][2 * u + e]
                        nc.tensor.matmul_mx(
                            bank[:, e, :], lhsT=codes, lhsT_scale=scales, rhs=words, rhs_scale=word_scales,
                            start=(a == 0 and e == 0), stop=(a == PASSES - 1 and e == 1),
                        )
                nc.scalar.copy(x_sb[pair][:, u, :, :, :], bank.rearrange("p e (n f) -> p n e f", f=2))

        h_w = held("h_w", [P, S], U32)
        h_s = held("h_s", [P, S], U8)
        h_bf = {}
        for c0, c1 in zip(QUANTISE_CUTS, QUANTISE_CUTS[1:]):
            tile = held(f"h_bf{c0}", [P, (c1 - c0) * chunk_words], BF16)
            for c in range(c0, c1):
                h_bf[c] = (tile, tile[:, (c - c0) * chunk_words : (c - c0 + 1) * chunk_words])

        def make_h(c):
            if c >= OPENED:
                add_av_pass(c, 0)
            add_av_pass(c, 1)
            nc.vector.tensor_tensor(
                h_bf[c][1].rearrange("p (n f u e) -> p n u e f", f=2, u=2, e=2),
                banks["av", c][:].rearrange("p (u e) (n f) -> p n u e f", u=2, f=2),
                x_sb[c // 2][:, :, c % 2 * CH // 2 : (c % 2 + 1) * CH // 2, :, :].rearrange("p u n e f -> p n u e f"),
                MULT,
            )

        def quantise_h(piece):
            c0, c1 = QUANTISE_CUTS[piece : piece + 2]
            nc.vector.quantize_mx(h_w[:, c0 * CH : c1 * CH].bitcast(FP8X4), h_s[:, c0 * CH : c1 * CH], h_bf[c0][0][:])

        b_sb = held("b_sb", [P, PACK, S], F32)
        scores = held("scores", [P, PACK, S], F32)
        squares, roots = {}, {}

        def h_of(c):
            return h_w[:, c * CH : (c + 1) * CH].bitcast(FP8X4), h_s[:, c * CH : (c + 1) * CH]

        def multiply_d(c):
            hw, hs = h_of(c)
            banks["d", c] = new_bank(f"d{c}", D_BANKS[min(c, 1)])[:].rearrange("p i m -> p (i m)")
            for u in range(2):
                nc.tensor.matmul_mx(
                    banks["d", c][:, u * HALF : (u + 1) * HALF], lhsT=hw, lhsT_scale=hs,
                    rhs=w8_w[:, u * HALF : (u + 1) * HALF].bitcast(FP8X4), rhs_scale=planes[:, u * ROW + FIRST + H : (u + 1) * ROW],
                    start=True, stop=True,
                )

        def square_d(c, i0=0, i1=PACK):
            squares[c, i0] = held(f"square{c}_{i0}", [P, i1 - i0, P], F32)
            nc.scalar.activation(
                squares[c, i0][:], banks["d", c].rearrange("p (m i) -> p i m", i=PACK)[:, i0:i1, :], ACT.Square
            )

        def take_roots(c, i0=0, i1=PACK):
            if i0 == 0:
                roots[c] = held(f"root{c}", [P, PACK, P], F32)
            for g in range(GROUPS):
                factor = winv[:, g * CHUNKS + c : g * CHUNKS + c + 1]
                nc.scalar.activation(
                    roots[c][:, i0:i1, g * GP : (g + 1) * GP], squares[c, i0][:, :, g * GP : (g + 1) * GP], ACT.Abs_reciprocal_sqrt,
                    bias=factor, scale=factor,
                )

        def multiply_b(c, i0=0, i1=PACK):
            hw, hs = h_of(c)
            banks["b", c, i0] = new_bank(f"b{c}_{i0}", TURN_BANKS[(c + 1) % 2] if c else EARLY_B_BANKS[i0 // 2])
            for i in range(i0, i1):
                nc.tensor.matmul_mx(
                    banks["b", c, i0][:, i, :], lhsT=wb_q[i][0], lhsT_scale=wb_q[i][1], rhs=hw, rhs_scale=hs, start=True, stop=True
                )

        def copy_b(c, i0=0, i1=PACK):
            nc.scalar.copy(b_sb[:, i0:i1, c * CH : (c + 1) * CH], banks["b", c, i0][:, i0:i1, :])

        def turn_roots(c, i0=0, i1=PACK):
            banks["r", c, i0] = new_bank(f"r{c}_{i0}", TURN_BANKS[c % 2 if i1 == PACK else 1])
            for i in range(i0, i1):
                nc.tensor.transpose(banks["r", c, i0][:, i, :], roots[c][:, i, :], ident[:])

        def weigh(c, i0=0, i1=PACK):
            nc.scalar.activation(scores[:, i0:i1, c * CH : (c + 1) * CH], banks["r", c, i0][:, i0:i1, :], ACT.Square)

        def put(i, c0, c1):
            nc.vector.tensor_tensor(
                pages[i][:].indirect(bins[:, c0 * CH // 16 : c1 * CH // 16]),
                b_sb[:, i, c0 * CH : c1 * CH], scores[:, i, c0 * CH : c1 * CH], MULT,
            )

        def second_stage(c):
            turn_roots(c)
            if c + 1 < CHUNKS:
                square_d(c + 1)
            if c + 2 < CHUNKS:
                multiply_d(c + 2)
            copy_b(c)
            weigh(c)
            if c + 1 < CHUNKS:
                multiply_b(c + 1)
                take_roots(c + 1)

        def scatter(c):
            for i in range(PACK):
                if c in PIECES[i][1:-1]:
                    put(i, PIECES[i][PIECES[i].index(c) - 1], c)

        grouped = {(name, t0): held(f"{name}_{t0}", [P, 2, P, PACK], BF16) for name, t0 in (("wa0", 0), ("wa0", 2), ("wa1", 2), ("wb", 0), ("wb", 2))}
        grouped["wa1", 0] = placed("wa1_0", [P, 2, P, PACK], BF16, at_grouped)
        gather_words(GATHERS[:-1])
        project_pair(0)
        project_pair(1)
        for t0 in (0, 2):
            regroup(grouped["wa0", t0], nc.vector.tensor_copy, wa_raw0, t0)
        wa_q = [quantise("wa_q0a", grouped["wa0", 0]) + quantise("wa_q0b", grouped["wa0", 2])]
        for c in range(OPENED):
            add_av_pass(c, 0)
        regroup(grouped["wa1", 0], nc.vector.tensor_copy, wa_raw1, 0)
        regroup(grouped["wa1", 2], nc.scalar.copy, wa_raw1, 2, 0, SHARED)
        regroup(grouped["wa1", 2], nc.vector.tensor_copy, wa_raw1, 2, SHARED, P)
        project_pair(2)
        wa_q.append(quantise("wa_q1a", grouped["wa1", 0]) + quantise("wa_q1b", grouped["wa1", 2]))
        gather_words(GATHERS[-1:], at_grouped)
        regroup(grouped["wb", 0], nc.vector.tensor_copy, wb_raw[0], 0, 0, P // 2)
        regroup(grouped["wb", 2], nc.scalar.copy, wb_raw[0], 2, 0, P // 2)
        for t0 in (0, 2):
            regroup(grouped["wb", t0], nc.scalar.copy, wb_raw[1], t0, P // 2, P, P // 2)
        make_h(0)
        make_h(1)
        quantise_h(0)
        multiply_d(0)
        make_h(2)
        make_h(3)
        wb_q = quantise("wb_qa", grouped["wb", 0])
        quantise_h(1)
        make_h(4)
        make_h(5)
        wb_q = wb_q + quantise("wb_qb", grouped["wb", 2])
        quantise_h(2)
        square_d(0, 0, 2)
        square_d(0, 2, PACK)
        take_roots(0, 0, 2)
        turn_roots(0, 0, 2)
        multiply_b(0, 0, 2)
        weigh(0, 0, 2)
        copy_b(0, 0, 2)
        take_roots(0, 2, PACK)
        turn_roots(0, 2, PACK)
        multiply_b(0, 2, PACK)
        multiply_d(1)
        copy_b(0, 2, PACK)
        weigh(0, 2, PACK)
        square_d(1)
        project_pair(3)
        multiply_d(2)
        multiply_b(1)
        take_roots(1)
        scatter(1)
        make_h(6)
        make_h(7)
        quantise_h(3)
        quantise_h(4)
        for c in range(1, CHUNKS):
            second_stage(c)
            scatter(c + 1)
        for i in range(PACK):
            put(i, PIECES[i][-2], CHUNKS)
            nc.sync.dma_start(out.rearrange("(p i) t -> p i t", i=PACK)[:, i, :], pages[i][:])
